import numpy as np, ml_dtypes
CORES = [2,3,42,43,82,83,122,123]
N = 8
BF = ml_dtypes.bfloat16
def gentries(a):
    return np.ascontiguousarray(a.reshape(8, 16, -1).transpose(0, 2, 1)).reshape(8, -1)
def gtable(e):
    e = np.asarray(e); return np.ascontiguousarray(e.reshape(8, -1, 16).transpose(0, 2, 1)).reshape(128, -1).astype(np.int32)
S, Q, T, CAP, RO = 2048, 2, 256, 112, 3
B = Q * S
def near(rng, c, a):
    return np.clip(np.take_along_axis(c, a[:, :, None, :], 3) + rng.integers(-40, 41, (N, 8, 16, T)), 0, 255)
def parts(rng):
    c = rng.integers(0, 256, (N, 8, 16, S)); g = rng.integers(-16, 16, (N, 8, 16, B))
    H = S >> 4; hub = np.argsort(rng.random((N, 8, S)), axis=2)[..., :H]
    i = np.minimum((H * rng.random((N, 8, 16 * S)) ** 2).astype(np.int64), H - 1)
    u = np.take_along_axis(hub, i, 2).reshape(N, 8, 16, S); u = np.where(rng.random(u.shape) < 0.5, u, rng.integers(0, S, u.shape))
    i = np.minimum((H * rng.random((N, 8, T)) ** 2).astype(np.int64), H - 1)
    a = np.take_along_axis(hub, i, 2); a = np.where(rng.random(a.shape) < 0.5, a, rng.integers(0, S, a.shape))
    h = rng.integers(0, Q, (N, 8, S)); e = rng.choice(np.array([0.1, 0.3, 0.6]), (N, 8, 1))
    f = np.where(rng.random((N, 8, S)) < e, 0, rng.integers(0, Q + 1, (N, 8, S)))
    return c, u, g, h, f, a, near(rng, c, a)
def pack(c, u, g, h, f, a, z):
    return {"xs": np.ascontiguousarray(c.reshape(N, 128, S)).astype(np.float32).astype(BF), "su": np.ascontiguousarray(u.reshape(N, 128, S)).astype(np.int32),
            "gs": np.ascontiguousarray(g.reshape(N, 128, B)).astype(np.float32).astype(BF), "hd0": h.astype(np.int32), "fl0": f.astype(np.int32),
            "a0": np.stack([gtable(v) for v in a]), "z0": np.ascontiguousarray(z.reshape(N, 128, T)).astype(np.float32).astype(BF)}
def setup_inputs(rng):
    return pack(*parts(rng))
def setup_inputs_room(rng):
    c, u, g, h, f, a, z = parts(rng); num = (CAP, CAP + 1, T, CAP - 1, 1, 0, CAP, CAP + 1)
    for r in range(N):
        for k in range(8):
            j = (r + k) % 8; o = rng.permutation(S)[:T]; a[r, k] = o
            full = rng.integers(1, Q + 1, T)
            if j in (3, 5, 6):
                full[:] = 1 if j == 5 else Q
                u[r, k] = np.arange(S)
            f[r, k, o] = np.where(rng.permutation(T) < num[j], 0, full)
    return pack(c, u, g, h, f, a, near(rng, c, a))
def setup_inputs_crowd(rng):
    c, u, g, h, f, a, z = parts(rng)
    for r in range(N):
        for k in range(8):
            j = (r + k) % 8
            if j == 7: continue
            o = np.concatenate([rng.permutation(np.array([0, S - 1])), 1 + rng.permutation(S - 2)])
            if j < 4:
                n = (1, 2, 5, 12)[j]; a[r, k] = o[rng.integers(0, n, T)]; u[r, k] = o[rng.integers(0, n, (16, S))]
            else:
                w = (Q, Q, Q + 1)[j - 4]; o = o[:(T + w - 1) // w]
                a[r, k] = rng.permutation(np.repeat(o, w)[:T]); f[r, k, o] = (Q, 0, 0)[j - 4]
    return pack(c, u, g, h, f, a, near(rng, c, a))
def setup_inputs_ties(rng):
    c, u, g, h, f, a, z = parts(rng); pro = rng.integers(2, 254, (8, 16, 3))
    for k in range(8):
        if k % 2 == 0:
            c[:, k] = pro[k][:, np.arange(S) % 3]; g[:, k] = 2 * rng.integers(0, 2, (N, 16, B)) - 1; f[:, k] = f[:, k] * (rng.random((N, S)) < 0.5)
            if k % 4 == 2:
                g[:, k] = g[:, k] * rng.integers(0, 2, (N, 1, B)); u[:, k, 0] = np.where(rng.random((N, S)) < 0.5, np.arange(S), u[:, k, 0])
        else:
            c[:, k] = c[:, k][..., np.arange(S) // 2 * 2]; g[:, k] = g[:, k][..., np.arange(B) & 31]
    z = near(rng, c, a); z[:, ::2] = np.take_along_axis(c[:, ::2], a[:, ::2, None, :], 3)
    return pack(c, u, g, h, f, a, z)
def setup_inputs_ends(rng):
    c, u, g, h, f, a, z = parts(rng)
    c = 255 * rng.integers(0, 2, c.shape); g = 31 * rng.integers(0, 2, g.shape) - 16; z = 255 * rng.integers(0, 2, z.shape)
    k = rng.integers(0, 3, (N, 8, 1, T)); z = np.where(k == 0, 0, np.where(k == 1, 255, z))
    p = rng.permutation(8)
    f[:, p[0]] = 0; f[:, p[1]] = Q; h[:, p[2]] = Q - 1; h[:, p[3]] = 0
    for j in (4, 5, 6):
        w = p[j]; cw = rng.integers(0, 2, (N, 16, S)); zw = 255 - rng.integers(0, 2, (N, 16, T)); f[:, w] = Q * rng.integers(0, 2, (N, S))
        if j < 6:
            two = np.argsort(rng.random((N, 16, B)), axis=1) < 2
            gw = np.where(two, -rng.integers(1, 9, (N, 16, B)), rng.integers(6, 16, (N, 16, B)))
            if j == 5: cw = 255 - cw; zw = 255 - zw; gw = -gw
            g[:, w] = gw
        c[:, w] = cw; z[:, w] = zw
    a[..., 0] = 0; a[..., 1] = S - 1; a[..., T - 2] = 0; a[..., T - 1] = S - 1
    u = np.where(rng.random(u.shape) < 0.3, (S - 1) * rng.integers(0, 2, u.shape), u)
    return pack(c, u, g, h, f, a, z)
def setup_inputs_spread(rng):
    c, u, g, h, f, a, z = parts(rng)
    c = np.minimum((256 * rng.random(c.shape) ** np.exp2(rng.uniform(-3, 3, (N, 8, 1, S)))).astype(np.int64), 255)
    z = np.minimum((256 * rng.random(z.shape) ** np.exp2(rng.uniform(-3, 3, (N, 8, 1, T)))).astype(np.int64), 255)
    g = np.clip(np.floor((rng.random(g.shape) * 2 - 1) * np.exp2(rng.uniform(-2, 4, (N, 8, 1, B)))).astype(np.int64), -16, 15)
    m = rng.permuted(np.tile(np.arange(S), (N, 8, 1)), axis=2)
    i = np.minimum((S * rng.random((N, 8, 16 * S)) ** rng.uniform(1, 5, (N, 8, 1))).astype(np.int64), S - 1); u = np.take_along_axis(m, i, 2).reshape(N, 8, 16, S)
    i = np.minimum((S * rng.random((N, 8, T)) ** rng.uniform(1, 5, (N, 8, 1))).astype(np.int64), S - 1); a = np.take_along_axis(m, i, 2)
    f = np.minimum(((Q + 1) * rng.random((N, 8, S)) ** np.exp2(rng.uniform(-2, 2, (N, 8, 1)))).astype(np.int64), Q)
    return pack(c, u, g, h, f, a, z)
def check_inputs(d):
    bad = []
    for k, lo, hi in (("xs", 0, 255), ("su", 0, S - 1), ("gs", -16, 15), ("hd0", 0, Q - 1), ("fl0", 0, Q), ("a0", 0, S - 1), ("z0", 0, 255)):
        v = np.asarray(d[k]).astype(np.float64)
        if not (np.all(v >= lo) and np.all(v <= hi) and np.all(v == np.floor(v))): bad.append("range of " + k)
    return bad
def reference(xs, su, gs, hd0, fl0, a0, z0):
    X = xs.astype(np.float32).astype(np.int64).reshape(N, 8, 16, S); U = su.astype(np.int64).reshape(N, 8, 16, S)
    G = gs.astype(np.float32).astype(np.int64).reshape(N, 8, 16, B); hd = hd0.astype(np.int64); fl = fl0.astype(np.int64)
    a = np.stack([gentries(v) for v in a0]).astype(np.int64); z = z0.astype(np.float32).astype(np.int64).reshape(N, 8, 16, T)
    low = np.tri(T, k=-1, dtype=bool); odd = 2 * np.arange(16)[:, None] + 1
    for t in range(RO):
        same = a[:, :, :, None] == a[:, :, None, :]
        place = np.sum(same & low, axis=3); count = np.sum(same, axis=3)
        ha = np.take_along_axis(hd, a, 2); fa = np.take_along_axis(fl, a, 2)
        pop = place < fa; slot = Q * a + ((ha + place) & (Q - 1))
        zn = np.clip(z + np.take_along_axis(G, slot[:, :, None, :], 3), 0, 255)
        s = np.take_along_axis(U, a[:, :, None, :], 3)
        c = np.take_along_axis(X, s.reshape(N, 8, 1, 16 * T), 3).reshape(N, 8, 16, 16, T)
        best = np.argmin(np.sum(np.abs(c - zn[:, :, :, None, :]), axis=2), axis=2)
        to = np.take_along_axis(s, best[:, :, None, :], 2)[:, :, 0]
        gone = np.minimum(count, fa)
        np.put_along_axis(hd, a, (ha + gone) & (Q - 1), 2); np.put_along_axis(fl, a, fa - gone, 2)
        ask = ~pop & (np.add.accumulate((~pop).astype(np.int64), axis=2) <= CAP)
        d = 1 + t % (N - 1); XR = np.roll(X, -d, axis=0); GR = np.roll(G, -d, axis=0)
        u = np.sum(odd * z, axis=2) & 4095
        ix = (((u * u) >> 5)[:, :, None, :] + odd * u[:, :, None, :]) & (B - 1)
        cand = np.take_along_axis(GR, ix.reshape(N, 8, 1, 16 * T), 3).reshape(N, 8, 16, 16, T)
        goal = np.take_along_axis(XR, a[:, :, None, :], 3)
        m = np.argmin(np.sum(np.abs(z[:, :, :, None, :] + cand - goal[:, :, :, None, :]), axis=2), axis=2)
        seg = np.take_along_axis(cand, m[:, :, None, None, :], 3)[:, :, :, 0]
        put = ask & (place - fa < Q)
        for r in range(N):
            for g in range(8):
                w = np.flatnonzero(put[r, g])
                G[r, g][:, slot[r, g, w]] = seg[r, g][:, w]
                np.add.at(fl[r, g], a[r, g, w], 1)
        a = np.where(pop, to, a); z = np.where(pop[:, :, None, :], zn, z)
    return {"yz": z.reshape(N, 128, T).astype(np.float32).astype(BF), "ya": a.astype(np.float32), "yh": hd.astype(np.float32), "yf": fl.astype(np.float32)}

@@ -1,0 +1,526 @@
+from concourse.bass import DstId, RemoteDMATransfer
+from concourse.mybir import AluOpType as A, ActivationFunctionType as F
+
+SCRATCH = {}
+
+
+def _b(n, c, d="bfloat16", w="sbuf", p=128):
+    SCRATCH[n] = (w, [p, c], d)
+
+
+for _n, _c in (("X", 2048), ("G", 4368), ("FB", 128), ("HB", 128), ("cS", 4096), ("cA", 4096), ("AB", 4096), ("AC", 4096),
+               ("E", 4096), ("mI", 128), ("mNI", 128), ("SG", 128), ("SGf", 128), ("SGh", 128), ("SGp", 128), ("ZE", 144),
+               ("ZW", 144), ("ZL", 144), ("ZA", 144), ("TRI", 128), ("Fa", 2048), ("Ff", 2048), ("Fh", 2048), ("LTm", 2048),
+               ("WR1", 128), ("WR2", 128), ("REP", 512), ("KBS", 48), ("KBA", 24), ("PH", 256), ("PL", 256), ("ONE", 128),
+               ("CRS", 512), ("CRA", 256), ("ZROW", 256), ("RR", 512), ("blB", 16), ("scB", 16), ("hpB", 16), ("fpB", 16),
+               ("vhB", 16), ("vlB", 16), ("shB", 256), ("slB", 256), ("zt", 256), ("WTS", 256), ("WTA", 256), ("goal", 256),
+               ("PB", 48), ("T16", 512), ("Z0", 256), ("Z1", 256), ("Z2", 256), ("Z3", 256), ("AN0", 256), ("AN1", 256),
+               ("LN0", 256), ("LN1", 256), ("QZ0", 256), ("QZ1", 256)):
+    _b(_n, _c)
+for _n, _c in (("HF", 2304), ("JX", 144), ("JG", 128), ("JM", 128), ("JPH", 256), ("JPL", 256), ("JR", 512), ("RA", 128),
+               ("RB", 128), ("J16", 16), ("KB2", 16), ("COL", 128), ("OH", 16), ("LT", 16), ("LA", 48), ("W1", 128),
+               ("ZR16", 16), ("LL", 512), ("KU", 256), ("K1", 256), ("K2", 128), ("K3", 64), ("HV", 256),
+               ("aF0", 48), ("aF1", 48), ("aF2", 48), ("aF3", 48), ("UV0", 32), ("UV1", 32), ("QU0", 32), ("QU1", 32)):
+    _b(_n, _c, "float32")
+for _n, _c in (("SU", 2048), ("IOT", 2048), ("FI", 128), ("HI", 128), ("aI", 16), ("CI", 8), ("LI", 320), ("TI", 256), ("TJ", 256),
+               ("sI", 256), ("sJ", 512), ("KI", 48), ("KJ", 48)):
+    _b(_n, _c, "int32")
+for _n, _c in (("aU0", 16), ("aU1", 16), ("aU2", 16), ("aU3", 16), ("AR", 256), ("sU", 256), ("gU", 16), ("nU", 48),
+               ("qU", 16), ("CL0", 256), ("CL1", 256), ("QC0", 256), ("QC1", 256), ("QA0", 16), ("QA1", 16)):
+    _b(_n, _c, "uint16")
+for _n in ("D0", "D1", "D2", "KEY", "PLB", "ML", "WTP", "TR"):
+    _b(_n, 512, "float32", "psum")
+SEMAPHORES = ["eV", "eS", "eP", "eG", "sent", "l_a", "l_z", "l_h", "l_f", "l_s", "l_x", "l_g", "o_z", "o_a", "o_h", "o_f",
+              "r_z0", "r_z1", "r_c0", "r_c1", "r_u0", "r_u1", "r_a0", "r_a1", "r_n0", "r_n1"]
+STEPS = 3
+
+
+def rank_program(g, core, T, topo):
+    rank = T.rank_of(core)
+    if rank is None:
+        return
+    n = len(T.cores)
+    H = {"V": g.vector, "S": g.scalar, "P": g.tensor, "G": g, "Y": g.sync}
+    cnt = {"V": 0, "S": 0, "P": 0, "G": 0}
+    known = {q: {} for q in H}
+    wr, rd, pacc = {}, {}, {}
+
+    def v(name, c0=0, c1=None, st=1, p0=0, p1=None):
+        sh = SCRATCH[name][1]
+        return (name, c0, sh[1] if c1 is None else c1, st, p0, sh[0] if p1 is None else p1)
+
+    def ap(x):
+        if not isinstance(x, tuple):
+            return x
+        if x[0] == "ind":
+            return ap(x[1]).indirect(ap(x[2]))
+        name, c0, c1, st, p0, p1 = x
+        return T[name][p0:p1, c0:c1] if st == 1 else T[name][p0:p1, c0:c1:st]
+
+    def ind(win, off):
+        return ("ind", win, off)
+
+    def wait(q, rec):
+        sem, val, kn = rec[1], rec[2], rec[3]
+        if known[q].get(sem, 0) >= val:
+            return
+        H[q].wait_ge(T.sem[sem], val)
+        for s, x in list(kn.items()) + [(sem, val)]:
+            if known[q].get(s, 0) < x:
+                known[q][s] = x
+
+    def flat(xs):
+        out = []
+        for x in xs:
+            if isinstance(x, tuple):
+                out += [x[1], x[2]] if x[0] == "ind" else [x]
+        return out
+
+    def deps(q, ws, rs):
+        need = []
+        for x in ws + rs:
+            if SCRATCH[x[0]][0] == "psum":
+                need += [r for k, r in pacc.get(x[0], {}).items() if k != q]
+            need += [r for lo, hi, r in wr.get(x[0], []) if lo < x[2] and x[1] < hi]
+        for x in ws:
+            need += [r for lo, hi, r in rd.get(x[0], []) if lo < x[2] and x[1] < hi]
+        for r in sorted(need, key=lambda r: -r[2]):
+            wait(q, r)
+
+    def note(rec, ws, rs, cover=True):
+        for x in ws + rs:
+            if SCRATCH[x[0]][0] == "psum":
+                pacc.setdefault(x[0], {})[rec[0]] = rec
+        for x in ws:
+            if SCRATCH[x[0]][0] == "psum":
+                continue
+            if x[3] == 1 and cover:
+                wr[x[0]] = [e for e in wr.get(x[0], []) if not (x[1] <= e[0] and e[1] <= x[2])]
+                rd[x[0]] = [e for e in rd.get(x[0], []) if not (x[1] <= e[0] and e[1] <= x[2])]
+            wr.setdefault(x[0], []).append((x[1], x[2], rec))
+        for x in rs:
+            if SCRATCH[x[0]][0] != "psum":
+                rd[x[0]] = [e for e in rd.get(x[0], []) if not (e[2][0] == rec[0] and not e[2][4] and x[1] <= e[0] and e[1] <= x[2])]
+                rd[x[0]].append((x[1], x[2], rec))
+
+    def op(q, call, out, *ins):
+        ws, rs = flat([out]), flat(ins)
+        if out[0] == "ind":
+            ws, rs = [out[1]], rs + [out[2]]
+        deps(q, ws, rs)
+        cnt[q] += 1
+        call().then_inc(T.sem["e" + q], 1)
+        note((q, "e" + q, cnt[q], dict(known[q]), False), ws, rs, out[0] != "ind")
+
+    def vcopy(out, in_):
+        op("V", lambda: g.vector.tensor_copy(out=ap(out), in_=ap(in_)), out, in_)
+
+    def tt(out, a, b, o):
+        op("V", lambda: g.vector.tensor_tensor(out=ap(out), in0=ap(a), in1=ap(b), op=o), out, a, b)
+
+    def ts(out, a, s1, o1, s2=None, o2=None):
+        if o2 is None:
+            op("V", lambda: g.vector.tensor_scalar(out=ap(out), in0=ap(a), scalar1=ap(s1), scalar2=None, op0=o1), out, a, s1)
+        else:
+            op("V", lambda: g.vector.tensor_scalar(out=ap(out), in0=ap(a), scalar1=ap(s1), scalar2=ap(s2), op0=o1, op1=o2), out, a, s1, s2)
+
+    def act(out, in_, f=F.Copy, scale=1.0):
+        op("S", lambda: g.scalar.activation(out=ap(out), in_=ap(in_), func=f, scale=ap(scale)), out, in_, scale)
+
+    def mm(out, lhsT, rhs, start, stop):
+        op("P", lambda: g.tensor.matmul(ap(out), ap(lhsT), ap(rhs), start, stop), out, lhsT, rhs)
+
+    def iota(out, pat, base=0, mult=0):
+        op("G", lambda: g.iota(ap(out), pat, base, mult, allow_small_or_imprecise_dtypes=True), out)
+
+    def fill(out, x):
+        op("V", lambda: g.vector.memset(ap(out), x), out)
+
+    def load(q, out, in_, sem):
+        H[q].dma_start(out=ap(out), in_=in_).then_inc(T.sem[sem], 16)
+        note((q, sem, 16, {}, True), [out], [])
+
+    final, sent = [], [0]
+
+    def store(out, in_, sem, row=None):
+        deps("Y", [], [in_])
+        src = ap(in_) if row is None else T[in_[0]][row:128:16, in_[1]:in_[2]]
+        g.sync.dma_start(out=out, in_=src).then_inc(T.sem[sem], 16)
+        final.append((sem, 16))
+
+    def send(dst, parts):
+        to = T.cores[dst]
+        rid, pid = topo.addr(to)[0], topo.addr(to)[1]
+        e = topo.engines(core, to)[:8]
+        deps("G", [], [p[0] for p in parts])
+        m = [sum(1 << x for x in e[k::len(parts)]) for k in range(len(parts))]
+        sent[0] += len(e)
+        if len(parts) == 1:
+            s, d, sem = parts[0]
+            g.remote_dma(ap(v(d)), ap(s), T.sem[sem], T.sem.sent, pid, rid, m[0])
+        else:
+            g.remote_dma_fused([RemoteDMATransfer(dst_ids=[DstId(rid=rid, pnc=pid)], dma_engine_mask=m[k], remote_sem=T.sem[sem],
+                                                  src=ap(s), dst=ap(v(d))) for k, (s, d, sem) in enumerate(parts)], local_sem=T.sem.sent)
+
+    def arrive(buf, sem, src, parts):
+        e = len(topo.engines(T.cores[src], core)[:8]) // parts
+        wr[buf] = [(0, SCRATCH[buf][1][1], ("R", sem, e, {}, True))]
+
+    load("Y", v("aI"), T.a0[:, :], "l_a")
+    load("S", v("Z0"), T.z0[:, :], "l_z")
+    load("Y", v("SU"), T.su[:, :], "l_s")
+    load("S", v("HI"), T.hd0[:, :], "l_h")
+    load("S", v("FI"), T.fl0[:, :], "l_f")
+    load("Y", v("X"), T.xs[:, :], "l_x")
+    load("S", v("G", 0, 4096), T.gs[:, :], "l_g")
+    for t in range(2):
+        p, q = (rank - 1 - t) % n, (rank + 1 + t) % n
+        for b, c in (("QZ", 2), ("QC", 2), ("QU", 1), ("QA", 1)):
+            arrive(b + str(t), "r_" + b[1].lower() + str(t), p, c)
+        arrive("LN%d" % t, "r_n%d" % t, q, 1)
+
+    iota(v("CI", 0, 1), [[0, 1]], 0, 1)
+    iota(v("JX"), [[1, 144]])
+    iota(v("J16"), [[1, 16]])
+    iota(v("JG"), [[1, 8], [0, 16]])
+    iota(v("RA"), [[0, 8], [8, 4], [0, 4]])
+    iota(v("RB"), [[0, 32], [2, 4]], 1)
+    iota(v("IOT"), [[1, 2048]])
+    iota(v("JR"), [[1, 32], [0, 16]])
+    iota(v("KB2"), [[0, 2], [1, 8]])
+    iota(v("CRA", p0=0, p1=1), [[1, 16], [0, 16]])
+    iota(v("CRS", p0=0, p1=1), [[64, 16], [0, 32]])
+    iota(v("JPH"), [[1, 16], [1000, 2], [16, 8]])
+    iota(v("JPL"), [[1, 16], [1000, 2], [16, 8]], -1000)
+
+    def col(k):
+        return v("COL", 4 * k, 4 * k + 1)
+    (pF, pm, pg, g0, g1, g15, wi, wE, c1, p8, p31, w8) = [col(k) for k in range(12)]
+
+    def cands(t, part):
+        z, uv, o, r = "Z%d" % t, "UV%d" % t, v("ML", 96, 112), "TR"
+        li = [v("LI", 16 * k, 16 * k + 16) for k in range(8)]
+        if part == 0:
+            for i in range(16):
+                mm(o, v("ZW", 15 - i, 143 - i), v(z, i, 256, 16), i == 0, i == 15)
+        if part == 1:
+            vcopy(li[0], o)
+            ts(li[1], li[0], 4095, A.bitwise_and)
+            tt(li[2], li[1], li[1], A.mult)
+            ts(li[3], li[2], 5, A.logical_shift_right)
+            ts(li[4], li[3], 4095, A.bitwise_and)
+            ts(li[5], li[4], 6, A.logical_shift_right)
+            ts(li[6], li[4], 63, A.bitwise_and)
+            ts(v("vhB"), li[5], 64.0, A.mult)
+            vcopy(v("vlB"), li[6])
+            mm(v(r, 0, 256), v("WR1"), v(z), True, False)
+            mm(v(r, 0, 256), v("WR2"), v(z), False, False)
+            for i in range(16):
+                for b in ("vhB", "vlB"):
+                    mm(v(r, i, 256, 16), v("Fa", 128 * i, 128 * i + 128), v(b), False, i == 15 and b == "vlB")
+        if part == 2:
+            vcopy(v("TI"), v(r, 0, 256))
+            ts(v("TJ"), v("TI"), 4095, A.bitwise_and)
+            vcopy(v("CL%d" % t), v("TJ"))
+            q = (rank + 1 + t) % n
+            send(q, [(v(z), "QZ%d" % t, "r_z%d" % t), (v("CL%d" % t), "QC%d" % t, "r_c%d" % t)])
+            vcopy(v(uv, 0, 16), li[1])
+            vcopy(v(uv, 16, 32), li[4])
+            send(q, [(v(uv), "QU%d" % t, "r_u%d" % t)])
+
+    def ask(t):
+        send((rank + 1 + t) % n, [(v("aU%d" % t), "QA%d" % t, "r_a%d" % t)])
+
+    vcopy(pF, v("CI", 0, 1))
+    for j, (out, o, s) in enumerate(((pm, A.bitwise_and, 15), (pg, A.logical_shift_right, 4), (p8, A.bitwise_and, 7),
+                                     (p31, A.bitwise_and, 31))):
+        ts(v("CI", 1 + j, 2 + j), v("CI", 0, 1), s, o)
+        vcopy(out, v("CI", 1 + j, 2 + j))
+    ts(g15, pg, 16.0, A.mult, 15.0, A.add)
+    ts(wi, pm, 2.0, A.mult, 1.0, A.add)
+    ts(v("ZW"), v("JX"), g15, A.is_equal, wi, A.mult)
+    ts(v("SG"), v("JG"), pg, A.is_equal)
+    ts(v("OH"), v("J16"), pm, A.is_equal)
+    cands(0, 0)
+    for i in range(16):
+        act(v("Fa", 128 * i, 128 * i + 128), v("SG"), scale=v("OH", i, i + 1))
+    vcopy(v("aU0"), v("aI"))
+    ask(0)
+    ts(g0, pg, 16.0, A.mult)
+    ts(g1, g0, 1.0, A.add)
+    ts(v("SGf"), v("JX", 0, 128), g0, A.is_equal)
+    ts(v("SGh"), v("JX", 0, 128), g1, A.is_equal)
+    ts(v("LT"), v("J16"), pm, A.is_gt)
+    for i in range(16):
+        act(v("Ff", 128 * i, 128 * i + 128), v("SGf"), scale=v("OH", i, i + 1))
+        act(v("Fh", 128 * i, 128 * i + 128), v("SGh"), scale=v("OH", i, i + 1))
+    for r, w in (("RA", "WR1"), ("RB", "WR2")):
+        ts(v("W1"), v(r), wi, A.mult)
+        tt(v(w), v("W1"), v("SG"), A.mult)
+    cands(0, 1)
+    cands(0, 2)
+    vcopy(v("HB"), v("HI"))
+    vcopy(v("FB"), v("FI"))
+    for b in range(4):
+        d = "D%d" % (b % 3)
+        for k in range(4):
+            i = 4 * b + k
+            mm(v(d, 128 * k, 128 * k + 128), v("Ff", 128 * i, 128 * i + 128), v("FB"), True, False)
+            mm(v(d, 128 * k, 128 * k + 128), v("Fh", 128 * i, 128 * i + 128), v("HB"), False, True)
+        act(v("HF", 512 * b, 512 * b + 512), v(d))
+    vcopy(v("aF0", 16, 32), v("aI"))
+    vcopy(v("aF0", 32, 48), v("aI"))
+    fill(v("ONE"), 1.0)
+    fill(v("ZROW"), 0.0)
+    fill(v("ZR16"), 0.0)
+    fill(v("G", 4096, 4112), 0.0)
+    tt(v("SGp"), v("SGf"), v("SGh"), A.add)
+    for i in range(1, 16):
+        act(v("LTm", 128 * i, 128 * i + 128), v("SGf"), scale=v("LT", i, i + 1))
+
+    def late_constants():
+        ts(wE, pm, 0.0, A.is_equal)
+        ts(c1, pm, 1.0, A.is_equal, 512.0, A.mult)
+        tt(wE, wE, c1, A.add)
+        ts(v("ZE"), v("JX"), g15, A.is_equal, wE, A.mult)
+        ts(v("mI"), v("JX", 0, 128), pF, A.is_equal)
+        act(v("mNI"), v("mI"), scale=-1.0)
+        ts(v("REP"), v("JR"), p31, A.is_equal)
+        ts(v("JM"), v("JG"), -16.0, A.mult)
+        tt(v("JM"), v("JM"), v("JX", 0, 128), A.add)
+        ts(v("W1"), v("JM"), pm, A.is_gt)
+        tt(v("TRI"), v("W1"), v("SG"), A.mult)
+        tt(v("TRI"), v("TRI"), v("SG"), A.subtract)
+        ts(v("LA", 0, 16), v("J16"), 16.0, A.mult, 4112.0, A.add)
+        ts(v("LA", 0, 16), v("LA", 0, 16), pm, A.add)
+        ts(v("LA", 16, 32), v("LA", 0, 16), -2064.0, A.add)
+        ts(v("LA", 32, 48), v("LA", 0, 16), -2064.0, A.add)
+        for k, f in enumerate((1.0, 2.0, -1.0)):
+            ts(v("KBA", 8 * k, 8 * k + 8), v("KB2", 0, 8), pg, A.is_equal, 16.0 * f, A.mult)
+            ts(v("KBS", 16 * k, 16 * k + 16), v("KB2"), pg, A.is_equal, 1024.0 * f, A.mult)
+        ts(c1, p8, 16.0, A.mult, 15.0, A.add)
+        ts(v("ZA"), v("JX"), c1, A.is_equal)
+        ts(w8, pF, 8.0, A.is_lt, 63.0, A.mult)
+        ts(w8, w8, 1.0, A.add)
+        ts(v("ZL"), v("ZA"), w8, A.mult)
+        ts(v("PH"), v("JPH"), pF, A.is_equal)
+        ts(v("PL"), v("JPL"), pF, A.is_equal)
+
+    def gather(q, out, k0, k1, win, lst):
+        o, i = v(out, 512 * k0, 512 * k1), ind(win, v(lst, 32 * k0, 32 * k1))
+        vcopy(o, i) if q == "V" else act(o, i)
+
+    def terms(bank, pos, neg):
+        for h in range(2):
+            o, s = v(bank, 128 * h, 128 * h + 128), (128 * h, 128 * h + 128)
+            mm(o, v(pos, *s), v("mI"), True, not neg)
+            if neg:
+                mm(o, v(neg, *s), v("mNI"), False, True)
+
+    def dist(ab, src, term, order):
+        for k in order:
+            h, r = k // 4, 32 * (k % 4)
+            d = v(("D0", "D1")[k % 2] if h == 0 else ("D2", "WTP")[k % 2])
+            s, o = v(src, 512 * k, 512 * k + 512), v(ab, 512 * k, 512 * k + 512)
+            if h == 0:
+                mm(d, v("mNI"), s, True, False)
+            mm(d, v(term, 128 * h, 128 * h + 128, 1, r, r + 32), v("REP", p0=r, p1=r + 32), h == 1, True)
+            if h == 0:
+                act(o, d, F.Abs)
+            else:
+                tt(o, s, d, A.max)
+
+    def sums(bank, src, h, kb, k, w, last):
+        for m in range(16):
+            mm(v(bank, m * 2 * w + h, (m + 1) * 2 * w, 2), v(src, m + 2048 * h, 2048 * h + 2048, 16), v(kb, k * w, k * w + w), False,
+               last and m == 15)
+
+    def least(bank, w, k0):
+        u = 16 * w
+        vcopy(v("KU", 0, u), v(bank, u, 2 * u))
+        tt(v("K1", 0, u), v(bank, 0, u), v("KU", 0, u), A.min)
+        tt(v("K2", 0, u // 2), v("K1", 0, u // 2), v("K1", u // 2, u), A.min)
+        tt(v("K3", 0, u // 4), v("K2", 0, u // 4), v("K2", u // 4, u // 2), A.min)
+        tt(v("KI", k0, k0 + u // 8), v("K3", 0, u // 8), v("K3", u // 8, u // 4), A.min)
+
+    def turn(w, mask, k0, bank):
+        ts(v("KJ", k0, k0 + 2 * w), v("KI", k0, k0 + 2 * w), mask, A.bitwise_and)
+        vcopy(v("PB", k0, k0 + 2 * w), v("KJ", k0, k0 + 2 * w))
+        for h in range(2):
+            mm(v(bank, 256 + 128 * h, 384 + 128 * h, 1, 0, w), v("PB", k0 + h, k0 + 2 * w, 2), v("mI"), True, True)
+
+    def row(w, k0, bank):
+        vcopy(v("T16", 8 * k0, 8 * k0 + 256, 1, 0, w), v(bank, 256, 512, 1, 0, w))
+
+    def lists(w, k0, zs, o):
+        for i in range(16):
+            mm(o, v(zs, 15 - i, 143 - i, 1, 0, w), v("T16", 8 * k0 + i, 8 * k0 + 256, 16, 0, w), i == 0, i == 15)
+
+    for t in range(STEPS):
+        last = t == STEPS - 1
+        aF, aU, z, zn = "aF%d" % t, v("aU%d" % t), "Z%d" % t, "Z%d" % (t + 1)
+        aL, slot, bank = v(aF, 16, 32), v(aF, 0, 16), v("G", 0, 4096)
+        nn, ss, t1, segf, ask_, q1, n0, lf, pop, fm, ak, put, wA, n1 = [v("LL", 16 * x, 16 * x + 16) for x in range(14)]
+        three, t2 = v("LL", 176, 224), v("LL", 240, 256)
+        k, f, ct, hh, hs, hk = [v("LI", x, x + 16) for x in (224, 240, 256, 272, 128, 144)]
+        o, ro, mo, so = v("ML", 0, 32), v("ML", 64, 80), v("ML", 160, 176), v("ML", 128, 144)
+
+        def keys():
+            mm(v("KEY"), v("ONE", p0=0, p1=1), v("CRS", p0=0, p1=1), True, False)
+            for h in range(2):
+                for b, w in (("shB", "PH"), ("slB", "PL")):
+                    mm(v("KEY", h, 512, 2), v(b, 128 * h, 128 * h + 128), v(w), False, False)
+            sums("KEY", "cS", 1, "KBS", 2, 16, False)
+
+        def ready():
+            terms("TR", zn, None)
+            vcopy(v("WTS"), v("TR", 0, 256))
+            mm(ro, v("SG"), v("scB"), True, False)
+            mm(ro, v("TRI"), v("blB"), False, True)
+
+        def decide():
+            ts(ask_, ro, 112.0, A.is_lt)
+            ts(pop, v("blB"), -1.0, A.mult, 1.0, A.add)
+            ts(q1, nn, 1.0, A.is_le)
+            ts(t1, nn, 1.0, A.add)
+            ts(n0, nn, 0.0, A.is_equal)
+            tt(ask_, ask_, v("blB"), A.mult)
+            ts(t2, nn, -1.0, A.mult, -1.0, A.add)
+            tt(lf, ct, k, A.subtract)
+            tt(fm, t1, ask_, A.mult)
+            tt(v("hpB"), n0, hk, A.is_equal)
+            tt(v("fpB"), t2, fm, A.max)
+            ts(lf, lf, 1.0, A.is_equal)
+            tt(put, q1, ask_, A.mult)
+            ts(n1, nn, 1.0, A.is_equal)
+            tt(lf, lf, pop, A.mult)
+            tt(ak, aL, v("blB"), A.mult)
+            tt(wA, n0, lf, A.max)
+            tt(n1, n1, ask_, A.mult)
+            ts(three, three, -1.0, A.mult, 1.0, A.add)
+            tt(three, three, v("LA"), A.mult)
+            tt(three, three, v(aF), A.max)
+            vcopy(v("nU"), three)
+
+        def values():
+            for i in range(16):
+                mm(v("TR", i, 256, 16), v("Ff", 128 * i, 128 * i + 128), v("fpB"), True, False)
+                mm(v("TR", i, 256, 16), v("Fh", 128 * i, 128 * i + 128), v("hpB"), False, True)
+            act(v("HV"), v("TR", 0, 256))
+
+        vcopy(v("AR"), ind(v("IOT"), aU))
+        mm(v("PLB", 0, 256), v("ONE", p0=0, p1=1), v("ZROW", p0=0, p1=1), True, False)
+        for c in range(16):
+            e = 256 * c
+            ts(v("E", e, e + 256), v("AR"), v(aF, 16 + c, 17 + c), A.is_equal)
+            mm(v("PLB", 0, 16 * c + 16), v("SGh"), v("E", e, e + 16 * c + 16), False, False)
+            if c < 15:
+                mm(v("PLB", 16 * c + 16, 256), v("SGp"), v("E", e + 16 * c + 16, e + 256), False, False)
+            if c == 1:
+                vcopy(v("sI"), ind(v("SU"), aU))
+                vcopy(v("sU"), v("sI"))
+                gather("S", "cS", 4, 8, v("X"), "sU")
+        if t == 0:
+            late_constants()
+        for i in range(1, 16):
+            mm(v("PLB", i, 256, 16), v("LTm", 128 * i, 128 * i + 128), v("E", i, 4096, 272), False, i == 15)
+        act(v("RR", 0, 256), v("PLB", 0, 256))
+        ts(v("sJ", 0, 256), v("sI"), 6, A.logical_shift_right)
+        ts(v("sJ", 256, 512), v("sI"), 63, A.bitwise_and)
+        vcopy(v("shB"), v("sJ", 0, 256))
+        vcopy(v("slB"), v("sJ", 256, 512))
+        act(v("RR", 256, 512), ind(v("HF", 0, 2048), aU))
+        for i in range(16):
+            mm(o, v("ZE", 15 - i, 143 - i), v("RR", i, 512, 16), i == 0, i == 15)
+        if t:
+            vcopy(ind(v("G"), v("nU", 0, 16)), v("LN%d" % (t - 1)))
+        if last:
+            gather("S", "cS", 0, 3, v("X"), "sU")
+            gather("V", "cS", 3, 4, v("X"), "sU")
+        else:
+            act(v("goal"), ind(v("X"), v("QA%d" % t)))
+            gather("S", "cA", 0, 4, bank, "QC%d" % t)
+            gather("V", "cA", 4, 8, bank, "QC%d" % t)
+            terms("WTP", "goal", "QZ%d" % t)
+            ts(v("WTA"), v("WTP", 0, 256), -16.0, A.max, 16.0, A.min)
+        keys()
+        vcopy(v("LI", 192, 224), o)
+        ts(v("LI", 224, 256), v("LI", 192, 224), 511, A.bitwise_and)
+        ts(v("LI", 256, 288), v("LI", 192, 224), 9, A.logical_shift_right)
+        tt(nn, k, f, A.subtract)
+        tt(hs, hh, k, A.add)
+        ts(v("blB"), nn, 0.0, A.is_ge)
+        ts(hk, hs, 1, A.bitwise_and)
+        ts(ss, aL, 2.0, A.mult)
+        ts(t1, v("blB"), 4096.0, A.mult)
+        tt(slot, ss, hk, A.add)
+        tt(segf, t1, slot, A.max)
+        vcopy(v("gU"), segf)
+        tt(v("zt"), ind(v("G", 0, 4112), v("gU")), v(z), A.add)
+        ts(v(zn), v("zt"), 0.0, A.max, 255.0, A.min)
+        op("V", lambda: g.vector.tensor_tensor_scan(out=ap(v("scB")), data0=ap(v("blB")), data1=ap(v("ZR16")), initial=0.0, op0=A.add, op1=A.add),
+           v("scB"), v("blB"), v("ZR16"))
+        if last:
+            store(T.yz[:, :], v(zn), "o_z")
+            ready()
+            decide()
+            dist("AB", "cS", "WTS", (0, 1, 4, 2, 5, 3, 6, 7))
+            sums("KEY", "AB", 0, "KBS", 0, 16, False)
+            sums("KEY", "AB", 1, "KBS", 1, 16, True)
+        else:
+            mm(v("PLB", 0, 256), v("ONE", p0=0, p1=1), v("CRA", p0=0, p1=1), True, False)
+            sums("PLB", "cA", 1, "KBA", 2, 8, False)
+            dist("AC", "cA", "WTA", (0, 4, 1, 5, 2, 3, 6, 7))
+            if t == 0:
+                cands(1, 0)
+            ready()
+            if t == 0:
+                cands(1, 1)
+            gather("S", "cS", 0, 4, v("X"), "sU")
+            if t == 0:
+                cands(1, 2)
+            sums("PLB", "AC", 0, "KBA", 0, 8, False)
+            sums("PLB", "AC", 1, "KBA", 1, 8, True)
+            decide()
+            dist("AB", "cS", "WTS", (4, 5))
+            values()
+            dist("AB", "cS", "WTS", (0, 6, 1, 7, 2, 3))
+            vcopy(ind(v("HF"), v("nU", 16, 32)), v("HV"))
+            least("PLB", 8, 32)
+            sums("KEY", "AB", 1, "KBS", 1, 16, False)
+            turn(8, 15, 32, "PLB")
+            vcopy(ind(v("HF"), v("nU", 32, 48)), v("HV"))
+            row(8, 32, "PLB")
+            sums("KEY", "AB", 0, "KBS", 0, 16, True)
+            lists(8, 32, "ZA", mo)
+        least("KEY", 16, 0)
+        turn(16, 63, 0, "TR")
+        if not last:
+            ts(t1, mo, 2.0, A.mult, 1.0, A.add)
+            tt(t1, t1, v("QU%d" % t, 0, 16), A.mult)
+            tt(v("LI", 160, 176), t1, v("QU%d" % t, 16, 32), A.add)
+            ts(v("LI", 176, 192), v("LI", 160, 176), 4095, A.bitwise_and)
+            vcopy(v("qU"), v("LI", 176, 192))
+            vcopy(v("AN%d" % t), ind(bank, v("qU")))
+            send((rank - 1 - t) % n, [(v("AN%d" % t), "LN%d" % t, "r_n%d" % t)])
+        row(16, 0, "TR")
+        lists(16, 0, "ZL", so)
+        if last:
+            values()
+            vcopy(ind(v("HF"), v("nU", 16, 32)), v("HV"))
+        aN = "aF%d" % (t + 1)
+        tt(t2, so, pop, A.mult)
+        tt(v(aN, 16, 32), t2, ak, A.add)
+        vcopy(v("aU%d" % (t + 1)), v(aN, 16, 32))
+        vcopy(v(aN, 32, 48), v(aN, 16, 32))
+        if t + 1 < STEPS - 1:
+            ask(t + 1)
+    vcopy(v("KU"), ind(v("IOT"), v("aU%d" % STEPS)))
+    store(T.ya[:, :], v("KU"), "o_a", 0)
+    vcopy(ind(v("HF"), v("nU", 32, 48)), v("HV"))
+    store(T.yh[:, :], v("HF", 0, 2048), "o_h", 1)
+    store(T.yf[:, :], v("HF", 0, 2048), "o_f", 0)
+    g.wait_ge(T.sem.sent, sent[0])
+    for s, x in [("e" + q, cnt[q]) for q in cnt] + final:
+        if known["G"].get(s, 0) < x:
+            g.wait_ge(T.sem[s], x)

@@ -1,4 +1,3 @@
-from concourse.bass import DstId, RemoteDMATransfer
 from concourse.mybir import AluOpType as A, ActivationFunctionType as F
 
 SCRATCH = {}
@@ -8,31 +7,30 @@ def _b(n, c, d="bfloat16", w="sbuf", p=128):
     SCRATCH[n] = (w, [p, c], d)
 
 
-for _n, _c in (("X", 2048), ("G", 4368), ("FB", 128), ("HB", 128), ("cS", 4096), ("cA", 4096), ("AB", 4096), ("AC", 4096),
-               ("E", 4096), ("mI", 128), ("mNI", 128), ("SG", 128), ("SGf", 128), ("SGh", 128), ("SGp", 128), ("ZE", 144),
-               ("ZW", 144), ("ZL", 144), ("ZA", 144), ("TRI", 128), ("Fa", 2048), ("Ff", 2048), ("Fh", 2048), ("LTm", 2048),
-               ("WR1", 128), ("WR2", 128), ("REP", 512), ("KBS", 48), ("KBA", 24), ("PH", 256), ("PL", 256), ("ONE", 128),
-               ("CRS", 512), ("CRA", 256), ("ZROW", 256), ("RR", 512), ("blB", 16), ("scB", 16), ("hpB", 16), ("fpB", 16),
-               ("vhB", 16), ("vlB", 16), ("shB", 256), ("slB", 256), ("zt", 256), ("WTS", 256), ("WTA", 256), ("goal", 256),
-               ("PB", 48), ("T16", 512), ("Z0", 256), ("Z1", 256), ("Z2", 256), ("Z3", 256), ("AN0", 256), ("AN1", 256),
-               ("LN0", 256), ("LN1", 256), ("QZ0", 256), ("QZ1", 256)):
+for _n, _c in (("X", 2048), ("G", 4368), ("HF", 4352), ("cS", 4096), ("AB", 4096), ("cA", 1792), ("AC", 1792), ("E", 4096),
+               ("mI", 128), ("mNI", 128), ("m48", 128), ("SG", 128), ("SGp", 16), ("SGc", 16), ("LTm", 128), ("ZE", 144),
+               ("ZK", 144), ("ZC", 144), ("ZS", 432), ("TRI", 128), ("WX", 128), ("REP", 512), ("KBS", 48), ("ONE", 256),
+               ("NR", 16), ("CRS", 512), ("BR", 128), ("JL", 256), ("BM", 512), ("V0", 128), ("RR", 256), ("RH", 512),
+               ("blB", 16), ("scB", 16), ("hB", 256), ("zt", 256), ("WTS", 256), ("WTA", 128), ("goal", 256), ("zc", 112),
+               ("gk", 112), ("CR", 512), ("PB", 32), ("HV", 256), ("LX", 256), ("SA", 128), ("SB", 128),
+               ("Z0", 256), ("Z1", 256), ("Z2", 256), ("Z3", 256), ("AN0", 128), ("AN1", 128), ("LN0", 128), ("LN1", 128),
+               ("QZ0", 256), ("QZ1", 256)):
     _b(_n, _c)
-for _n, _c in (("HF", 2304), ("JX", 144), ("JG", 128), ("JM", 128), ("JPH", 256), ("JPL", 256), ("JR", 512), ("RA", 128),
-               ("RB", 128), ("J16", 16), ("KB2", 16), ("COL", 128), ("OH", 16), ("LT", 16), ("LA", 48), ("W1", 128),
-               ("ZR16", 16), ("LL", 512), ("KU", 256), ("K1", 256), ("K2", 128), ("K3", 64), ("HV", 256),
-               ("aF0", 48), ("aF1", 48), ("aF2", 48), ("aF3", 48), ("UV0", 32), ("UV1", 32), ("QU0", 32), ("QU1", 32)):
+for _n, _c in (("mIh", 128), ("ZA", 144), ("RP", 128), ("s16", 256), ("T16", 256)):
+    _b(_n, _c, "float16")
+for _n, _c in (("COL", 128), ("OH", 16), ("LA", 48), ("W1", 128), ("W2", 128), ("ZR16", 16), ("LL", 512), ("KS", 512), ("KT", 128),
+               ("aF", 16), ("Y1", 112), ("Y2", 112), ("YA", 256), ("YH", 128), ("YF", 128)):
     _b(_n, _c, "float32")
-for _n, _c in (("SU", 2048), ("IOT", 2048), ("FI", 128), ("HI", 128), ("aI", 16), ("CI", 8), ("LI", 320), ("TI", 256), ("TJ", 256),
-               ("sI", 256), ("sJ", 512), ("KI", 48), ("KJ", 48)):
+for _n, _c in (("SI", 4096), ("FI", 128), ("HI", 128), ("aI", 16), ("CI", 8), ("LI", 256), ("JG", 128), ("JR", 512),
+               ("TI", 128), ("TJ", 128), ("TK", 128), ("KI", 64), ("KQ", 32)):
     _b(_n, _c, "int32")
-for _n, _c in (("aU0", 16), ("aU1", 16), ("aU2", 16), ("aU3", 16), ("AR", 256), ("sU", 256), ("gU", 16), ("nU", 48),
-               ("qU", 16), ("CL0", 256), ("CL1", 256), ("QC0", 256), ("QC1", 256), ("QA0", 16), ("QA1", 16)):
+for _n, _c in (("aU0", 32), ("aU1", 32), ("aU2", 32), ("AR", 256), ("sU", 256), ("gU", 16), ("nU", 32), ("pU", 16), ("vU", 16),
+               ("cU", 16), ("jU", 16), ("qU", 8), ("CC", 112), ("CL0", 8), ("CL1", 8), ("QL0", 8), ("QL1", 8), ("QA0", 16), ("QA1", 16)):
     _b(_n, _c, "uint16")
-for _n in ("D0", "D1", "D2", "KEY", "PLB", "ML", "WTP", "TR"):
+for _n in ("D0", "D1", "D2", "D3", "KEY", "ML", "TR", "KA"):
     _b(_n, 512, "float32", "psum")
-SEMAPHORES = ["eV", "eS", "eP", "eG", "sent", "l_a", "l_z", "l_h", "l_f", "l_s", "l_x", "l_g", "o_z", "o_a", "o_h", "o_f",
-              "r_z0", "r_z1", "r_c0", "r_c1", "r_u0", "r_u1", "r_a0", "r_a1", "r_n0", "r_n1"]
-STEPS = 3
+SEMAPHORES = ["eV", "eS", "eP", "eG", "sent", "l_a", "l_z", "l_h", "l_f", "l_s", "l_x", "l_g", "l_p", "l_q", "o_z", "o_a", "o_h", "o_f",
+              "r_z0", "r_z1", "r_l0", "r_l1", "r_a0", "r_a1", "r_n0", "r_n1"]
 
 
 def rank_program(g, core, T, topo):
@@ -124,6 +122,9 @@ def rank_program(g, core, T, topo):
         else:
             op("V", lambda: g.vector.tensor_scalar(out=ap(out), in0=ap(a), scalar1=ap(s1), scalar2=ap(s2), op0=o1, op1=o2), out, a, s1, s2)
 
+    def scan(out, a, b, o0, o1):
+        op("V", lambda: g.vector.tensor_tensor_scan(out=ap(out), data0=ap(a), data1=ap(b), initial=0.0, op0=o0, op1=o1), out, a, b)
+
     def act(out, in_, f=F.Copy, scale=1.0):
         op("S", lambda: g.scalar.activation(out=ap(out), in_=ap(in_), func=f, scale=ap(scale)), out, in_, scale)
 
@@ -131,7 +132,10 @@ def rank_program(g, core, T, topo):
         op("P", lambda: g.tensor.matmul(ap(out), ap(lhsT), ap(rhs), start, stop), out, lhsT, rhs)
 
     def iota(out, pat, base=0, mult=0):
-        op("G", lambda: g.iota(ap(out), pat, base, mult, allow_small_or_imprecise_dtypes=True), out)
+        if SCRATCH[out[0]][2] == "int32":
+            op("G", lambda: g.iota(ap(out), pat, base, mult), out)
+        else:
+            op("G", lambda: g.iota(ap(out), pat, base, mult, allow_small_or_imprecise_dtypes=True), out)
 
     def fill(out, x):
         op("V", lambda: g.vector.memset(ap(out), x), out)
@@ -142,384 +146,532 @@ def rank_program(g, core, T, topo):
 
     final, sent = [], [0]
 
-    def store(out, in_, sem, row=None):
-        deps("Y", [], [in_])
-        src = ap(in_) if row is None else T[in_[0]][row:128:16, in_[1]:in_[2]]
-        g.sync.dma_start(out=out, in_=src).then_inc(T.sem[sem], 16)
+    def store(q, out, in_, sem):
+        deps(q, [], [in_])
+        H[q].dma_start(out=out, in_=ap(in_)).then_inc(T.sem[sem], 16)
         final.append((sem, 16))
 
-    def send(dst, parts):
-        to = T.cores[dst]
+    def send(dst, src, buf, sem):
+        to = T.cores[dst % n]
         rid, pid = topo.addr(to)[0], topo.addr(to)[1]
         e = topo.engines(core, to)[:8]
-        deps("G", [], [p[0] for p in parts])
-        m = [sum(1 << x for x in e[k::len(parts)]) for k in range(len(parts))]
+        deps("G", [], [src])
         sent[0] += len(e)
-        if len(parts) == 1:
-            s, d, sem = parts[0]
-            g.remote_dma(ap(v(d)), ap(s), T.sem[sem], T.sem.sent, pid, rid, m[0])
-        else:
-            g.remote_dma_fused([RemoteDMATransfer(dst_ids=[DstId(rid=rid, pnc=pid)], dma_engine_mask=m[k], remote_sem=T.sem[sem],
-                                                  src=ap(s), dst=ap(v(d))) for k, (s, d, sem) in enumerate(parts)], local_sem=T.sem.sent)
+        g.remote_dma(ap(v(buf)), ap(src), T.sem[sem], T.sem.sent, pid, rid, sum(1 << x for x in e))
 
-    def arrive(buf, sem, src, parts):
-        e = len(topo.engines(T.cores[src], core)[:8]) // parts
+    def arrive(buf, sem, src):
+        e = len(topo.engines(T.cores[src % n], core)[:8])
         wr[buf] = [(0, SCRATCH[buf][1][1], ("R", sem, e, {}, True))]
 
     load("Y", v("aI"), T.a0[:, :], "l_a")
-    load("S", v("Z0"), T.z0[:, :], "l_z")
-    load("Y", v("SU"), T.su[:, :], "l_s")
-    load("S", v("HI"), T.hd0[:, :], "l_h")
     load("S", v("FI"), T.fl0[:, :], "l_f")
-    load("Y", v("X"), T.xs[:, :], "l_x")
-    load("S", v("G", 0, 4096), T.gs[:, :], "l_g")
+    load("Y", v("HI"), T.hd0[:, :], "l_h")
+    load("S", v("Z0"), T.z0[:, :], "l_z")
+    load("Y", v("SI", 0, 2048), T.su[:, :], "l_s")
+    load("S", v("X"), T.xs[:, :], "l_x")
+    load("Y", v("G", 0, 4096), T.gs[:, :], "l_g")
     for t in range(2):
-        p, q = (rank - 1 - t) % n, (rank + 1 + t) % n
-        for b, c in (("QZ", 2), ("QC", 2), ("QU", 1), ("QA", 1)):
-            arrive(b + str(t), "r_" + b[1].lower() + str(t), p, c)
-        arrive("LN%d" % t, "r_n%d" % t, q, 1)
+        for b in ("QZ", "QA", "QL"):
+            arrive(b + str(t), "r_" + b[1].lower() + str(t), rank - 1 - t)
+        arrive("LN%d" % t, "r_n%d" % t, rank + 1 + t)
 
-    iota(v("CI", 0, 1), [[0, 1]], 0, 1)
-    iota(v("JX"), [[1, 144]])
-    iota(v("J16"), [[1, 16]])
-    iota(v("JG"), [[1, 8], [0, 16]])
-    iota(v("RA"), [[0, 8], [8, 4], [0, 4]])
-    iota(v("RB"), [[0, 32], [2, 4]], 1)
-    iota(v("IOT"), [[1, 2048]])
-    iota(v("JR"), [[1, 32], [0, 16]])
-    iota(v("KB2"), [[0, 2], [1, 8]])
-    iota(v("CRA", p0=0, p1=1), [[1, 16], [0, 16]])
-    iota(v("CRS", p0=0, p1=1), [[64, 16], [0, 32]])
-    iota(v("JPH"), [[1, 16], [1000, 2], [16, 8]])
-    iota(v("JPL"), [[1, 16], [1000, 2], [16, 8]], -1000)
+    def J(a, b):
+        return v("SI", 2048 + a, 2048 + b)
 
     def col(k):
         return v("COL", 4 * k, 4 * k + 1)
-    (pF, pm, pg, g0, g1, g15, wi, wE, c1, p8, p31, w8) = [col(k) for k in range(12)]
+    (pF, pm, pg, g15, wi, k15, c15, p31, ycol, rcol, pg8, c1) = [col(k) for k in range(12)]
+    one_row = v("ONE", 0, 128, 1, 0, 1)
 
-    def cands(t, part):
-        z, uv, o, r = "Z%d" % t, "UV%d" % t, v("ML", 96, 112), "TR"
-        li = [v("LI", 16 * k, 16 * k + 16) for k in range(8)]
+    def constants(part):
         if part == 0:
-            for i in range(16):
-                mm(o, v("ZW", 15 - i, 143 - i), v(z, i, 256, 16), i == 0, i == 15)
+            iota(v("CI", 0, 1), [[0, 1]], 0, 1)
+            iota(J(0, 512), [[1, 512]])
+            iota(v("JG"), [[1, 8], [0, 16]])
+            iota(J(1536, 2048), [[1, 512]], 1536)
+            iota(v("TI"), [[0, 16], [1, 8]])
+            iota(v("TJ"), [[1, 16], [0, 8]])
+            iota(v("TK"), [[0, 8], [1, 16]])
+            iota(v("JL"), [[1, 256]])
+            fill(v("HF", 2048, 4352), 0.0)
+            vcopy(pF, v("CI", 0, 1))
+            bits = ((pm, A.bitwise_and, 15), (pg, A.logical_shift_right, 4), (p31, A.bitwise_and, 31))
+            for j, (out, o, s) in enumerate(bits):
+                ts(v("CI", 1 + j, 2 + j), v("CI", 0, 1), s, o)
+            fill(v("ONE"), 1.0)
+            for j, (out, o, s) in enumerate(bits):
+                vcopy(out, v("CI", 1 + j, 2 + j))
+            ts(J(512, 1024), J(0, 512), 512.0, A.add)
+            ts(v("OH"), J(0, 16), pm, A.is_equal)
+            ts(v("SG"), v("JG"), pg, A.is_equal)
+            ts(J(1024, 1536), J(0, 512), 1024.0, A.add)
         if part == 1:
-            vcopy(li[0], o)
-            ts(li[1], li[0], 4095, A.bitwise_and)
-            tt(li[2], li[1], li[1], A.mult)
-            ts(li[3], li[2], 5, A.logical_shift_right)
-            ts(li[4], li[3], 4095, A.bitwise_and)
-            ts(li[5], li[4], 6, A.logical_shift_right)
-            ts(li[6], li[4], 63, A.bitwise_and)
-            ts(v("vhB"), li[5], 64.0, A.mult)
-            vcopy(v("vlB"), li[6])
-            mm(v(r, 0, 256), v("WR1"), v(z), True, False)
-            mm(v(r, 0, 256), v("WR2"), v(z), False, False)
-            for i in range(16):
-                for b in ("vhB", "vlB"):
-                    mm(v(r, i, 256, 16), v("Fa", 128 * i, 128 * i + 128), v(b), False, i == 15 and b == "vlB")
+            fill(v("NR", 0, 8), 0.0)
+            fill(v("NR", 8, 16), -1.0)
+            ts(pg8, pg, 8.0, A.add)
+            ts(v("SGp"), J(0, 16), pg, A.is_equal)
+            ts(v("SGc"), J(0, 16), pg8, A.is_equal)
+            ts(g15, pg, 16.0, A.mult, 15.0, A.add)
+            tt(v("SGp"), v("SGp"), v("SGc"), A.add)
         if part == 2:
-            vcopy(v("TI"), v(r, 0, 256))
-            ts(v("TJ"), v("TI"), 4095, A.bitwise_and)
-            vcopy(v("CL%d" % t), v("TJ"))
-            q = (rank + 1 + t) % n
-            send(q, [(v(z), "QZ%d" % t, "r_z%d" % t), (v("CL%d" % t), "QC%d" % t, "r_c%d" % t)])
-            vcopy(v(uv, 0, 16), li[1])
-            vcopy(v(uv, 16, 32), li[4])
-            send(q, [(v(uv), "QU%d" % t, "r_u%d" % t)])
+            ts(k15, pF, 16.0, A.mult, 15.0, A.add)
+            ts(v("W1"), v("TI"), pg, A.is_equal)
+            ts(c15, k15, -128.0, A.add)
+            ts(v("W2"), v("TJ"), pm, A.is_gt)
+            ts(v("ZK"), J(0, 144), k15, A.is_equal)
+            tt(v("LTm"), v("W1"), v("W2"), A.mult)
+            ts(v("ZE"), J(0, 144), g15, A.is_equal, 0.0625, A.mult)
+            ts(v("ZC"), J(0, 144), c15, A.is_equal)
+        if part == 3:
+            ts(v("mI"), J(0, 128), pF, A.is_equal)
+            ts(v("W1"), v("TK"), pm, A.is_gt, -1.0, A.add)
+            ts(v("LA", 32, 48), J(0, 16), 16.0, A.mult, pm, A.add)
+            ts(v("W2"), v("mI"), -511.0, A.mult)
+            tt(v("W1"), v("W1"), v("SG"), A.mult)
+            ts(v("LA", 0, 16), v("LA", 32, 48), 4112.0, A.add)
+            ts(v("LA", 16, 32), v("LA", 32, 48), 4096.0, A.add)
+            tt(v("TRI"), v("W1"), v("W2"), A.add)
+            ts(v("LA", 32, 48), v("LA", 32, 48), -255.0, A.add)
+            fill(v("ZR16"), 0.0)
+            fill(v("CR", 0, 128), 0.0)
+            fill(v("G", 4096, 4112), 0.0)
+        if part == 4:
+            iota(v("JR"), [[1, 32], [0, 16]])
+            iota(v("BR", p0=0, p1=1), [[0, 8], [128, 16]])
+            for h in range(2):
+                iota(v("CRS", 256 * h, 256 * h + 256, 1, 0, 1), [[6304, 2], [0, 8], [64, 16]], -128)
+            ts(wi, pm, 2.0, A.mult, 1.0, A.add)
+            act(v("mNI"), v("mI"), scale=-1.0)
+            act(v("m48"), v("mI"), scale=-48.0)
+            act(v("WX"), v("SG"), scale=wi)
+            for k, f in enumerate((1.0, 2.0, -1.0)):
+                act(v("KBS", 16 * k, 16 * k + 16), v("SGp"), scale=1024.0 * f)
+                act(v("ZS", 144 * k, 144 * k + 144), v("ZE"), scale=32768.0 * f)
+        if part == 5:
+            fill(v("BM"), 0.0)
+            tt(c1, wi, wi, A.mult)
+            fill(v("BM", 0, 512, 16), 33554432.0)
+            vcopy(v("mIh"), v("mI"))
+            vcopy(v("ZA"), v("ZK"))
+            ts(v("RP"), v("JG"), pF, A.is_equal)
+            ts(ycol, wi, 16.0, A.mult)
+            ts(rcol, c1, -8.0, A.mult, -0.40625, A.add)
+            ts(v("REP"), v("JR"), p31, A.is_equal)
+            ts(v("BR", p0=0, p1=1), v("BR", p0=0, p1=1), 1664.0, A.min)
 
-    def ask(t):
-        send((rank + 1 + t) % n, [(v("aU%d" % t), "QA%d" % t, "r_a%d" % t)])
+    def start():
+        vcopy(v("aU0", 0, 16), v("aI"))
+        ts(v("W1"), v("FI"), 2.0, A.mult)
+        vcopy(v("aF"), v("aI"))
+        tt(v("V0"), v("W1"), v("HI"), A.add)
+        ts(v("aU0", 16, 32), v("aI"), 2048.0, A.add)
+        vcopy(v("AR"), ind(J(0, 2048), v("aU0", 0, 16)))
+        send(rank + 1, v("aU0", 0, 16), "QA0", "r_a0")
+        send(rank + 1, v("Z0"), "QZ0", "r_z0")
+        for b in range(4):
+            for k in range(4 * b, 4 * b + 4):
+                act(v("AB", 128 * k, 128 * k + 128), v("V0"), scale=v("OH", k, k + 1))
+            mm(v("D%d" % b), v("SG"), v("AB", 512 * b, 512 * b + 512), True, True)
+        for b in range(4):
+            act(v("HF", 512 * b, 512 * b + 512), v("D%d" % b))
 
-    vcopy(pF, v("CI", 0, 1))
-    for j, (out, o, s) in enumerate(((pm, A.bitwise_and, 15), (pg, A.logical_shift_right, 4), (p8, A.bitwise_and, 7),
-                                     (p31, A.bitwise_and, 31))):
-        ts(v("CI", 1 + j, 2 + j), v("CI", 0, 1), s, o)
-        vcopy(out, v("CI", 1 + j, 2 + j))
-    ts(g15, pg, 16.0, A.mult, 15.0, A.add)
-    ts(wi, pm, 2.0, A.mult, 1.0, A.add)
-    ts(v("ZW"), v("JX"), g15, A.is_equal, wi, A.mult)
-    ts(v("SG"), v("JG"), pg, A.is_equal)
-    ts(v("OH"), v("J16"), pm, A.is_equal)
-    cands(0, 0)
-    for i in range(16):
-        act(v("Fa", 128 * i, 128 * i + 128), v("SG"), scale=v("OH", i, i + 1))
-    vcopy(v("aU0"), v("aI"))
-    ask(0)
-    ts(g0, pg, 16.0, A.mult)
-    ts(g1, g0, 1.0, A.add)
-    ts(v("SGf"), v("JX", 0, 128), g0, A.is_equal)
-    ts(v("SGh"), v("JX", 0, 128), g1, A.is_equal)
-    ts(v("LT"), v("J16"), pm, A.is_gt)
-    for i in range(16):
-        act(v("Ff", 128 * i, 128 * i + 128), v("SGf"), scale=v("OH", i, i + 1))
-        act(v("Fh", 128 * i, 128 * i + 128), v("SGh"), scale=v("OH", i, i + 1))
-    for r, w in (("RA", "WR1"), ("RB", "WR2")):
-        ts(v("W1"), v(r), wi, A.mult)
-        tt(v(w), v("W1"), v("SG"), A.mult)
-    cands(0, 1)
-    cands(0, 2)
-    vcopy(v("HB"), v("HI"))
-    vcopy(v("FB"), v("FI"))
-    for b in range(4):
-        d = "D%d" % (b % 3)
-        for k in range(4):
-            i = 4 * b + k
-            mm(v(d, 128 * k, 128 * k + 128), v("Ff", 128 * i, 128 * i + 128), v("FB"), True, False)
-            mm(v(d, 128 * k, 128 * k + 128), v("Fh", 128 * i, 128 * i + 128), v("HB"), False, True)
-        act(v("HF", 512 * b, 512 * b + 512), v(d))
-    vcopy(v("aF0", 16, 32), v("aI"))
-    vcopy(v("aF0", 32, 48), v("aI"))
-    fill(v("ONE"), 1.0)
-    fill(v("ZROW"), 0.0)
-    fill(v("ZR16"), 0.0)
-    fill(v("G", 4096, 4112), 0.0)
-    tt(v("SGp"), v("SGf"), v("SGh"), A.add)
-    for i in range(1, 16):
-        act(v("LTm", 128 * i, 128 * i + 128), v("SGf"), scale=v("LT", i, i + 1))
+    def lists(o, zs, src, c1, rows=128):
+        for i in range(16):
+            mm(o, v(zs, 15 - i, 143 - i, 1, 0, rows), v(src, i, c1, 16, 0, rows), i == 0, i == 15)
 
-    def late_constants():
-        ts(wE, pm, 0.0, A.is_equal)
-        ts(c1, pm, 1.0, A.is_equal, 512.0, A.mult)
-        tt(wE, wE, c1, A.add)
-        ts(v("ZE"), v("JX"), g15, A.is_equal, wE, A.mult)
-        ts(v("mI"), v("JX", 0, 128), pF, A.is_equal)
-        act(v("mNI"), v("mI"), scale=-1.0)
-        ts(v("REP"), v("JR"), p31, A.is_equal)
-        ts(v("JM"), v("JG"), -16.0, A.mult)
-        tt(v("JM"), v("JM"), v("JX", 0, 128), A.add)
-        ts(v("W1"), v("JM"), pm, A.is_gt)
-        tt(v("TRI"), v("W1"), v("SG"), A.mult)
-        tt(v("TRI"), v("TRI"), v("SG"), A.subtract)
-        ts(v("LA", 0, 16), v("J16"), 16.0, A.mult, 4112.0, A.add)
-        ts(v("LA", 0, 16), v("LA", 0, 16), pm, A.add)
-        ts(v("LA", 16, 32), v("LA", 0, 16), -2064.0, A.add)
-        ts(v("LA", 32, 48), v("LA", 0, 16), -2064.0, A.add)
-        for k, f in enumerate((1.0, 2.0, -1.0)):
-            ts(v("KBA", 8 * k, 8 * k + 8), v("KB2", 0, 8), pg, A.is_equal, 16.0 * f, A.mult)
-            ts(v("KBS", 16 * k, 16 * k + 16), v("KB2"), pg, A.is_equal, 1024.0 * f, A.mult)
-        ts(c1, p8, 16.0, A.mult, 15.0, A.add)
-        ts(v("ZA"), v("JX"), c1, A.is_equal)
-        ts(w8, pF, 8.0, A.is_lt, 63.0, A.mult)
-        ts(w8, w8, 1.0, A.add)
-        ts(v("ZL"), v("ZA"), w8, A.mult)
-        ts(v("PH"), v("JPH"), pF, A.is_equal)
-        ts(v("PL"), v("JPL"), pF, A.is_equal)
+    L = [v("LL", 16 * x, 16 * x + 16) for x in range(32)]
+    (cb, fm1, ss, nn1, nn4, segf, t1, ask, q1, pn, mn1, fp, mn, w, n1s, e0, hp, v1, v2, pos, t2, t3) = L[:22]
+    put, wm, slot, base = L[24:28]
+    two, own = v("LL", 384, 416), v("LL", 416, 448)
+    mx, fi, hh, hs, hk, q8 = [v("LI", 16 * x, 16 * x + 16) for x in range(6)]
+    kP, oth, ro = v("ML", 32, 48), v("D1", 0, 16), v("ML", 64, 80)
+    aF, bank = v("aF"), v("G", 0, 4096)
+    turn = {"S": 0, "V": 0}
 
-    def gather(q, out, k0, k1, win, lst):
-        o, i = v(out, 512 * k0, 512 * k1), ind(win, v(lst, 32 * k0, 32 * k1))
+    def centres(q, c0, c1):
+        o, i = v("cS", c0, c1), ind(v("X"), v("sU", c0 // 16, c1 // 16))
         vcopy(o, i) if q == "V" else act(o, i)
 
-    def terms(bank, pos, neg):
-        for h in range(2):
-            o, s = v(bank, 128 * h, 128 * h + 128), (128 * h, 128 * h + 128)
-            mm(o, v(pos, *s), v("mI"), True, not neg)
-            if neg:
-                mm(o, v(neg, *s), v("mNI"), False, True)
+    def cands(q, c0, c1):
+        o, i = v("cA", c0, c1), ind(bank, v("CC", c0 // 16, c1 // 16))
+        vcopy(o, i) if q == "V" else act(o, i)
 
-    def dist(ab, src, term, order):
-        for k in order:
-            h, r = k // 4, 32 * (k % 4)
-            d = v(("D0", "D1")[k % 2] if h == 0 else ("D2", "WTP")[k % 2])
-            s, o = v(src, 512 * k, 512 * k + 512), v(ab, 512 * k, 512 * k + 512)
-            if h == 0:
-                mm(d, v("mNI"), s, True, False)
-            mm(d, v(term, 128 * h, 128 * h + 128, 1, r, r + 32), v("REP", p0=r, p1=r + 32), h == 1, True)
-            if h == 0:
-                act(o, d, F.Abs)
-            else:
-                tt(o, s, d, A.max)
+    def dist(ab, src, term, k, mode):
+        wd = min(512, SCRATCH[src][1][1] - 512 * k)
+        h, r = k // 4, 32 * (k % 4)
+        d = v("D%d" % (turn[mode] % 2 + (2 if mode == "V" else 0)), 0, wd)
+        turn[mode] += 1
+        s, o = v(src, 512 * k, 512 * k + wd), v(ab, 512 * k, 512 * k + wd)
+        if mode == "S":
+            mm(d, v("mNI"), s, True, False)
+        mm(d, v(term, 128 * h, 128 * h + 128, 1, r, r + wd // 16), v("REP", 0, wd, 1, r, r + wd // 16), mode == "V", True)
+        if mode == "S":
+            act(o, d, F.Abs)
+        else:
+            tt(o, s, d, A.max)
 
-    def sums(bank, src, h, kb, k, w, last):
+    def dS(*ks):
+        for k, mode in ks:
+            dist("AB", "cS", "WTS", int(k), mode)
+
+    def dA(*ks):
+        for k, mode in ks:
+            if mode == "V":
+                blocks("cA", int(k), 2)
+            dist("AC", "cA", "WTA", int(k), mode)
+
+    def sums(src, k0, k1, kb, stop=False):
+        h, r0, r1 = k0 // 4, 32 * (k0 % 4), 32 * ((k1 - 1) % 4 + 1)
         for m in range(16):
-            mm(v(bank, m * 2 * w + h, (m + 1) * 2 * w, 2), v(src, m + 2048 * h, 2048 * h + 2048, 16), v(kb, k * w, k * w + w), False,
-               last and m == 15)
+            mm(v("KEY", 256 * h + m, 256 * h + 256, 16, r0, r1), v(src, 512 * k0 + m, 512 * k1, 16), v("KBS", 16 * kb, 16 * kb + 16), False,
+               stop and m == 15)
 
-    def least(bank, w, k0):
-        u = 16 * w
-        vcopy(v("KU", 0, u), v(bank, u, 2 * u))
-        tt(v("K1", 0, u), v(bank, 0, u), v("KU", 0, u), A.min)
-        tt(v("K2", 0, u // 2), v("K1", 0, u // 2), v("K1", u // 2, u), A.min)
-        tt(v("K3", 0, u // 4), v("K2", 0, u // 4), v("K2", u // 4, u // 2), A.min)
-        tt(v("KI", k0, k0 + u // 8), v("K3", 0, u // 8), v("K3", u // 8, u // 4), A.min)
+    def blocks(src, k, kb, stop=False):
+        bs = range(4 * k, min(4 * k + 4, 14))
+        for b in bs:
+            mm(v("KA", 0, 128), v("ZS", 144 * kb + 15 - b, 144 * kb + 143 - b), v(src, 128 * b, 128 * b + 128), False, stop and b == bs[-1])
 
-    def turn(w, mask, k0, bank):
-        ts(v("KJ", k0, k0 + 2 * w), v("KI", k0, k0 + 2 * w), mask, A.bitwise_and)
-        vcopy(v("PB", k0, k0 + 2 * w), v("KJ", k0, k0 + 2 * w))
-        for h in range(2):
-            mm(v(bank, 256 + 128 * h, 384 + 128 * h, 1, 0, w), v("PB", k0 + h, k0 + 2 * w, 2), v("mI"), True, True)
+    def sA(*ks):
+        for k, mode in ks:
+            blocks("AC", int(k), 0 if mode == "S" else 1, (k, mode) == tuple(ks[-1]))
 
-    def row(w, k0, bank):
-        vcopy(v("T16", 8 * k0, 8 * k0 + 256, 1, 0, w), v(bank, 256, 512, 1, 0, w))
+    def succ(t):
+        vcopy(v("sU"), ind(v("SI", 0, 2048), v("aU%d" % t, 0, 16)))
 
-    def lists(w, k0, zs, o):
-        for i in range(16):
-            mm(o, v(zs, 15 - i, 143 - i, 1, 0, w), v("T16", 8 * k0 + i, 8 * k0 + 256, 16, 0, w), i == 0, i == 15)
+    def cells(t, part):
+        if part == 0:
+            act(v("RH"), ind(v("HF", 0, 4096), v("aU%d" % t)))
+        if part == 1:
+            lists(v("ML", 0, 32), "ZE", "RH", 512)
+        if part == 2:
+            vcopy(cb, v("ML", 16, 32))
+            ts(ss, aF, 2.0, A.mult)
+            tt(mx, v("ML", 0, 16), cb, A.max)
+            ts(fi, mx, 7, A.bitwise_and, 1, A.logical_shift_right)
+            ts(hh, mx, 1, A.bitwise_and)
+            ts(fm1, fi, -1.0, A.add)
 
-    for t in range(STEPS):
-        last = t == STEPS - 1
-        aF, aU, z, zn = "aF%d" % t, v("aU%d" % t), "Z%d" % t, "Z%d" % (t + 1)
-        aL, slot, bank = v(aF, 16, 32), v(aF, 0, 16), v("G", 0, 4096)
-        nn, ss, t1, segf, ask_, q1, n0, lf, pop, fm, ak, put, wA, n1 = [v("LL", 16 * x, 16 * x + 16) for x in range(14)]
-        three, t2 = v("LL", 176, 224), v("LL", 240, 256)
-        k, f, ct, hh, hs, hk = [v("LI", x, x + 16) for x in (224, 240, 256, 272, 128, 144)]
-        o, ro, mo, so = v("ML", 0, 32), v("ML", 64, 80), v("ML", 160, 176), v("ML", 128, 144)
+    def pl(a, b, st=1, rows=16):
+        return v("TR", a, b, st, 0, rows)
 
-        def keys():
-            mm(v("KEY"), v("ONE", p0=0, p1=1), v("CRS", p0=0, p1=1), True, False)
-            for h in range(2):
-                for b, w in (("shB", "PH"), ("slB", "PL")):
-                    mm(v("KEY", h, 512, 2), v(b, 128 * h, 128 * h + 128), v(w), False, False)
-            sums("KEY", "cS", 1, "KBS", 2, 16, False)
-
-        def ready():
-            terms("TR", zn, None)
-            vcopy(v("WTS"), v("TR", 0, 256))
-            mm(ro, v("SG"), v("scB"), True, False)
-            mm(ro, v("TRI"), v("blB"), False, True)
-
-        def decide():
-            ts(ask_, ro, 112.0, A.is_lt)
-            ts(pop, v("blB"), -1.0, A.mult, 1.0, A.add)
-            ts(q1, nn, 1.0, A.is_le)
-            ts(t1, nn, 1.0, A.add)
-            ts(n0, nn, 0.0, A.is_equal)
-            tt(ask_, ask_, v("blB"), A.mult)
-            ts(t2, nn, -1.0, A.mult, -1.0, A.add)
-            tt(lf, ct, k, A.subtract)
-            tt(fm, t1, ask_, A.mult)
-            tt(v("hpB"), n0, hk, A.is_equal)
-            tt(v("fpB"), t2, fm, A.max)
-            ts(lf, lf, 1.0, A.is_equal)
-            tt(put, q1, ask_, A.mult)
-            ts(n1, nn, 1.0, A.is_equal)
-            tt(lf, lf, pop, A.mult)
-            tt(ak, aL, v("blB"), A.mult)
-            tt(wA, n0, lf, A.max)
-            tt(n1, n1, ask_, A.mult)
-            ts(three, three, -1.0, A.mult, 1.0, A.add)
-            tt(three, three, v("LA"), A.mult)
-            tt(three, three, v(aF), A.max)
-            vcopy(v("nU"), three)
-
-        def values():
-            for i in range(16):
-                mm(v("TR", i, 256, 16), v("Ff", 128 * i, 128 * i + 128), v("fpB"), True, False)
-                mm(v("TR", i, 256, 16), v("Fh", 128 * i, 128 * i + 128), v("hpB"), False, True)
-            act(v("HV"), v("TR", 0, 256))
-
-        vcopy(v("AR"), ind(v("IOT"), aU))
-        mm(v("PLB", 0, 256), v("ONE", p0=0, p1=1), v("ZROW", p0=0, p1=1), True, False)
-        for c in range(16):
+    def compare(c0, c1):
+        if c0 == 0:
+            mm(pl(0, 256), v("NR", p0=0, p1=1), v("ONE", p0=0, p1=1), True, False)
+        for c in range(c0, c1):
             e = 256 * c
-            ts(v("E", e, e + 256), v("AR"), v(aF, 16 + c, 17 + c), A.is_equal)
-            mm(v("PLB", 0, 16 * c + 16), v("SGh"), v("E", e, e + 16 * c + 16), False, False)
+            ts(v("E", e, e + 256), v("AR"), v("aF", c, c + 1), A.is_equal)
+            mm(pl(0, 16 * c + 16), v("SGc"), v("E", e, e + 16 * c + 16), False, False)
             if c < 15:
-                mm(v("PLB", 16 * c + 16, 256), v("SGp"), v("E", e + 16 * c + 16, e + 256), False, False)
-            if c == 1:
-                vcopy(v("sI"), ind(v("SU"), aU))
-                vcopy(v("sU"), v("sI"))
-                gather("S", "cS", 4, 8, v("X"), "sU")
-        if t == 0:
-            late_constants()
+                mm(pl(16 * c + 16, 256), v("SGp"), v("E", e + 16 * c + 16, e + 256), False, False)
+
+    def places():
         for i in range(1, 16):
-            mm(v("PLB", i, 256, 16), v("LTm", 128 * i, 128 * i + 128), v("E", i, 4096, 272), False, i == 15)
-        act(v("RR", 0, 256), v("PLB", 0, 256))
-        ts(v("sJ", 0, 256), v("sI"), 6, A.logical_shift_right)
-        ts(v("sJ", 256, 512), v("sI"), 63, A.bitwise_and)
-        vcopy(v("shB"), v("sJ", 0, 256))
-        vcopy(v("slB"), v("sJ", 256, 512))
-        act(v("RR", 256, 512), ind(v("HF", 0, 2048), aU))
-        for i in range(16):
-            mm(o, v("ZE", 15 - i, 143 - i), v("RR", i, 512, 16), i == 0, i == 15)
-        if t:
-            vcopy(ind(v("G"), v("nU", 0, 16)), v("LN%d" % (t - 1)))
-        if last:
-            gather("S", "cS", 0, 3, v("X"), "sU")
-            gather("V", "cS", 3, 4, v("X"), "sU")
-        else:
-            act(v("goal"), ind(v("X"), v("QA%d" % t)))
-            gather("S", "cA", 0, 4, bank, "QC%d" % t)
-            gather("V", "cA", 4, 8, bank, "QC%d" % t)
-            terms("WTP", "goal", "QZ%d" % t)
-            ts(v("WTA"), v("WTP", 0, 256), -16.0, A.max, 16.0, A.min)
-        keys()
-        vcopy(v("LI", 192, 224), o)
-        ts(v("LI", 224, 256), v("LI", 192, 224), 511, A.bitwise_and)
-        ts(v("LI", 256, 288), v("LI", 192, 224), 9, A.logical_shift_right)
-        tt(nn, k, f, A.subtract)
-        tt(hs, hh, k, A.add)
-        ts(v("blB"), nn, 0.0, A.is_ge)
+            mm(pl(i, 256, 16, 8), v("LTm", 8 * i, 8 * i + 8), v("E", i, 4096, 272), False, i == 15)
+        vcopy(v("RR", p1=16), pl(0, 256))
+        lists(kP, "ZK", "RR", 256, 16)
+        lists(oth, "ZC", "RR", 256, 16)
+
+    def pops():
+        tt(nn1, kP, fm1, A.subtract)
+        tt(hs, kP, hh, A.add)
+        ts(v("blB"), nn1, 1.0, A.is_ge)
         ts(hk, hs, 1, A.bitwise_and)
-        ts(ss, aL, 2.0, A.mult)
-        ts(t1, v("blB"), 4096.0, A.mult)
+        scan(v("scB"), v("blB"), v("ZR16"), A.add, A.add)
+        ts(nn4, nn1, 4096.0, A.mult)
         tt(slot, ss, hk, A.add)
-        tt(segf, t1, slot, A.max)
-        vcopy(v("gU"), segf)
-        tt(v("zt"), ind(v("G", 0, 4112), v("gU")), v(z), A.add)
-        ts(v(zn), v("zt"), 0.0, A.max, 255.0, A.min)
-        op("V", lambda: g.vector.tensor_tensor_scan(out=ap(v("scB")), data0=ap(v("blB")), data1=ap(v("ZR16")), initial=0.0, op0=A.add, op1=A.add),
-           v("scB"), v("blB"), v("ZR16"))
-        if last:
-            store(T.yz[:, :], v(zn), "o_z")
-            ready()
-            decide()
-            dist("AB", "cS", "WTS", (0, 1, 4, 2, 5, 3, 6, 7))
-            sums("KEY", "AB", 0, "KBS", 0, 16, False)
-            sums("KEY", "AB", 1, "KBS", 1, 16, True)
-        else:
-            mm(v("PLB", 0, 256), v("ONE", p0=0, p1=1), v("CRA", p0=0, p1=1), True, False)
-            sums("PLB", "cA", 1, "KBA", 2, 8, False)
-            dist("AC", "cA", "WTA", (0, 4, 1, 5, 2, 3, 6, 7))
-            if t == 0:
-                cands(1, 0)
-            ready()
-            if t == 0:
-                cands(1, 1)
-            gather("S", "cS", 0, 4, v("X"), "sU")
-            if t == 0:
-                cands(1, 2)
-            sums("PLB", "AC", 0, "KBA", 0, 8, False)
-            sums("PLB", "AC", 1, "KBA", 1, 8, True)
-            decide()
-            dist("AB", "cS", "WTS", (4, 5))
-            values()
-            dist("AB", "cS", "WTS", (0, 6, 1, 7, 2, 3))
+        mm(ro, v("SG"), v("scB"), True, False)
+        mm(ro, v("TRI"), v("blB"), False, True)
+        tt(segf, nn4, slot, A.max)
+        tt(mn, oth, fi, A.min)
+        ts(v("gU"), segf, 4096.0, A.min)
+
+    def move(t, part):
+        if part == 0:
+            tt(v("zt"), ind(v("G", 0, 4112), v("gU")), v("Z%d" % t), A.add)
+            for h in range(2):
+                mm(v("TR", 128 * h, 128 * h + 128), v("zt", 128 * h, 128 * h + 128), v("mI"), True, True)
+        if part == 1:
+            ts(v("WTS"), v("TR", 0, 256), 0.0, A.max, 255.0, A.min)
+        if part == 2:
+            ts(v("Z%d" % (t + 1)), v("zt"), 0.0, A.max, 255.0, A.min)
+
+    def compact(t, part):
+        if part == 0:
+            tt(pos, ro, v("LA", 32, 48), A.min)
+            ts(v("cU"), pos, 511.0, A.add)
+            vcopy(ind(v("CR"), v("cU")), v("JL"))
+            lists(v("ML", 80, 88), "ZE", "CR", 128)
+        if part == 1:
+            vcopy(v("CL%d" % t), v("ML", 80, 88))
+            send(rank + 1 + t, v("CL%d" % t), "QL%d" % t, "r_l%d" % t)
+
+    def payload():
+        ts(t1, nn1, 1.0, A.is_ge, 2048.0, A.mult)
+        tt(t1, t1, aF, A.add)
+        vcopy(v("pU"), t1)
+        vcopy(v("s16"), ind(v("SI"), v("pU")))
+        ts(v("hB"), v("s16"), 1.0 / 48, A.mult, 128.0, A.add)
+
+    def keys(part):
+        if part == 0:
+            mm(v("KEY"), one_row, v("CRS", p0=0, p1=1), True, False)
+        if part == 1:
+            for h in range(2):
+                s = (128 * h, 128 * h + 128)
+                mm(v("KEY", 256 * h, 256 * h + 128), v("hB", *s), v("mI"), False, False)
+                mm(v("KEY", 256 * h + 128, 256 * h + 256), v("hB", *s), v("m48"), False, False)
+                mm(v("KEY", 256 * h + 128, 256 * h + 256), v("s16", *s), v("mIh"), False, False)
+
+    def decide(t, part):
+        if part == 0:
+            ts(ask, ro, -399.0, A.is_lt)
+            ts(q1, nn1, 2.0, A.is_le)
+            tt(w, kP, mn, A.is_equal)
+            tt(put, ask, q1, A.mult)
+            ts(e0, nn1, 1.0, A.is_equal)
+            ts(mn1, nn1, -1.0, A.mult)
+            tt(pn, put, nn1, A.mult)
+            tt(hp, e0, hk, A.is_equal)
+            tt(fp, mn1, pn, A.max)
+            ts(n1s, pn, 2.0, A.is_equal, 2048.0, A.mult)
+            ts(v1, fp, 2.0, A.mult, 8.0 * (t + 1), A.add)
+            tt(wm, w, n1s, A.max)
+            tt(v2, v1, hp, A.add)
+            tt(base, n1s, aF, A.add)
+            vcopy(v("vU"), v2)
+        if part == 1:
+            act(v("HV"), ind(v("JL"), v("vU")))
+        if part == 2:
+            ts(two, two, 0.0, A.is_equal)
+            if t < 2:
+                ts(q8, ro, 0.125, A.mult, 63.4375, A.add)
+            tt(two, two, v("LA", 0, 32), A.mult)
+            if t < 2:
+                ts(t2, q8, -7.9375, A.mult, 511.0, A.add)
+            tt(two, two, own, A.max)
+            if t < 2:
+                tt(t3, ro, t2, A.add)
+            vcopy(v("nU"), two)
+            if t < 2:
+                ts(v("jU"), t3, 16.0, A.mult, 127.0, A.min)
+        if part == 3:
             vcopy(ind(v("HF"), v("nU", 16, 32)), v("HV"))
-            least("PLB", 8, 32)
-            sums("KEY", "AB", 1, "KBS", 1, 16, False)
-            turn(8, 15, 32, "PLB")
-            vcopy(ind(v("HF"), v("nU", 32, 48)), v("HV"))
-            row(8, 32, "PLB")
-            sums("KEY", "AB", 0, "KBS", 0, 16, True)
-            lists(8, 32, "ZA", mo)
-        least("KEY", 16, 0)
-        turn(16, 63, 0, "TR")
-        if not last:
-            ts(t1, mo, 2.0, A.mult, 1.0, A.add)
-            tt(t1, t1, v("QU%d" % t, 0, 16), A.mult)
-            tt(v("LI", 160, 176), t1, v("QU%d" % t, 16, 32), A.add)
-            ts(v("LI", 176, 192), v("LI", 160, 176), 4095, A.bitwise_and)
-            vcopy(v("qU"), v("LI", 176, 192))
-            vcopy(v("AN%d" % t), ind(bank, v("qU")))
-            send((rank - 1 - t) % n, [(v("AN%d" % t), "LN%d" % t, "r_n%d" % t)])
-        row(16, 0, "TR")
-        lists(16, 0, "ZL", so)
-        if last:
-            values()
-            vcopy(ind(v("HF"), v("nU", 16, 32)), v("HV"))
-        aN = "aF%d" % (t + 1)
-        tt(t2, so, pop, A.mult)
-        tt(v(aN, 16, 32), t2, ak, A.add)
-        vcopy(v("aU%d" % (t + 1)), v(aN, 16, 32))
-        vcopy(v(aN, 32, 48), v(aN, 16, 32))
-        if t + 1 < STEPS - 1:
-            ask(t + 1)
-    vcopy(v("KU"), ind(v("IOT"), v("aU%d" % STEPS)))
-    store(T.ya[:, :], v("KU"), "o_a", 0)
-    vcopy(ind(v("HF"), v("nU", 32, 48)), v("HV"))
-    store(T.yh[:, :], v("HF", 0, 2048), "o_h", 1)
-    store(T.yf[:, :], v("HF", 0, 2048), "o_f", 0)
+
+    def refill(t, part):
+        if part == 0:
+            act(v("LX"), ind(v("LN%d" % t), v("jU")))
+        if part == 1:
+            vcopy(ind(v("G"), v("nU", 0, 16)), v("LX"))
+
+    def question(t, part):
+        ql = v("QL%d" % t, 0, 7)
+        if part == 0:
+            act(v("goal"), ind(v("X"), v("QA%d" % t)))
+        if part == 1:
+            act(v("zc"), ind(v("QZ%d" % t), ql))
+            act(v("gk"), ind(v("goal"), ql))
+        if part == 2:
+            mm(v("KA", 256, 368), v("WX"), v("zc"), True, True)
+            mm(v("KA", 384, 512, 1, 0, 112), v("gk"), v("mI"), True, False)
+            mm(v("KA", 384, 512, 1, 0, 112), v("zc"), v("mNI"), False, True)
+        if part == 3:
+            a, b = v("TI", 0, 112), v("TJ", 0, 112)
+            vcopy(a, v("KA", 256, 368))
+            ts(v("WTA", p1=112), v("KA", 384, 512, 1, 0, 112), -16.0, A.max, 16.0, A.min)
+            ts(b, a, 4095, A.bitwise_and)
+            ts(v("Y1"), b, ycol, A.add)
+            tt(v("Y2"), v("Y1"), v("Y1"), A.mult)
+            ts(a, v("Y2"), 0.03125, A.mult, rcol, A.add)
+            ts(b, a, 4095, A.bitwise_and)
+            vcopy(v("CC"), b)
+        if part == 4:
+            mm(v("KA", 0, 128), one_row, v("JL", 0, 128, 1, 0, 1), True, False)
+            mm(v("KA", 0, 128), v("BR", p0=0, p1=1), one_row, False, False)
+        if part == 5:
+            scan(v("KT"), v("BM", 0, 128), v("KA", 0, 128), A.add, A.min)
+            vcopy(v("KQ", 0, 8), v("KT", 15, 128, 16))
+            ts(v("KQ", 16, 24), v("KQ", 0, 8), 2047, A.bitwise_and)
+            vcopy(v("qU"), v("KQ", 16, 24))
+        if part == 6:
+            vcopy(v("AN%d" % t), ind(v("cA"), v("qU")))
+            send(rank - 1 - t, v("AN%d" % t), "LN%d" % t, "r_n%d" % t)
+
+    def least(t, part):
+        if part == 0:
+            scan(v("KS"), v("BM"), v("KEY"), A.add, A.min)
+            vcopy(v("KI", 0, 32), v("KS", 15, 512, 16))
+            ts(v("KI", 32, 64), v("KI", 0, 32), 63, A.bitwise_and)
+            vcopy(v("PB"), v("KI", 32, 64))
+            for h in range(2):
+                o = v("TR", 256 + 128 * h, 384 + 128 * h, 1, 0, 8)
+                mm(o, v("PB", 16 * h, 16 * h + 8), v("m48"), True, False)
+                mm(o, v("PB", 16 * h + 8, 16 * h + 16), v("mNI"), False, True)
+        if part == 1:
+            ts(v("YA" if t == 2 else "T16", p1=8), v("TR", 256, 512, 1, 0, 8), -1.0, A.mult, -32.0, A.add)
+            if t < 2:
+                mm(v("D2", 0, 256), v("RP", p1=8), v("T16", p1=8), True, True)
+                lists(v("ML", 96, 112), "ZA", "T16", 256, 8)
+        if part == 2:
+            vcopy(v("AR"), v("D2", 0, 256))
+        if part == 3:
+            aN = "aU%d" % (t + 1)
+            vcopy(v(aN, 0, 16), v("ML", 96, 112))
+            vcopy(aF, v("ML", 96, 112))
+            ts(v(aN, 16, 32), v("ML", 96, 112), 2048.0, A.add)
+
+    constants(0)
+    start()
+    constants(1)
+    compare(0, 16)
+    constants(2)
+    cells(0, 0)
+    places()
+    cells(0, 1)
+    constants(3)
+    cells(0, 2)
+    pops()
+    compact(0, 0)
+    decide(0, 0)
+    compact(0, 1)
+    constants(4)
+    decide(0, 1)
+    decide(0, 2)
+    succ(0)
+    centres("S", 0, 1024)
+    decide(0, 3)
+    question(0, 0)
+    centres("S", 1024, 2048)
+    constants(5)
+    payload()
+    centres("V", 3072, 4096)
+    question(0, 1)
+    question(0, 2)
+    centres("S", 2048, 3072)
+    question(0, 3)
+    keys(0)
+    keys(1)
+    sums("cS", 0, 2, 2)
+    sums("cS", 4, 8, 2)
+    question(0, 4)
+    move(0, 0)
+    cands("S", 0, 1024)
+    move(0, 1)
+    move(0, 2)
+    send(rank + 2, v("Z1"), "QZ1", "r_z1")
+    dS("4V", "5V", "6V")
+    cands("S", 1024, 1792)
+    dS("7V", "0V")
+    sums("AB", 4, 8, 1)
+    dS("2S", "1V", "3S")
+    sums("AB", 0, 2, 1, True)
+    dA("0S")
+    sums("AB", 2, 4, 0, True)
+    dA("1S")
+    least(0, 0)
+    dA("2S")
+    least(0, 1)
+    dA("3S")
+    least(0, 2)
+    sA("0S", "1S", "2S", "3S")
+    least(0, 3)
+    send(rank + 2, v("aU1", 0, 16), "QA1", "r_a1")
+    cells(1, 0)
+    succ(1)
+    question(0, 5)
+    centres("S", 2048, 3072)
+    question(0, 6)
+    compare(0, 6)
+    cells(1, 1)
+    compare(6, 11)
+    cells(1, 2)
+    compare(11, 16)
+    centres("S", 3072, 4096)
+    places()
+    refill(0, 0)
+    centres("S", 0, 1024)
+    pops()
+    compact(1, 0)
+    refill(0, 1)
+    compact(1, 1)
+    question(1, 0)
+    centres("S", 1024, 2048)
+    keys(0)
+    sums("cS", 4, 8, 2)
+    move(1, 0)
+    payload()
+    move(1, 1)
+    move(1, 2)
+    dS("4V", "0S", "5V", "1S")
+    keys(1)
+    question(1, 1)
+    dS("6V", "2S", "7V", "3S")
+    question(1, 2)
+    sums("AB", 4, 8, 1)
+    sums("AB", 0, 3, 0, True)
+    sums("AB", 3, 4, 0, True)
+    question(1, 3)
+    cands("S", 0, 1024)
+    least(1, 0)
+    question(1, 4)
+    decide(1, 0)
+    cands("S", 1024, 1792)
+    least(1, 1)
+    decide(1, 2)
+    least(1, 2)
+    decide(1, 1)
+    dA("0S", "1S")
+    least(1, 3)
+    succ(2)
+    dA("2V", "3S")
+    decide(1, 3)
+    sA("0S", "1S", "2V", "3S")
+    cells(2, 0)
+    question(1, 5)
+    question(1, 6)
+    centres("S", 2048, 3072)
+    compare(0, 8)
+    cells(2, 1)
+    compare(8, 13)
+    cells(2, 2)
+    compare(13, 16)
+    centres("S", 3072, 4096)
+    places()
+    centres("V", 0, 512)
+    pops()
+    refill(1, 0)
+    centres("S", 1024, 2048)
+    keys(0)
+    sums("cS", 4, 8, 2)
+    payload()
+    centres("V", 512, 1024)
+    keys(1)
+    refill(1, 1)
+    move(2, 0)
+    decide(2, 0)
+    move(2, 1)
+    decide(2, 1)
+    decide(2, 2)
+    move(2, 2)
+    store("Y", T.yz[:, :], v("Z3"), "o_z")
+    dS("0S", "4V", "1S", "5V")
+    decide(2, 3)
+    for b, c0, s in (("SA", 0, "l_p"), ("SB", 2048, "l_q")):
+        deps("Y", [v(b)], [v("HF")])
+        load("Y", v(b), T.HF[0:128:16, c0:c0 + 2048], s)
+    dS("2S", "6V", "3S", "7V")
+    sums("AB", 0, 4, 0)
+    sums("AB", 4, 7, 1, True)
+    sums("AB", 7, 8, 1, True)
+    least(2, 0)
+    tt(v("TI"), v("SA"), v("SB"), A.max)
+    least(2, 1)
+    store("S", T.ya[:, :], v("YA", p1=8), "o_a")
+    ts(v("TJ"), v("TI"), 7, A.bitwise_and, 1, A.logical_shift_right)
+    ts(v("TK"), v("TI"), 1, A.bitwise_and)
+    vcopy(v("YF"), v("TJ"))
+    vcopy(v("YH"), v("TK"))
+    store("Y", T.yf[:, :], v("YF"), "o_f")
+    store("S", T.yh[:, :], v("YH"), "o_h")
     g.wait_ge(T.sem.sent, sent[0])
     for s, x in [("e" + q, cnt[q]) for q in cnt] + final:
         if known["G"].get(s, 0) < x:

@@ -7,30 +7,30 @@ def _b(n, c, d="bfloat16", w="sbuf", p=128):
     SCRATCH[n] = (w, [p, c], d)
 
 
-for _n, _c in (("X", 2048), ("G", 4368), ("HF", 4352), ("cS", 4096), ("AB", 4096), ("cA", 1792), ("AC", 1792), ("E", 4096),
-               ("mI", 128), ("mNI", 128), ("m48", 128), ("SG", 128), ("SGp", 16), ("SGc", 16), ("LTm", 128), ("ZE", 144),
-               ("ZK", 144), ("ZC", 144), ("ZS", 432), ("TRI", 128), ("WX", 128), ("REP", 512), ("KBS", 48), ("ONE", 256),
-               ("NR", 16), ("CRS", 512), ("BR", 128), ("JL", 256), ("BM", 512), ("V0", 128), ("RR", 256), ("RH", 512),
+for _n, _c in (("X", 2048), ("G", 4368), ("HF", 8448), ("cS", 4096), ("AB", 4096), ("cA", 1792), ("AC", 1792), ("E", 4096),
+               ("mI", 128), ("mNI", 128), ("m48", 128), ("SG", 128), ("G8", 128), ("LTm", 128), ("ZE", 144), ("NG", 128),
+               ("ZS", 432), ("TRI", 128), ("WX", 128), ("REP", 512), ("KBS", 48), ("ONE", 128), ("JG", 128), ("J8", 128), ("JR", 512),
+               ("BR", 128), ("JL", 256), ("BM", 512), ("BQ", 128), ("V0", 128), ("RR", 256), ("RH", 1024), ("TT", 128),
                ("blB", 16), ("scB", 16), ("hB", 256), ("zt", 256), ("WTS", 256), ("WTA", 128), ("goal", 256), ("zc", 112),
-               ("gk", 112), ("CR", 512), ("PB", 32), ("HV", 256), ("LX", 256), ("SA", 128), ("SB", 128),
+               ("gk", 112), ("CR", 512), ("PB", 32), ("HV", 256), ("LX", 256), ("SA", 512),
                ("Z0", 256), ("Z1", 256), ("Z2", 256), ("Z3", 256), ("AN0", 128), ("AN1", 128), ("LN0", 128), ("LN1", 128),
                ("QZ0", 256), ("QZ1", 256)):
     _b(_n, _c)
-for _n, _c in (("mIh", 128), ("ZA", 144), ("RP", 128), ("s16", 256), ("T16", 256)):
+for _n, _c in (("mIh", 128), ("RP", 128), ("s16", 256), ("T16", 256), ("TH", 128)):
     _b(_n, _c, "float16")
-for _n, _c in (("COL", 128), ("OH", 16), ("LA", 48), ("W1", 128), ("W2", 128), ("ZR16", 16), ("LL", 512), ("KS", 512), ("KT", 128),
-               ("aF", 16), ("Y1", 112), ("Y2", 112), ("YA", 256), ("YH", 128), ("YF", 128)):
+for _n, _c in (("COL", 128), ("OH", 16), ("LA", 48), ("W1", 128), ("W2", 256), ("ZR16", 16), ("LL", 512), ("KS", 512), ("KT", 128),
+               ("aF", 16), ("Y1", 112), ("Y2", 112), ("YA", 256), ("YH", 128), ("YF", 128), ("CK", 32), ("cb", 64)):
     _b(_n, _c, "float32")
-for _n, _c in (("SI", 4096), ("FI", 128), ("HI", 128), ("aI", 16), ("CI", 8), ("LI", 256), ("JG", 128), ("JR", 512),
+for _n, _c in (("SI", 4096), ("FI", 128), ("HI", 128), ("aI", 16), ("CI", 8), ("LI", 256),
                ("TI", 128), ("TJ", 128), ("TK", 128), ("KI", 64), ("KQ", 32)):
     _b(_n, _c, "int32")
-for _n, _c in (("aU0", 32), ("aU1", 32), ("aU2", 32), ("AR", 256), ("sU", 256), ("gU", 16), ("nU", 32), ("pU", 16), ("vU", 16),
+for _n, _c in (("aU0", 16), ("aU1", 64), ("aU2", 64), ("AR", 256), ("sU", 256), ("gU", 16), ("nU", 32), ("pU", 16), ("vU", 16),
                ("cU", 16), ("jU", 16), ("qU", 8), ("CC", 112), ("CL0", 8), ("CL1", 8), ("QL0", 8), ("QL1", 8), ("QA0", 16), ("QA1", 16)):
     _b(_n, _c, "uint16")
 for _n in ("D0", "D1", "D2", "D3", "KEY", "ML", "TR", "KA"):
     _b(_n, 512, "float32", "psum")
-SEMAPHORES = ["eV", "eS", "eP", "eG", "sent", "l_a", "l_z", "l_h", "l_f", "l_s", "l_x", "l_g", "l_p", "l_q", "o_z", "o_a", "o_h", "o_f",
-              "r_z0", "r_z1", "r_l0", "r_l1", "r_a0", "r_a1", "r_n0", "r_n1"]
+SEMAPHORES = ["eV", "eS", "eP", "eG", "sent", "l_a", "l_z", "l_h", "l_f", "l_s", "l_x", "l_g", "l_p0", "l_p1", "l_p2", "l_p3",
+              "o_z", "o_a", "o_h", "o_f", "r_z0", "r_z1", "r_l0", "r_l1", "r_a0", "r_a1", "r_n0", "r_n1"]
 
 
 def rank_program(g, core, T, topo):
@@ -128,6 +128,9 @@ def rank_program(g, core, T, topo):
     def act(out, in_, f=F.Copy, scale=1.0):
         op("S", lambda: g.scalar.activation(out=ap(out), in_=ap(in_), func=f, scale=ap(scale)), out, in_, scale)
 
+    def copy(q, out, in_):
+        vcopy(out, in_) if q == "V" else act(out, in_)
+
     def mm(out, lhsT, rhs, start, stop):
         op("P", lambda: g.tensor.matmul(ap(out), ap(lhsT), ap(rhs), start, stop), out, lhsT, rhs)
 
@@ -136,6 +139,9 @@ def rank_program(g, core, T, topo):
             op("G", lambda: g.iota(ap(out), pat, base, mult), out)
         else:
             op("G", lambda: g.iota(ap(out), pat, base, mult, allow_small_or_imprecise_dtypes=True), out)
+
+    def select(out, in_, pat, o, x, mult):
+        op("G", lambda: g.affine_select(ap(out), ap(in_), pat, o, x, 0, mult), out, in_)
 
     def fill(out, x):
         op("V", lambda: g.vector.memset(ap(out), x), out)
@@ -180,121 +186,118 @@ def rank_program(g, core, T, topo):
 
     def col(k):
         return v("COL", 4 * k, 4 * k + 1)
-    (pF, pm, pg, g15, wi, k15, c15, p31, ycol, rcol, pg8, c1) = [col(k) for k in range(12)]
-    one_row = v("ONE", 0, 128, 1, 0, 1)
+    (pF, pm, pg, g15, wi, p31, ycol, rcol, c1) = [col(k) for k in range(9)]
+    one_row = v("ONE", p1=1)
 
     def constants(part):
         if part == 0:
             iota(v("CI", 0, 1), [[0, 1]], 0, 1)
             iota(J(0, 512), [[1, 512]])
+            iota(v("JL"), [[1, 256]])
             iota(v("JG"), [[1, 8], [0, 16]])
             iota(J(1536, 2048), [[1, 512]], 1536)
-            iota(v("TI"), [[0, 16], [1, 8]])
-            iota(v("TJ"), [[1, 16], [0, 8]])
-            iota(v("TK"), [[0, 8], [1, 16]])
-            iota(v("JL"), [[1, 256]])
-            fill(v("HF", 2048, 4352), 0.0)
+            iota(v("J8"), [[0, 16], [1, 8]])
+            fill(v("HF", 2048, 4096), 0.0)
             vcopy(pF, v("CI", 0, 1))
             bits = ((pm, A.bitwise_and, 15), (pg, A.logical_shift_right, 4), (p31, A.bitwise_and, 31))
             for j, (out, o, s) in enumerate(bits):
                 ts(v("CI", 1 + j, 2 + j), v("CI", 0, 1), s, o)
-            fill(v("ONE"), 1.0)
+            fill(v("ZR16"), 0.0)
             for j, (out, o, s) in enumerate(bits):
                 vcopy(out, v("CI", 1 + j, 2 + j))
             ts(J(512, 1024), J(0, 512), 512.0, A.add)
-            ts(v("OH"), J(0, 16), pm, A.is_equal)
-            ts(v("SG"), v("JG"), pg, A.is_equal)
             ts(J(1024, 1536), J(0, 512), 1024.0, A.add)
-        if part == 1:
-            fill(v("NR", 0, 8), 0.0)
-            fill(v("NR", 8, 16), -1.0)
-            ts(pg8, pg, 8.0, A.add)
-            ts(v("SGp"), J(0, 16), pg, A.is_equal)
-            ts(v("SGc"), J(0, 16), pg8, A.is_equal)
+            ts(v("OH"), v("JL", 0, 16), pm, A.is_equal)
+            ts(v("SG"), v("JG"), pg, A.is_equal)
             ts(g15, pg, 16.0, A.mult, 15.0, A.add)
-            tt(v("SGp"), v("SGp"), v("SGc"), A.add)
+            ts(v("mI"), v("JL", 0, 128), pF, A.is_equal)
+            ts(v("NG"), v("JG"), pg, A.is_equal, -1.0, A.mult)
+        if part == 1:
+            ts(v("G8"), v("J8"), pg, A.is_equal)
+            select(v("LTm"), v("G8"), [[1, 16], [16, 8]], A.is_gt, 0.0, -1)
+            select(v("NG"), v("NG"), [[-1, 128]], A.is_ge, 0.0, 1)
+            select(v("TRI"), v("NG"), [[-1, 128]], A.not_equal, -512.0, 1)
         if part == 2:
-            ts(k15, pF, 16.0, A.mult, 15.0, A.add)
-            ts(v("W1"), v("TI"), pg, A.is_equal)
-            ts(c15, k15, -128.0, A.add)
-            ts(v("W2"), v("TJ"), pm, A.is_gt)
-            ts(v("ZK"), J(0, 144), k15, A.is_equal)
-            tt(v("LTm"), v("W1"), v("W2"), A.mult)
-            ts(v("ZE"), J(0, 144), g15, A.is_equal, 0.0625, A.mult)
-            ts(v("ZC"), J(0, 144), c15, A.is_equal)
-        if part == 3:
-            ts(v("mI"), J(0, 128), pF, A.is_equal)
-            ts(v("W1"), v("TK"), pm, A.is_gt, -1.0, A.add)
-            ts(v("LA", 32, 48), J(0, 16), 16.0, A.mult, pm, A.add)
-            ts(v("W2"), v("mI"), -511.0, A.mult)
-            tt(v("W1"), v("W1"), v("SG"), A.mult)
-            ts(v("LA", 0, 16), v("LA", 32, 48), 4112.0, A.add)
-            ts(v("LA", 16, 32), v("LA", 32, 48), 4096.0, A.add)
-            tt(v("TRI"), v("W1"), v("W2"), A.add)
-            ts(v("LA", 32, 48), v("LA", 32, 48), -255.0, A.add)
-            fill(v("ZR16"), 0.0)
+            ts(v("ZE"), v("JL", 0, 144), g15, A.is_equal, 0.0625, A.mult)
+            ts(v("LA", 32, 48), v("JL", 0, 16), 16.0, A.mult, pm, A.add)
             fill(v("CR", 0, 128), 0.0)
             fill(v("G", 4096, 4112), 0.0)
-        if part == 4:
+            ts(v("LA", 0, 16), v("LA", 32, 48), 4112.0, A.add)
+            ts(v("LA", 16, 32), v("LA", 32, 48), 8192.0, A.add)
+            ts(v("LA", 32, 48), v("LA", 32, 48), -255.0, A.add)
+        if part == 3:
             iota(v("JR"), [[1, 32], [0, 16]])
-            iota(v("BR", p0=0, p1=1), [[0, 8], [128, 16]])
-            for h in range(2):
-                iota(v("CRS", 256 * h, 256 * h + 256, 1, 0, 1), [[6304, 2], [0, 8], [64, 16]], -128)
+            iota(v("BR", p1=1), [[0, 8], [128, 16]])
+            iota(v("CK"), [[0, 2], [32, 2], [0, 8]])
+        if part == 4:
             ts(wi, pm, 2.0, A.mult, 1.0, A.add)
-            act(v("mNI"), v("mI"), scale=-1.0)
-            act(v("m48"), v("mI"), scale=-48.0)
-            act(v("WX"), v("SG"), scale=wi)
-            for k, f in enumerate((1.0, 2.0, -1.0)):
-                act(v("KBS", 16 * k, 16 * k + 16), v("SGp"), scale=1024.0 * f)
-                act(v("ZS", 144 * k, 144 * k + 144), v("ZE"), scale=32768.0 * f)
-        if part == 5:
-            fill(v("BM"), 0.0)
+            ts(v("mNI"), v("mI"), -1.0, A.mult)
+            ts(v("WX"), v("SG"), wi, A.mult)
             tt(c1, wi, wi, A.mult)
-            fill(v("BM", 0, 512, 16), 33554432.0)
-            vcopy(v("mIh"), v("mI"))
-            vcopy(v("ZA"), v("ZK"))
-            ts(v("RP"), v("JG"), pF, A.is_equal)
             ts(ycol, wi, 16.0, A.mult)
+            ts(v("m48"), v("mI"), -48.0, A.mult)
             ts(rcol, c1, -8.0, A.mult, -0.40625, A.add)
+            vcopy(v("mIh"), v("mI"))
+            for k, f in enumerate((1.0, 2.0, -1.0)):
+                ts(v("KBS", 16 * k, 16 * k + 16), v("G8", 0, 16), 1024.0 * f, A.mult)
+        if part == 5:
             ts(v("REP"), v("JR"), p31, A.is_equal)
-            ts(v("BR", p0=0, p1=1), v("BR", p0=0, p1=1), 1664.0, A.min)
+        if part == 6:
+            fill(v("ONE"), 1.0)
+            fill(v("BM"), -64.0)
+            ts(v("RP"), v("JG"), pF, A.is_equal)
+            fill(v("BM", 0, 512, 16), 33554432.0)
+            for k, f in enumerate((1.0, 2.0, -1.0)):
+                ts(v("ZS", 144 * k, 144 * k + 144), v("ZE"), 32768.0 * f, A.mult)
+            ts(v("BR", p1=1), v("BR", p1=1), 1664.0, A.min)
+            ts(v("BQ"), v("BM", 0, 128), 0.0, A.max)
+        if part == 7:
+            fill(v("HF", 4096, 6144), 0.0)
+        if part == 8:
+            fill(v("HF", 6144, 8448), 0.0)
 
     def start():
-        vcopy(v("aU0", 0, 16), v("aI"))
-        ts(v("W1"), v("FI"), 2.0, A.mult)
+        vcopy(v("aU0"), v("aI"))
+        ts(v("W1"), v("FI"), 2.0, A.mult, 2.0, A.add)
         vcopy(v("aF"), v("aI"))
         tt(v("V0"), v("W1"), v("HI"), A.add)
-        ts(v("aU0", 16, 32), v("aI"), 2048.0, A.add)
-        vcopy(v("AR"), ind(J(0, 2048), v("aU0", 0, 16)))
-        send(rank + 1, v("aU0", 0, 16), "QA0", "r_a0")
-        send(rank + 1, v("Z0"), "QZ0", "r_z0")
-        for b in range(4):
-            for k in range(4 * b, 4 * b + 4):
-                act(v("AB", 128 * k, 128 * k + 128), v("V0"), scale=v("OH", k, k + 1))
-            mm(v("D%d" % b), v("SG"), v("AB", 512 * b, 512 * b + 512), True, True)
-        for b in range(4):
-            act(v("HF", 512 * b, 512 * b + 512), v("D%d" % b))
+        vcopy(v("AR"), ind(J(0, 2048), v("aU0")))
+        for k in range(16):
+            act(v("AB", 128 * k, 128 * k + 128), v("V0"), scale=v("OH", k, k + 1))
 
-    def lists(o, zs, src, c1, rows=128):
+    def table(b):
+        mm(v("D%d" % b), v("SG"), v("AB", 512 * b, 512 * b + 512), True, True)
+        act(v("HF", 512 * b, 512 * b + 512), v("D%d" % b))
+
+    def lists(o, src, c1):
         for i in range(16):
-            mm(o, v(zs, 15 - i, 143 - i, 1, 0, rows), v(src, i, c1, 16, 0, rows), i == 0, i == 15)
+            mm(o, v("ZE", 15 - i, 143 - i), v(src, i, c1, 16), i == 0, i == 15)
+
+    def turn_a(src, c1, rows, sel):
+        for i in range(16):
+            mm(v("TR", 256 + i, 384, 16, 0, c1 // 16), v(src, i, c1, 16, 0, rows), v(sel, 0, 8, 1, 0, rows), True, True)
+
+    def turn_b(o, m, buf, ident, f=None):
+        if f:
+            ts(v(buf, p1=m), v("TR", 256, 384, 1, 0, m), f, A.mult)
+        else:
+            vcopy(v(buf, p1=m), v("TR", 256, 384, 1, 0, m))
+        mm(o, v(buf, p1=m), v(ident, 0, m, 1, 0, m), True, True)
 
     L = [v("LL", 16 * x, 16 * x + 16) for x in range(32)]
-    (cb, fm1, ss, nn1, nn4, segf, t1, ask, q1, pn, mn1, fp, mn, w, n1s, e0, hp, v1, v2, pos, t2, t3) = L[:22]
-    put, wm, slot, base = L[24:28]
+    (fm1, ss, nn1, nn4, segf, t1, ask2, popf, e0, hp, v1, v2, k3, pos, t2, t3, a1, a2) = L[:18]
+    nput, nw, slot, base = L[24:28]
     two, own = v("LL", 384, 416), v("LL", 416, 448)
     mx, fi, hh, hs, hk, q8 = [v("LI", 16 * x, 16 * x + 16) for x in range(6)]
-    kP, oth, ro = v("ML", 32, 48), v("D1", 0, 16), v("ML", 64, 80)
+    kP, ro, cP, aP = v("ML", 64, 80), v("ML", 80, 96), v("ML", 96, 104), v("ML", 112, 128)
     aF, bank = v("aF"), v("G", 0, 4096)
     turn = {"S": 0, "V": 0}
 
     def centres(q, c0, c1):
-        o, i = v("cS", c0, c1), ind(v("X"), v("sU", c0 // 16, c1 // 16))
-        vcopy(o, i) if q == "V" else act(o, i)
+        copy(q, v("cS", c0, c1), ind(v("X"), v("sU", c0 // 16, c1 // 16)))
 
     def cands(q, c0, c1):
-        o, i = v("cA", c0, c1), ind(bank, v("CC", c0 // 16, c1 // 16))
-        vcopy(o, i) if q == "V" else act(o, i)
+        copy(q, v("cA", c0, c1), ind(bank, v("CC", c0 // 16, c1 // 16)))
 
     def dist(ab, src, term, k, mode):
         wd = min(512, SCRATCH[src][1][1] - 512 * k)
@@ -316,60 +319,64 @@ def rank_program(g, core, T, topo):
 
     def dA(*ks):
         for k, mode in ks:
-            if mode == "V":
-                blocks("cA", int(k), 2)
             dist("AC", "cA", "WTA", int(k), mode)
 
-    def sums(src, k0, k1, kb, stop=False):
+    def sums(src, k0, k1, kb, start=False, stop=False):
         h, r0, r1 = k0 // 4, 32 * (k0 % 4), 32 * ((k1 - 1) % 4 + 1)
         for m in range(16):
-            mm(v("KEY", 256 * h + m, 256 * h + 256, 16, r0, r1), v(src, 512 * k0 + m, 512 * k1, 16), v("KBS", 16 * kb, 16 * kb + 16), False,
-               stop and m == 15)
+            mm(v("KEY", 256 * h + m, 256 * h + 256, 16, r0, r1), v(src, 512 * k0 + m, 512 * k1, 16), v("KBS", 16 * kb, 16 * kb + 16),
+               start and m == 0, stop and m == 15)
 
     def blocks(src, k, kb, stop=False):
         bs = range(4 * k, min(4 * k + 4, 14))
         for b in bs:
             mm(v("KA", 0, 128), v("ZS", 144 * kb + 15 - b, 144 * kb + 143 - b), v(src, 128 * b, 128 * b + 128), False, stop and b == bs[-1])
 
-    def sA(*ks):
+    def sA(*ks, stop=False):
         for k, mode in ks:
-            blocks("AC", int(k), 0 if mode == "S" else 1, (k, mode) == tuple(ks[-1]))
+            blocks("cA" if mode == "R" else "AC", int(k), "SVR".index(mode), stop and (k, mode) == tuple(ks[-1]))
 
     def succ(t):
         vcopy(v("sU"), ind(v("SI", 0, 2048), v("aU%d" % t, 0, 16)))
 
     def cells(t, part):
+        k = 4 if t else 1
         if part == 0:
-            act(v("RH"), ind(v("HF", 0, 4096), v("aU%d" % t)))
+            act(v("RH", 0, 256 * k), ind(v("HF", 0, 2048 * k), v("aU%d" % t)))
         if part == 1:
-            lists(v("ML", 0, 32), "ZE", "RH", 512)
+            lists(v("ML", 0, 16 * k), "RH", 256 * k)
         if part == 2:
-            vcopy(cb, v("ML", 16, 32))
-            ts(ss, aF, 2.0, A.mult)
-            tt(mx, v("ML", 0, 16), cb, A.max)
+            if t:
+                vcopy(v("cb", 0, 32), v("ML", 32, 64))
+                ts(ss, aF, 2.0, A.mult)
+                tt(v("cb", 32, 64), v("ML", 0, 32), v("cb", 0, 32), A.max)
+                tt(mx, v("cb", 32, 48), v("cb", 48, 64), A.max)
+            else:
+                vcopy(mx, v("ML", 0, 16))
+                ts(ss, aF, 2.0, A.mult)
             ts(fi, mx, 7, A.bitwise_and, 1, A.logical_shift_right)
             ts(hh, mx, 1, A.bitwise_and)
-            ts(fm1, fi, -1.0, A.add)
-
-    def pl(a, b, st=1, rows=16):
-        return v("TR", a, b, st, 0, rows)
+            ts(a1, fi, -2.0, A.add)
+            ts(a2, fi, -1.0, A.mult)
+            tt(fm1, a1, a2, A.max)
 
     def compare(c0, c1):
-        if c0 == 0:
-            mm(pl(0, 256), v("NR", p0=0, p1=1), v("ONE", p0=0, p1=1), True, False)
         for c in range(c0, c1):
-            e = 256 * c
-            ts(v("E", e, e + 256), v("AR"), v("aF", c, c + 1), A.is_equal)
-            mm(pl(0, 16 * c + 16), v("SGc"), v("E", e, e + 16 * c + 16), False, False)
+            e = 272 * c
+            ts(v("E", e, e + 256 - 16 * c), v("AR", 16 * c, 256), v("aF", c, c + 1), A.is_equal)
             if c < 15:
-                mm(pl(16 * c + 16, 256), v("SGp"), v("E", e + 16 * c + 16, e + 256), False, False)
+                mm(v("TR", 16 * c + 16, 256, 1, 0, 8), v("G8", 0, 8), v("E", e + 16, e + 256 - 16 * c), c == 0, False)
+            if c == 0:
+                mm(v("TR", 0, 16, 1, 0, 8), v("LTm", 0, 8), v("E", 0, 16), False, False)
 
-    def places():
-        for i in range(1, 16):
-            mm(pl(i, 256, 16, 8), v("LTm", 8 * i, 8 * i + 8), v("E", i, 4096, 272), False, i == 15)
-        vcopy(v("RR", p1=16), pl(0, 256))
-        lists(kP, "ZK", "RR", 256, 16)
-        lists(oth, "ZC", "RR", 256, 16)
+    def places(part):
+        if part == 0:
+            for i in range(1, 16):
+                mm(v("TR", i, 256, 16, 0, 8), v("LTm", 8 * i, 8 * i + 8), v("E", i, 4096, 272), False, i == 15)
+            vcopy(v("RR", p1=8), v("TR", 0, 256, 1, 0, 8))
+            turn_a("RR", 256, 8, "mI")
+        if part == 1:
+            turn_b(kP, 16, "TT", "mI")
 
     def pops():
         tt(nn1, kP, fm1, A.subtract)
@@ -379,10 +386,10 @@ def rank_program(g, core, T, topo):
         scan(v("scB"), v("blB"), v("ZR16"), A.add, A.add)
         ts(nn4, nn1, 4096.0, A.mult)
         tt(slot, ss, hk, A.add)
+        ts(k3, kP, 3.0, A.min, 2048.0, A.mult)
         mm(ro, v("SG"), v("scB"), True, False)
         mm(ro, v("TRI"), v("blB"), False, True)
         tt(segf, nn4, slot, A.max)
-        tt(mn, oth, fi, A.min)
         ts(v("gU"), segf, 4096.0, A.min)
 
     def move(t, part):
@@ -400,9 +407,11 @@ def rank_program(g, core, T, topo):
             tt(pos, ro, v("LA", 32, 48), A.min)
             ts(v("cU"), pos, 511.0, A.add)
             vcopy(ind(v("CR"), v("cU")), v("JL"))
-            lists(v("ML", 80, 88), "ZE", "CR", 128)
+            turn_a("CR", 128, 128, "G8")
         if part == 1:
-            vcopy(v("CL%d" % t), v("ML", 80, 88))
+            turn_b(cP, 8, "TT", "mI", 0.0625)
+        if part == 2:
+            vcopy(v("CL%d" % t), cP)
             send(rank + 1 + t, v("CL%d" % t), "QL%d" % t, "r_l%d" % t)
 
     def payload():
@@ -412,47 +421,37 @@ def rank_program(g, core, T, topo):
         vcopy(v("s16"), ind(v("SI"), v("pU")))
         ts(v("hB"), v("s16"), 1.0 / 48, A.mult, 128.0, A.add)
 
-    def keys(part):
-        if part == 0:
-            mm(v("KEY"), one_row, v("CRS", p0=0, p1=1), True, False)
-        if part == 1:
-            for h in range(2):
-                s = (128 * h, 128 * h + 128)
-                mm(v("KEY", 256 * h, 256 * h + 128), v("hB", *s), v("mI"), False, False)
-                mm(v("KEY", 256 * h + 128, 256 * h + 256), v("hB", *s), v("m48"), False, False)
-                mm(v("KEY", 256 * h + 128, 256 * h + 256), v("s16", *s), v("mIh"), False, False)
+    def keys(start=False):
+        for h in range(2):
+            s = (128 * h, 128 * h + 128)
+            mm(v("KEY", 256 * h, 256 * h + 128), v("hB", *s), v("mI"), start and h == 0, False)
+            mm(v("KEY", 256 * h + 128, 256 * h + 256), v("hB", *s), v("m48"), False, False)
+            mm(v("KEY", 256 * h + 128, 256 * h + 256), v("s16", *s), v("mIh"), False, False)
 
     def decide(t, part):
         if part == 0:
-            ts(ask, ro, -399.0, A.is_lt)
-            ts(q1, nn1, 2.0, A.is_le)
-            tt(w, kP, mn, A.is_equal)
-            tt(put, ask, q1, A.mult)
+            ts(ask2, ro, -399.0, A.is_lt, 2.0, A.mult)
             ts(e0, nn1, 1.0, A.is_equal)
-            ts(mn1, nn1, -1.0, A.mult)
-            tt(pn, put, nn1, A.mult)
+            ts(v1, nn1, 2.0, A.mult, 8.0 * t + 10.0, A.add)
             tt(hp, e0, hk, A.is_equal)
-            tt(fp, mn1, pn, A.max)
-            ts(n1s, pn, 2.0, A.is_equal, 2048.0, A.mult)
-            ts(v1, fp, 2.0, A.mult, 8.0 * (t + 1), A.add)
-            tt(wm, w, n1s, A.max)
+            tt(nw, nn1, ask2, A.is_gt)
+            ts(popf, nn1, 0.0, A.is_le)
             tt(v2, v1, hp, A.add)
-            tt(base, n1s, aF, A.add)
-            vcopy(v("vU"), v2)
+            tt(nput, nw, popf, A.max)
+            tt(base, k3, aF, A.add)
+            ts(v("vU"), v2, 255.0, A.min)
+            tt(two, two, v("LA", 0, 32), A.mult)
         if part == 1:
             act(v("HV"), ind(v("JL"), v("vU")))
         if part == 2:
-            ts(two, two, 0.0, A.is_equal)
             if t < 2:
                 ts(q8, ro, 0.125, A.mult, 63.4375, A.add)
-            tt(two, two, v("LA", 0, 32), A.mult)
-            if t < 2:
-                ts(t2, q8, -7.9375, A.mult, 511.0, A.add)
             tt(two, two, own, A.max)
             if t < 2:
-                tt(t3, ro, t2, A.add)
+                ts(t2, q8, -7.9375, A.mult, 511.0, A.add)
             vcopy(v("nU"), two)
             if t < 2:
+                tt(t3, ro, t2, A.add)
                 ts(v("jU"), t3, 16.0, A.mult, 127.0, A.min)
         if part == 3:
             vcopy(ind(v("HF"), v("nU", 16, 32)), v("HV"))
@@ -486,9 +485,9 @@ def rank_program(g, core, T, topo):
             vcopy(v("CC"), b)
         if part == 4:
             mm(v("KA", 0, 128), one_row, v("JL", 0, 128, 1, 0, 1), True, False)
-            mm(v("KA", 0, 128), v("BR", p0=0, p1=1), one_row, False, False)
+            mm(v("KA", 0, 128), v("BR", p1=1), one_row, False, False)
         if part == 5:
-            scan(v("KT"), v("BM", 0, 128), v("KA", 0, 128), A.add, A.min)
+            scan(v("KT"), v("BQ"), v("KA", 0, 128), A.add, A.min)
             vcopy(v("KQ", 0, 8), v("KT", 15, 128, 16))
             ts(v("KQ", 16, 24), v("KQ", 0, 8), 2047, A.bitwise_and)
             vcopy(v("qU"), v("KQ", 16, 24))
@@ -499,152 +498,169 @@ def rank_program(g, core, T, topo):
     def least(t, part):
         if part == 0:
             scan(v("KS"), v("BM"), v("KEY"), A.add, A.min)
-            vcopy(v("KI", 0, 32), v("KS", 15, 512, 16))
+            tt(v("KI", 0, 32), v("KS", 15, 512, 16), v("CK"), A.add)
             ts(v("KI", 32, 64), v("KI", 0, 32), 63, A.bitwise_and)
             vcopy(v("PB"), v("KI", 32, 64))
             for h in range(2):
-                o = v("TR", 256 + 128 * h, 384 + 128 * h, 1, 0, 8)
+                o = v("TR", 128 * h, 128 * h + 128, 1, 0, 8)
                 mm(o, v("PB", 16 * h, 16 * h + 8), v("m48"), True, False)
                 mm(o, v("PB", 16 * h + 8, 16 * h + 16), v("mNI"), False, True)
         if part == 1:
-            ts(v("YA" if t == 2 else "T16", p1=8), v("TR", 256, 512, 1, 0, 8), -1.0, A.mult, -32.0, A.add)
+            ts(v("YA" if t == 2 else "T16", p1=8), v("TR", 0, 256, 1, 0, 8), -1.0, A.mult, -32.0, A.add)
             if t < 2:
+                turn_a("T16", 256, 8, "mIh")
                 mm(v("D2", 0, 256), v("RP", p1=8), v("T16", p1=8), True, True)
-                lists(v("ML", 96, 112), "ZA", "T16", 256, 8)
         if part == 2:
+            turn_b(aP, 16, "TH", "mIh")
             vcopy(v("AR"), v("D2", 0, 256))
         if part == 3:
             aN = "aU%d" % (t + 1)
-            vcopy(v(aN, 0, 16), v("ML", 96, 112))
-            vcopy(aF, v("ML", 96, 112))
-            ts(v(aN, 16, 32), v("ML", 96, 112), 2048.0, A.add)
+            vcopy(v(aN, 0, 16), aP)
+            vcopy(aF, aP)
+        if part == 4:
+            aN = "aU%d" % (t + 1)
+            for r in range(1, 4):
+                ts(v(aN, 16 * r, 16 * r + 16), aP, 2048.0 * r, A.add)
 
     constants(0)
     start()
     constants(1)
-    compare(0, 16)
-    constants(2)
-    cells(0, 0)
-    places()
-    cells(0, 1)
+    send(rank + 1, v("aU0"), "QA0", "r_a0")
+    send(rank + 1, v("Z0"), "QZ0", "r_z0")
     constants(3)
+    compare(0, 8)
+    table(0)
+    table(1)
+    compare(8, 16)
+    constants(2)
+    places(0)
+    table(2)
+    table(3)
+    places(1)
+    constants(4)
+    cells(0, 0)
+    cells(0, 1)
+    constants(7)
+    succ(0)
+    centres("S", 2048, 3072)
     cells(0, 2)
     pops()
     compact(0, 0)
-    decide(0, 0)
+    centres("S", 3072, 4096)
     compact(0, 1)
-    constants(4)
-    decide(0, 1)
-    decide(0, 2)
-    succ(0)
-    centres("S", 0, 1024)
-    decide(0, 3)
-    question(0, 0)
-    centres("S", 1024, 2048)
     constants(5)
+    compact(0, 2)
     payload()
-    centres("V", 3072, 4096)
-    question(0, 1)
-    question(0, 2)
-    centres("S", 2048, 3072)
-    question(0, 3)
-    keys(0)
-    keys(1)
-    sums("cS", 0, 2, 2)
+    keys(True)
+    centres("S", 0, 1024)
     sums("cS", 4, 8, 2)
-    question(0, 4)
     move(0, 0)
-    cands("S", 0, 1024)
+    constants(6)
     move(0, 1)
     move(0, 2)
     send(rank + 2, v("Z1"), "QZ1", "r_z1")
-    dS("4V", "5V", "6V")
-    cands("S", 1024, 1792)
-    dS("7V", "0V")
+    question(0, 0)
+    centres("S", 1024, 2048)
+    dS("4V", "5V", "6V", "7V")
+    question(0, 1)
+    dS("0S")
+    decide(0, 0)
     sums("AB", 4, 8, 1)
-    dS("2S", "1V", "3S")
-    sums("AB", 0, 2, 1, True)
-    dA("0S")
-    sums("AB", 2, 4, 0, True)
-    dA("1S")
+    question(0, 2)
+    dS("1S")
+    decide(0, 2)
+    dS("2S")
+    question(0, 3)
+    dS("3S")
+    sums("AB", 0, 3, 0, stop=True)
+    sums("AB", 3, 4, 0, stop=True)
+    decide(0, 1)
+    cands("S", 0, 1024)
+    constants(8)
     least(0, 0)
-    dA("2S")
+    question(0, 4)
+    cands("S", 1024, 1792)
     least(0, 1)
-    dA("3S")
     least(0, 2)
-    sA("0S", "1S", "2S", "3S")
     least(0, 3)
     send(rank + 2, v("aU1", 0, 16), "QA1", "r_a1")
-    cells(1, 0)
     succ(1)
-    question(0, 5)
+    dA("0S", "1S")
+    least(0, 4)
+    decide(0, 3)
+    dA("2S", "3S")
+    cells(1, 0)
+    sA("0S", "1S", "2S", "3S", stop=True)
     centres("S", 2048, 3072)
+    compare(0, 8)
+    question(0, 5)
     question(0, 6)
-    compare(0, 6)
     cells(1, 1)
-    compare(6, 11)
-    cells(1, 2)
-    compare(11, 16)
+    compare(8, 16)
     centres("S", 3072, 4096)
-    places()
-    refill(0, 0)
+    places(0)
+    cells(1, 2)
+    places(1)
     centres("S", 0, 1024)
     pops()
     compact(1, 0)
-    refill(0, 1)
+    refill(0, 0)
     compact(1, 1)
+    payload()
+    compact(1, 2)
     question(1, 0)
     centres("S", 1024, 2048)
-    keys(0)
+    keys(True)
     sums("cS", 4, 8, 2)
+    refill(0, 1)
     move(1, 0)
-    payload()
+    decide(1, 0)
     move(1, 1)
     move(1, 2)
     dS("4V", "0S", "5V", "1S")
-    keys(1)
     question(1, 1)
-    dS("6V", "2S", "7V", "3S")
+    decide(1, 2)
+    dS("6V")
     question(1, 2)
-    sums("AB", 4, 8, 1)
-    sums("AB", 0, 3, 0, True)
-    sums("AB", 3, 4, 0, True)
+    dS("2S", "7V")
     question(1, 3)
+    dS("3S")
+    sums("AB", 4, 8, 1)
+    decide(1, 1)
     cands("S", 0, 1024)
+    sums("AB", 0, 3, 0, stop=True)
+    sums("AB", 3, 4, 0, stop=True)
+    decide(1, 3)
     least(1, 0)
     question(1, 4)
-    decide(1, 0)
     cands("S", 1024, 1792)
+    dA("0S")
     least(1, 1)
-    decide(1, 2)
     least(1, 2)
-    decide(1, 1)
-    dA("0S", "1S")
+    dA("1S")
     least(1, 3)
     succ(2)
-    dA("2V", "3S")
-    decide(1, 3)
-    sA("0S", "1S", "2V", "3S")
+    least(1, 4)
+    dA("2S", "3S")
+    sA("0S", "1S", "2S", "3S", stop=True)
     cells(2, 0)
+    compare(0, 4)
     question(1, 5)
     question(1, 6)
     centres("S", 2048, 3072)
-    compare(0, 8)
+    compare(4, 16)
     cells(2, 1)
-    compare(8, 13)
-    cells(2, 2)
-    compare(13, 16)
     centres("S", 3072, 4096)
-    places()
-    centres("V", 0, 512)
+    places(0)
+    cells(2, 2)
+    places(1)
     pops()
     refill(1, 0)
     centres("S", 1024, 2048)
-    keys(0)
-    sums("cS", 4, 8, 2)
     payload()
-    centres("V", 512, 1024)
-    keys(1)
+    keys(True)
+    sums("cS", 4, 8, 2)
+    centres("V", 0, 1024)
     refill(1, 1)
     move(2, 0)
     decide(2, 0)
@@ -653,25 +669,28 @@ def rank_program(g, core, T, topo):
     decide(2, 2)
     move(2, 2)
     store("Y", T.yz[:, :], v("Z3"), "o_z")
-    dS("0S", "4V", "1S", "5V")
+    dS("4V", "0S", "5V", "1S")
     decide(2, 3)
-    for b, c0, s in (("SA", 0, "l_p"), ("SB", 2048, "l_q")):
-        deps("Y", [v(b)], [v("HF")])
-        load("Y", v(b), T.HF[0:128:16, c0:c0 + 2048], s)
-    dS("2S", "6V", "3S", "7V")
-    sums("AB", 0, 4, 0)
-    sums("AB", 4, 7, 1, True)
-    sums("AB", 7, 8, 1, True)
+    for r in range(4):
+        o = v("SA", 128 * r, 128 * r + 128)
+        deps("Y", [o], [v("HF")])
+        load("Y", o, T.HF[0:128:16, 2048 * r:2048 * r + 2048], "l_p%d" % r)
+    dS("6V", "2S", "7V", "3S")
+    sums("AB", 4, 8, 1)
+    sums("AB", 0, 3, 0, stop=True)
+    sums("AB", 3, 4, 0, stop=True)
+    tt(v("W2"), v("SA", 0, 256), v("SA", 256, 512), A.max)
     least(2, 0)
-    tt(v("TI"), v("SA"), v("SB"), A.max)
+    tt(v("TI"), v("W2", 0, 128), v("W2", 128, 256), A.max)
     least(2, 1)
     store("S", T.ya[:, :], v("YA", p1=8), "o_a")
     ts(v("TJ"), v("TI"), 7, A.bitwise_and, 1, A.logical_shift_right)
     ts(v("TK"), v("TI"), 1, A.bitwise_and)
-    vcopy(v("YF"), v("TJ"))
+    ts(v("W1"), v("TJ"), -1.0, A.add)
     vcopy(v("YH"), v("TK"))
-    store("Y", T.yf[:, :], v("YF"), "o_f")
-    store("S", T.yh[:, :], v("YH"), "o_h")
+    act(v("YF"), v("W1"), F.Abs)
+    store("Y", T.yh[:, :], v("YH"), "o_h")
+    store("S", T.yf[:, :], v("YF"), "o_f")
     g.wait_ge(T.sem.sent, sent[0])
     for s, x in [("e" + q, cnt[q]) for q in cnt] + final:
         if known["G"].get(s, 0) < x:

@@ -8,24 +8,23 @@ def _b(n, c, d="bfloat16", w="sbuf", p=128):
 
 
 for _n, _c in (("X", 2048), ("G", 4368), ("HF", 8448), ("cS", 4096), ("AB", 4096), ("cA", 1792), ("AC", 1792), ("E", 4096),
-               ("mI", 128), ("mNI", 128), ("m48", 128), ("SG", 128), ("G8", 128), ("LTm", 128), ("ZE", 144), ("NG", 128),
-               ("ZS", 432), ("TRI", 128), ("WX", 128), ("REP", 512), ("KBS", 48), ("ONE", 128), ("JG", 128), ("J8", 128), ("JR", 512),
-               ("BR", 128), ("JL", 256), ("BM", 512), ("BQ", 128), ("V0", 128), ("RR", 256), ("RH", 1024), ("TT", 128),
-               ("blB", 16), ("scB", 16), ("hB", 256), ("zt", 256), ("WTS", 256), ("WTA", 128), ("goal", 256), ("zc", 112),
-               ("gk", 112), ("CR", 512), ("PB", 32), ("HV", 256), ("LX", 256), ("SA", 512),
+               ("mI", 128), ("mNI", 128), ("m48", 128), ("mE", 256), ("SG", 128), ("G8", 128), ("LTm", 128), ("ZE", 144), ("ZK", 144),
+               ("NG", 128), ("ZS", 432), ("eB", 112), ("TRI", 128), ("WX", 128), ("KBS", 48), ("ONE", 128), ("JG", 128), ("J8", 128),
+               ("BR", 128), ("JL", 256), ("BM", 512), ("BQ", 128), ("B4", 64), ("V0", 128), ("RR", 256), ("RH", 1024),
+               ("blB", 16), ("scB", 16), ("hB", 256), ("zt", 256), ("goal", 256), ("PB", 32), ("HV", 256), ("LX", 256), ("SA", 512),
                ("Z0", 256), ("Z1", 256), ("Z2", 256), ("Z3", 256), ("AN0", 128), ("AN1", 128), ("LN0", 128), ("LN1", 128),
                ("QZ0", 256), ("QZ1", 256)):
     _b(_n, _c)
-for _n, _c in (("mIh", 128), ("RP", 128), ("s16", 256), ("T16", 256), ("TH", 128)):
+for _n, _c in (("mIh", 128), ("RP", 128), ("s16", 256), ("T16", 256), ("ZA", 144)):
     _b(_n, _c, "float16")
 for _n, _c in (("COL", 128), ("OH", 16), ("LA", 48), ("W1", 128), ("W2", 256), ("ZR16", 16), ("LL", 512), ("KS", 512), ("KT", 128),
-               ("aF", 16), ("Y1", 112), ("Y2", 112), ("YA", 256), ("YH", 128), ("YF", 128), ("CK", 32), ("cb", 64)):
+               ("aF", 16), ("Y1", 256), ("Y2", 256), ("YA", 256), ("YH", 128), ("YF", 128), ("CK", 32), ("cb", 64)):
     _b(_n, _c, "float32")
-for _n, _c in (("SI", 4096), ("FI", 128), ("HI", 128), ("aI", 16), ("CI", 8), ("LI", 256),
-               ("TI", 128), ("TJ", 128), ("TK", 128), ("KI", 64), ("KQ", 32)):
+for _n, _c in (("SI", 4096), ("FI", 128), ("HI", 128), ("aI", 16), ("CI", 8), ("LI", 256), ("PK", 256), ("CW", 512),
+               ("TI", 256), ("TJ", 256), ("TK", 128), ("KI", 64), ("KQ", 32)):
     _b(_n, _c, "int32")
-for _n, _c in (("aU0", 16), ("aU1", 64), ("aU2", 64), ("AR", 256), ("sU", 256), ("gU", 16), ("nU", 32), ("pU", 16), ("vU", 16),
-               ("cU", 16), ("jU", 16), ("qU", 8), ("CC", 112), ("CL0", 8), ("CL1", 8), ("QL0", 8), ("QL1", 8), ("QA0", 16), ("QA1", 16)):
+for _n, _c in (("aS0", 16), ("aS1", 16), ("aS2", 16), ("aU", 64), ("AR", 256), ("sU", 256), ("gU", 16), ("nU", 32), ("pU", 16), ("vU", 16),
+               ("jU", 16), ("qU", 8), ("CC", 112), ("CL0", 16), ("CL1", 16), ("QL0", 16), ("QL1", 16), ("QA0", 16), ("QA1", 16)):
     _b(_n, _c, "uint16")
 for _n in ("D0", "D1", "D2", "D3", "KEY", "ML", "TR", "KA"):
     _b(_n, 512, "float32", "psum")
@@ -74,14 +73,17 @@ def rank_program(g, core, T, topo):
                 out += [x[1], x[2]] if x[0] == "ind" else [x]
         return out
 
+    def meet(e, x):
+        return e[0] < x[2] and x[1] < e[1] and not (e[3] == x[3] > 1 and (e[0] - x[1]) % x[3])
+
     def deps(q, ws, rs):
         need = []
         for x in ws + rs:
             if SCRATCH[x[0]][0] == "psum":
                 need += [r for k, r in pacc.get(x[0], {}).items() if k != q]
-            need += [r for lo, hi, r in wr.get(x[0], []) if lo < x[2] and x[1] < hi]
+            need += [e[2] for e in wr.get(x[0], []) if meet(e, x)]
         for x in ws:
-            need += [r for lo, hi, r in rd.get(x[0], []) if lo < x[2] and x[1] < hi]
+            need += [e[2] for e in rd.get(x[0], []) if meet(e, x)]
         for r in sorted(need, key=lambda r: -r[2]):
             wait(q, r)
 
@@ -91,17 +93,35 @@ def rank_program(g, core, T, topo):
                 pacc.setdefault(x[0], {})[rec[0]] = rec
         for x in ws:
             if SCRATCH[x[0]][0] == "psum":
+                if rec[0] == "V":
+                    pacc[x[0]]["w"] = rec
                 continue
             if x[3] == 1 and cover:
                 wr[x[0]] = [e for e in wr.get(x[0], []) if not (x[1] <= e[0] and e[1] <= x[2])]
                 rd[x[0]] = [e for e in rd.get(x[0], []) if not (x[1] <= e[0] and e[1] <= x[2])]
-            wr.setdefault(x[0], []).append((x[1], x[2], rec))
+            wr.setdefault(x[0], []).append((x[1], x[2], rec, x[3]))
         for x in rs:
             if SCRATCH[x[0]][0] != "psum":
-                rd[x[0]] = [e for e in rd.get(x[0], []) if not (e[2][0] == rec[0] and not e[2][4] and x[1] <= e[0] and e[1] <= x[2])]
-                rd[x[0]].append((x[1], x[2], rec))
+                rd[x[0]] = [e for e in rd.get(x[0], [])
+                            if not (e[2][0] == rec[0] and not e[2][4] and x[3] == 1 and x[1] <= e[0] and e[1] <= x[2])]
+                rd[x[0]].append((x[1], x[2], rec, x[3]))
+
+    held = []
+
+    def mix(*pieces):
+        rows = []
+        for p in pieces:
+            held.append([])
+            p[0](*p[1:])
+            rows.append(held.pop())
+        for k in range(max(len(r) for r in rows)):
+            for r in rows:
+                if k < len(r):
+                    r[k][0](*r[k][1:])
 
     def op(q, call, out, *ins):
+        if held:
+            return held[-1].append((op, q, call, out) + ins)
         ws, rs = flat([out]), flat(ins)
         if out[0] == "ind":
             ws, rs = [out[1]], rs + [out[2]]
@@ -158,6 +178,8 @@ def rank_program(g, core, T, topo):
         final.append((sem, 16))
 
     def send(dst, src, buf, sem):
+        if held:
+            return held[-1].append((send, dst, src, buf, sem))
         to = T.cores[dst % n]
         rid, pid = topo.addr(to)[0], topo.addr(to)[1]
         e = topo.engines(core, to)[:8]
@@ -167,14 +189,14 @@ def rank_program(g, core, T, topo):
 
     def arrive(buf, sem, src):
         e = len(topo.engines(T.cores[src % n], core)[:8])
-        wr[buf] = [(0, SCRATCH[buf][1][1], ("R", sem, e, {}, True))]
+        wr[buf] = [(0, SCRATCH[buf][1][1], ("R", sem, e, {}, True), 1)]
 
     load("Y", v("aI"), T.a0[:, :], "l_a")
     load("S", v("FI"), T.fl0[:, :], "l_f")
     load("Y", v("HI"), T.hd0[:, :], "l_h")
     load("S", v("Z0"), T.z0[:, :], "l_z")
     load("Y", v("SI", 0, 2048), T.su[:, :], "l_s")
-    load("S", v("X"), T.xs[:, :], "l_x")
+    load("Y", v("X"), T.xs[:, :], "l_x")
     load("Y", v("G", 0, 4096), T.gs[:, :], "l_g")
     for t in range(2):
         for b in ("QZ", "QA", "QL"):
@@ -186,54 +208,53 @@ def rank_program(g, core, T, topo):
 
     def col(k):
         return v("COL", 4 * k, 4 * k + 1)
-    (pF, pm, pg, g15, wi, p31, ycol, rcol, c1) = [col(k) for k in range(9)]
+    (pF, pm, pg, g15, wi, k15, ycol, rcol, c1) = [col(k) for k in range(9)]
     one_row = v("ONE", p1=1)
 
     def constants(part):
         if part == 0:
             iota(v("CI", 0, 1), [[0, 1]], 0, 1)
+            iota(v("JG"), [[1, 8], [0, 16]])
+            iota(v("J8"), [[0, 16], [1, 8]])
             iota(J(0, 512), [[1, 512]])
             iota(v("JL"), [[1, 256]])
-            iota(v("JG"), [[1, 8], [0, 16]])
-            iota(J(1536, 2048), [[1, 512]], 1536)
-            iota(v("J8"), [[0, 16], [1, 8]])
-            fill(v("HF", 2048, 4096), 0.0)
+            fill(v("HF", 2048, 3584), 0.0)
             vcopy(pF, v("CI", 0, 1))
-            bits = ((pm, A.bitwise_and, 15), (pg, A.logical_shift_right, 4), (p31, A.bitwise_and, 31))
+            bits = ((pm, A.bitwise_and, 15), (pg, A.logical_shift_right, 4))
             for j, (out, o, s) in enumerate(bits):
                 ts(v("CI", 1 + j, 2 + j), v("CI", 0, 1), s, o)
             fill(v("ZR16"), 0.0)
             for j, (out, o, s) in enumerate(bits):
                 vcopy(out, v("CI", 1 + j, 2 + j))
-            ts(J(512, 1024), J(0, 512), 512.0, A.add)
-            ts(J(1024, 1536), J(0, 512), 1024.0, A.add)
-            ts(v("OH"), v("JL", 0, 16), pm, A.is_equal)
-            ts(v("SG"), v("JG"), pg, A.is_equal)
             ts(g15, pg, 16.0, A.mult, 15.0, A.add)
-            ts(v("mI"), v("JL", 0, 128), pF, A.is_equal)
-            ts(v("NG"), v("JG"), pg, A.is_equal, -1.0, A.mult)
-        if part == 1:
             ts(v("G8"), v("J8"), pg, A.is_equal)
+            ts(v("NG"), v("JG"), pg, A.is_equal, -1.0, A.mult)
+            ts(v("SG"), v("JG"), pg, A.is_equal)
             select(v("LTm"), v("G8"), [[1, 16], [16, 8]], A.is_gt, 0.0, -1)
             select(v("NG"), v("NG"), [[-1, 128]], A.is_ge, 0.0, 1)
             select(v("TRI"), v("NG"), [[-1, 128]], A.not_equal, -512.0, 1)
+            for k in range(1, 4):
+                ts(J(512 * k, 512 * k + 512), J(0, 512), 512.0 * k, A.add)
+        if part == 1:
+            ts(v("OH"), v("JL", 0, 16), pm, A.is_equal)
+            ts(v("mI"), v("JL", 0, 128), pF, A.is_equal)
         if part == 2:
+            ts(k15, pF, 16.0, A.mult, 15.0, A.add)
             ts(v("ZE"), v("JL", 0, 144), g15, A.is_equal, 0.0625, A.mult)
             ts(v("LA", 32, 48), v("JL", 0, 16), 16.0, A.mult, pm, A.add)
-            fill(v("CR", 0, 128), 0.0)
+            ts(v("ZK"), v("JL", 0, 144), k15, A.is_equal)
             fill(v("G", 4096, 4112), 0.0)
             ts(v("LA", 0, 16), v("LA", 32, 48), 4112.0, A.add)
             ts(v("LA", 16, 32), v("LA", 32, 48), 8192.0, A.add)
+            ts(wi, pm, 2.0, A.mult, 1.0, A.add)
             ts(v("LA", 32, 48), v("LA", 32, 48), -255.0, A.add)
         if part == 3:
-            iota(v("JR"), [[1, 32], [0, 16]])
             iota(v("BR", p1=1), [[0, 8], [128, 16]])
             iota(v("CK"), [[0, 2], [32, 2], [0, 8]])
         if part == 4:
-            ts(wi, pm, 2.0, A.mult, 1.0, A.add)
-            ts(v("mNI"), v("mI"), -1.0, A.mult)
             ts(v("WX"), v("SG"), wi, A.mult)
             tt(c1, wi, wi, A.mult)
+            ts(v("mNI"), v("mI"), -1.0, A.mult)
             ts(ycol, wi, 16.0, A.mult)
             ts(v("m48"), v("mI"), -48.0, A.mult)
             ts(rcol, c1, -8.0, A.mult, -0.40625, A.add)
@@ -241,27 +262,35 @@ def rank_program(g, core, T, topo):
             for k, f in enumerate((1.0, 2.0, -1.0)):
                 ts(v("KBS", 16 * k, 16 * k + 16), v("G8", 0, 16), 1024.0 * f, A.mult)
         if part == 5:
-            ts(v("REP"), v("JR"), p31, A.is_equal)
+            for k, f in enumerate((4096.0, -4096.0)):
+                ts(v("mE", 128 * k, 128 * k + 128), v("mI"), f, A.mult)
+            fill(v("CW", 0, 112), 0)
+            fill(v("B4"), 0.0)
+            fill(v("BM"), -64.0)
+            fill(v("B4", 0, 64, 4), -1024.0)
+            fill(v("BM", 0, 512, 16), 33554432.0)
+            ts(v("RP"), v("JG"), pF, A.is_equal)
+            vcopy(v("ZA"), v("ZK"))
         if part == 6:
             fill(v("ONE"), 1.0)
-            fill(v("BM"), -64.0)
-            ts(v("RP"), v("JG"), pF, A.is_equal)
-            fill(v("BM", 0, 512, 16), 33554432.0)
             for k, f in enumerate((1.0, 2.0, -1.0)):
                 ts(v("ZS", 144 * k, 144 * k + 144), v("ZE"), 32768.0 * f, A.mult)
             ts(v("BR", p1=1), v("BR", p1=1), 1664.0, A.min)
             ts(v("BQ"), v("BM", 0, 128), 0.0, A.max)
         if part == 7:
-            fill(v("HF", 4096, 6144), 0.0)
+            iota(v("HF", 3584, 5120), [[0, 1536]])
         if part == 8:
-            fill(v("HF", 6144, 8448), 0.0)
+            iota(v("HF", 5120, 8448), [[0, 3328]])
 
     def start():
-        vcopy(v("aU0"), v("aI"))
-        ts(v("W1"), v("FI"), 2.0, A.mult, 2.0, A.add)
+        vcopy(v("aS0"), v("aI"))
+        ts(v("W1"), v("FI"), 2.0, A.mult)
+        constants(1)
         vcopy(v("aF"), v("aI"))
         tt(v("V0"), v("W1"), v("HI"), A.add)
-        vcopy(v("AR"), ind(J(0, 2048), v("aU0")))
+        vcopy(v("AR"), ind(J(0, 2048), v("aS0")))
+        ts(q8, v("aI"), 127, A.bitwise_and)
+        vcopy(v("vU"), q8)
         for k in range(16):
             act(v("AB", 128 * k, 128 * k + 128), v("V0"), scale=v("OH", k, k + 1))
 
@@ -269,29 +298,17 @@ def rank_program(g, core, T, topo):
         mm(v("D%d" % b), v("SG"), v("AB", 512 * b, 512 * b + 512), True, True)
         act(v("HF", 512 * b, 512 * b + 512), v("D%d" % b))
 
-    def lists(o, src, c1):
+    def lists(o, z, src, c1, rows=128):
         for i in range(16):
-            mm(o, v("ZE", 15 - i, 143 - i), v(src, i, c1, 16), i == 0, i == 15)
-
-    def turn_a(src, c1, rows, sel):
-        for i in range(16):
-            mm(v("TR", 256 + i, 384, 16, 0, c1 // 16), v(src, i, c1, 16, 0, rows), v(sel, 0, 8, 1, 0, rows), True, True)
-
-    def turn_b(o, m, buf, ident, f=None):
-        if f:
-            ts(v(buf, p1=m), v("TR", 256, 384, 1, 0, m), f, A.mult)
-        else:
-            vcopy(v(buf, p1=m), v("TR", 256, 384, 1, 0, m))
-        mm(o, v(buf, p1=m), v(ident, 0, m, 1, 0, m), True, True)
+            mm(o, v(z, 15 - i, 143 - i, 1, 0, rows), v(src, i, c1, 16, 0, rows), i == 0, i == 15)
 
     L = [v("LL", 16 * x, 16 * x + 16) for x in range(32)]
-    (fm1, ss, nn1, nn4, segf, t1, ask2, popf, e0, hp, v1, v2, k3, pos, t2, t3, a1, a2) = L[:18]
+    (ss, nn, nn4, segf, t1, ask2, popf, e0, hp, u1, u2, v1, v2, k3, pos, t2, t3, hq, sq) = L[:19]
     nput, nw, slot, base = L[24:28]
     two, own = v("LL", 384, 416), v("LL", 416, 448)
     mx, fi, hh, hs, hk, q8 = [v("LI", 16 * x, 16 * x + 16) for x in range(6)]
-    kP, ro, cP, aP = v("ML", 64, 80), v("ML", 80, 96), v("ML", 96, 104), v("ML", 112, 128)
+    kP, ro, aP = v("ML", 64, 80), v("ML", 80, 96), v("ML", 112, 128)
     aF, bank = v("aF"), v("G", 0, 4096)
-    turn = {"S": 0, "V": 0}
 
     def centres(q, c0, c1):
         copy(q, v("cS", c0, c1), ind(v("X"), v("sU", c0 // 16, c1 // 16)))
@@ -299,66 +316,62 @@ def rank_program(g, core, T, topo):
     def cands(q, c0, c1):
         copy(q, v("cA", c0, c1), ind(bank, v("CC", c0 // 16, c1 // 16)))
 
-    def dist(ab, src, term, k, mode):
-        wd = min(512, SCRATCH[src][1][1] - 512 * k)
-        h, r = k // 4, 32 * (k % 4)
-        d = v("D%d" % (turn[mode] % 2 + (2 if mode == "V" else 0)), 0, wd)
-        turn[mode] += 1
-        s, o = v(src, 512 * k, 512 * k + wd), v(ab, 512 * k, 512 * k + wd)
-        if mode == "S":
-            mm(d, v("mNI"), s, True, False)
-        mm(d, v(term, 128 * h, 128 * h + 128, 1, r, r + wd // 16), v("REP", 0, wd, 1, r, r + wd // 16), mode == "V", True)
-        if mode == "S":
-            act(o, d, F.Abs)
-        else:
-            tt(o, s, d, A.max)
-
-    def dS(*ks):
-        for k, mode in ks:
-            dist("AB", "cS", "WTS", int(k), mode)
-
-    def dA(*ks):
-        for k, mode in ks:
-            dist("AC", "cA", "WTA", int(k), mode)
-
-    def sums(src, k0, k1, kb, start=False, stop=False):
-        h, r0, r1 = k0 // 4, 32 * (k0 % 4), 32 * ((k1 - 1) % 4 + 1)
+    def dA(l0, l1):
         for m in range(16):
-            mm(v("KEY", 256 * h + m, 256 * h + 256, 16, r0, r1), v(src, 512 * k0 + m, 512 * k1, 16), v("KBS", 16 * kb, 16 * kb + 16),
-               start and m == 0, stop and m == 15)
+            tt(v("AC", 16 * l0 + m, 16 * l1, 16), v("cA", 16 * l0 + m, 16 * l1, 16), v("D3", l0, l1), A.max)
 
-    def blocks(src, k, kb, stop=False):
-        bs = range(4 * k, min(4 * k + 4, 14))
-        for b in bs:
-            mm(v("KA", 0, 128), v("ZS", 144 * kb + 15 - b, 144 * kb + 143 - b), v(src, 128 * b, 128 * b + 128), False, stop and b == bs[-1])
+    def dB(k, b, parts):
+        wd = min(512, 1792 - 512 * k)
+        if "e" in parts:
+            for m in range(16):
+                mm(v("D%d" % b, m, wd, 16), v("mI"), v("eB", 32 * k, 32 * k + wd // 16), m == 0, False)
+        if "c" in parts:
+            mm(v("D%d" % b, 0, wd), v("mNI"), v("cA", 512 * k, 512 * k + wd), False, True)
+        if "d" in parts:
+            act(v("AC", 512 * k, 512 * k + wd), v("D%d" % b, 0, wd), F.Abs)
 
-    def sA(*ks, stop=False):
-        for k, mode in ks:
-            blocks("cA" if mode == "R" else "AC", int(k), "SVR".index(mode), stop and (k, mode) == tuple(ks[-1]))
+    def dS(t, b, parts):
+        for p in parts.replace("d", ""):
+            for j in range(4):
+                w, s = (v("mNI"), v("cS", 4 * b + j, 2048, 16)) if p == "c" else (v("mI"), v("Z%d" % (t + 1), 0, 128))
+                mm(v("D%d" % b, 128 * j, 128 * j + 128), w, s, p == "c" and j == 0, p == "e" and j == 3)
+        if "d" in parts:
+            act(v("AB", 512 * b, 512 * b + 512), v("D%d" % b), F.Abs)
+
+    def dV(m0, m1):
+        for m in range(m0, m1):
+            tt(v("AB", 2048 + 128 * m, 2176 + 128 * m), v("cS", 2048 + m, 4096, 16), v("TR", 0, 128), A.max)
+
+    def sums(h, m0, m1, raw=False, stop=False):
+        for m in range(m0, m1):
+            s = v("cS", 2048 + m, 4096, 16) if raw else v("AB", 2048 * h + 128 * m, 2048 * h + 128 * m + 128)
+            kb = 2 if raw else h
+            mm(v("KEY", 256 * h + m, 256 * h + 256, 16), s, v("KBS", 16 * kb, 16 * kb + 16), False, stop and m == m1 - 1)
+
+    def blocks(b0, b1, kind, stop=False):
+        for b in range(b0, b1):
+            z = 144 * kind + 15 - b
+            mm(v("KA", 0, 128), v("ZS", z, z + 128), v("cA" if kind == 2 else "AC", 128 * b, 128 * b + 128), False, stop and b == b1 - 1)
 
     def succ(t):
-        vcopy(v("sU"), ind(v("SI", 0, 2048), v("aU%d" % t, 0, 16)))
+        vcopy(v("sU"), ind(v("SI", 0, 2048), v("aS%d" % t)))
 
     def cells(t, part):
-        k = 4 if t else 1
-        if part == 0:
-            act(v("RH", 0, 256 * k), ind(v("HF", 0, 2048 * k), v("aU%d" % t)))
+        if part == 0 and t:
+            act(v("RH"), ind(v("HF", 0, 8192), v("aU")))
+        if part == 0 and not t:
+            ts(v("TI"), v("AR"), 1.0 / 128, A.mult, -0.49609375, A.add)
+            ts(v("HV"), v("TI"), pm, A.is_equal, 16.0, A.mult)
+            tt(v("RH", 0, 256), ind(v("V0"), v("vU")), v("HV"), A.mult)
         if part == 1:
-            lists(v("ML", 0, 16 * k), "RH", 256 * k)
+            lists(v("ML", 0, 64 if t else 16), "ZE", "RH", 1024 if t else 256)
         if part == 2:
             if t:
-                vcopy(v("cb", 0, 32), v("ML", 32, 64))
-                ts(ss, aF, 2.0, A.mult)
-                tt(v("cb", 32, 64), v("ML", 0, 32), v("cb", 0, 32), A.max)
-                tt(mx, v("cb", 32, 48), v("cb", 48, 64), A.max)
-            else:
-                vcopy(mx, v("ML", 0, 16))
-                ts(ss, aF, 2.0, A.mult)
+                scan(v("cb"), v("B4"), v("ML", 0, 64), A.add, A.max)
+            ts(ss, aF, 2.0, A.mult)
+            vcopy(mx, v("cb", 3, 64, 4) if t else v("ML", 0, 16))
             ts(fi, mx, 7, A.bitwise_and, 1, A.logical_shift_right)
             ts(hh, mx, 1, A.bitwise_and)
-            ts(a1, fi, -2.0, A.add)
-            ts(a2, fi, -1.0, A.mult)
-            tt(fm1, a1, a2, A.max)
 
     def compare(c0, c1):
         for c in range(c0, c1):
@@ -373,49 +386,39 @@ def rank_program(g, core, T, topo):
         if part == 0:
             for i in range(1, 16):
                 mm(v("TR", i, 256, 16, 0, 8), v("LTm", 8 * i, 8 * i + 8), v("E", i, 4096, 272), False, i == 15)
-            vcopy(v("RR", p1=8), v("TR", 0, 256, 1, 0, 8))
-            turn_a("RR", 256, 8, "mI")
         if part == 1:
-            turn_b(kP, 16, "TT", "mI")
+            vcopy(v("RR", p1=8), v("TR", 0, 256, 1, 0, 8))
+            lists(kP, "ZK", "RR", 256, 8)
 
     def pops():
-        tt(nn1, kP, fm1, A.subtract)
-        tt(hs, kP, hh, A.add)
-        ts(v("blB"), nn1, 1.0, A.is_ge)
-        ts(hk, hs, 1, A.bitwise_and)
+        tt(v("blB"), kP, fi, A.is_ge)
+        tt(nn, kP, fi, A.subtract)
+        tt(hq, kP, hh, A.not_equal)
         scan(v("scB"), v("blB"), v("ZR16"), A.add, A.add)
-        ts(nn4, nn1, 4096.0, A.mult)
-        tt(slot, ss, hk, A.add)
+        ts(nn4, nn, 1.0, A.add, 4096.0, A.mult)
+        tt(sq, ss, hq, A.add)
+        tt(hs, kP, hh, A.add)
         ts(k3, kP, 3.0, A.min, 2048.0, A.mult)
         mm(ro, v("SG"), v("scB"), True, False)
         mm(ro, v("TRI"), v("blB"), False, True)
-        tt(segf, nn4, slot, A.max)
+        tt(segf, nn4, sq, A.max)
+        ts(hk, hs, 1, A.bitwise_and)
         ts(v("gU"), segf, 4096.0, A.min)
 
     def move(t, part):
         if part == 0:
             tt(v("zt"), ind(v("G", 0, 4112), v("gU")), v("Z%d" % t), A.add)
-            for h in range(2):
-                mm(v("TR", 128 * h, 128 * h + 128), v("zt", 128 * h, 128 * h + 128), v("mI"), True, True)
-        if part == 1:
-            ts(v("WTS"), v("TR", 0, 256), 0.0, A.max, 255.0, A.min)
-        if part == 2:
             ts(v("Z%d" % (t + 1)), v("zt"), 0.0, A.max, 255.0, A.min)
-
-    def compact(t, part):
-        if part == 0:
-            tt(pos, ro, v("LA", 32, 48), A.min)
-            ts(v("cU"), pos, 511.0, A.add)
-            vcopy(ind(v("CR"), v("cU")), v("JL"))
-            turn_a("CR", 128, 128, "G8")
         if part == 1:
-            turn_b(cP, 8, "TT", "mI", 0.0625)
-        if part == 2:
-            vcopy(v("CL%d" % t), cP)
-            send(rank + 1 + t, v("CL%d" % t), "QL%d" % t, "r_l%d" % t)
+            ts(v("TR", 0, 128), v("zt", 128, 256), 0.0, A.max, 255.0, A.min)
+
+    def post(t):
+        tt(pos, ro, v("LA", 32, 48), A.min)
+        ts(v("CL%d" % t), pos, 511.0, A.add)
+        send(rank + 1 + t, v("CL%d" % t), "QL%d" % t, "r_l%d" % t)
 
     def payload():
-        ts(t1, nn1, 1.0, A.is_ge, 2048.0, A.mult)
+        ts(t1, v("blB"), 2048.0, A.mult)
         tt(t1, t1, aF, A.add)
         vcopy(v("pU"), t1)
         vcopy(v("s16"), ind(v("SI"), v("pU")))
@@ -431,11 +434,14 @@ def rank_program(g, core, T, topo):
     def decide(t, part):
         if part == 0:
             ts(ask2, ro, -399.0, A.is_lt, 2.0, A.mult)
-            ts(e0, nn1, 1.0, A.is_equal)
-            ts(v1, nn1, 2.0, A.mult, 8.0 * t + 10.0, A.add)
+            ts(e0, nn, 0.0, A.is_equal)
+            ts(u1, nn, 10.0, A.mult, 32.0 * t + 50.0, A.add)
+            ts(u2, nn, 6.0, A.mult, 32.0 * t + 46.0, A.add)
             tt(hp, e0, hk, A.is_equal)
-            tt(nw, nn1, ask2, A.is_gt)
-            ts(popf, nn1, 0.0, A.is_le)
+            tt(nw, nn, ask2, A.is_ge)
+            tt(v1, u1, u2, A.max)
+            ts(popf, nn, 0.0, A.is_lt)
+            tt(slot, ss, hk, A.add)
             tt(v2, v1, hp, A.add)
             tt(nput, nw, popf, A.max)
             tt(base, k3, aF, A.add)
@@ -463,26 +469,33 @@ def rank_program(g, core, T, topo):
             vcopy(ind(v("G"), v("nU", 0, 16)), v("LX"))
 
     def question(t, part):
-        ql = v("QL%d" % t, 0, 7)
-        if part == 0:
-            act(v("goal"), ind(v("X"), v("QA%d" % t)))
-        if part == 1:
-            act(v("zc"), ind(v("QZ%d" % t), ql))
-            act(v("gk"), ind(v("goal"), ql))
-        if part == 2:
-            mm(v("KA", 256, 368), v("WX"), v("zc"), True, True)
-            mm(v("KA", 384, 512, 1, 0, 112), v("gk"), v("mI"), True, False)
-            mm(v("KA", 384, 512, 1, 0, 112), v("zc"), v("mNI"), False, True)
-        if part == 3:
-            a, b = v("TI", 0, 112), v("TJ", 0, 112)
-            vcopy(a, v("KA", 256, 368))
-            ts(v("WTA", p1=112), v("KA", 384, 512, 1, 0, 112), -16.0, A.max, 16.0, A.min)
+        a, b, qz = v("TI"), v("TJ"), v("QZ%d" % t)
+        if part == "x":
+            mm(v("KA", 0, 256), v("WX"), qz, True, True)
+        if part == "u":
+            vcopy(a, v("KA", 0, 256))
             ts(b, a, 4095, A.bitwise_and)
             ts(v("Y1"), b, ycol, A.add)
-            tt(v("Y2"), v("Y1"), v("Y1"), A.mult)
+        if part == "sq":
+            act(v("Y2"), v("Y1"), F.Square)
+        if part == "slot":
             ts(a, v("Y2"), 0.03125, A.mult, rcol, A.add)
             ts(b, a, 4095, A.bitwise_and)
-            vcopy(v("CC"), b)
+        if part == "goal":
+            act(v("goal"), ind(v("X"), v("QA%d" % t)))
+        if part == "e":
+            mm(v("KA", 256, 512), v("mE", 0, 128), v("goal"), True, False)
+            mm(v("KA", 256, 512), v("mE", 128, 256), qz, False, True)
+        if part == "pack":
+            tt(v("PK"), b, v("KA", 256, 512), A.add)
+        if part == "pick":
+            vcopy(ind(v("CW"), v("QL%d" % t)), v("PK"))
+            ts(v("TI", 0, 112), v("CW", 0, 112), 4095, A.bitwise_and)
+            ts(v("TJ", 0, 112), v("CW", 0, 112), 12, A.arith_shift_right)
+            vcopy(v("CC"), v("TI", 0, 112))
+            ts(v("eB"), v("TJ", 0, 112), -16.0, A.max, 16.0, A.min)
+        if part == "clip":
+            ts(v("D3", 64, 112), v("TJ", 64, 112), -16.0, A.max, 16.0, A.min)
         if part == 4:
             mm(v("KA", 0, 128), one_row, v("JL", 0, 128, 1, 0, 1), True, False)
             mm(v("KA", 0, 128), v("BR", p1=1), one_row, False, False)
@@ -508,189 +521,173 @@ def rank_program(g, core, T, topo):
         if part == 1:
             ts(v("YA" if t == 2 else "T16", p1=8), v("TR", 0, 256, 1, 0, 8), -1.0, A.mult, -32.0, A.add)
             if t < 2:
-                turn_a("T16", 256, 8, "mIh")
                 mm(v("D2", 0, 256), v("RP", p1=8), v("T16", p1=8), True, True)
+                lists(aP, "ZA", "T16", 256, 8)
         if part == 2:
-            turn_b(aP, 16, "TH", "mIh")
             vcopy(v("AR"), v("D2", 0, 256))
         if part == 3:
-            aN = "aU%d" % (t + 1)
-            vcopy(v(aN, 0, 16), aP)
+            for r in range(4):
+                ts(v("aU", r, 64, 4), aP, 2048.0 * r, A.add)
             vcopy(aF, aP)
-        if part == 4:
-            aN = "aU%d" % (t + 1)
-            for r in range(1, 4):
-                ts(v(aN, 16 * r, 16 * r + 16), aP, 2048.0 * r, A.add)
+            vcopy(v("aS%d" % (t + 1)), aP)
 
     constants(0)
     start()
-    constants(1)
-    send(rank + 1, v("aU0"), "QA0", "r_a0")
     send(rank + 1, v("Z0"), "QZ0", "r_z0")
-    constants(3)
-    compare(0, 8)
-    table(0)
-    table(1)
-    compare(8, 16)
-    constants(2)
-    places(0)
-    table(2)
-    table(3)
-    places(1)
-    constants(4)
-    cells(0, 0)
-    cells(0, 1)
+    send(rank + 1, v("aS0"), "QA0", "r_a0")
     constants(7)
-    succ(0)
-    centres("S", 2048, 3072)
-    cells(0, 2)
-    pops()
-    compact(0, 0)
-    centres("S", 3072, 4096)
-    compact(0, 1)
-    constants(5)
-    compact(0, 2)
-    payload()
-    keys(True)
-    centres("S", 0, 1024)
-    sums("cS", 4, 8, 2)
-    move(0, 0)
-    constants(6)
-    move(0, 1)
-    move(0, 2)
-    send(rank + 2, v("Z1"), "QZ1", "r_z1")
-    question(0, 0)
-    centres("S", 1024, 2048)
-    dS("4V", "5V", "6V", "7V")
-    question(0, 1)
-    dS("0S")
-    decide(0, 0)
-    sums("AB", 4, 8, 1)
-    question(0, 2)
-    dS("1S")
-    decide(0, 2)
-    dS("2S")
-    question(0, 3)
-    dS("3S")
-    sums("AB", 0, 3, 0, stop=True)
-    sums("AB", 3, 4, 0, stop=True)
-    decide(0, 1)
-    cands("S", 0, 1024)
-    constants(8)
-    least(0, 0)
-    question(0, 4)
-    cands("S", 1024, 1792)
-    least(0, 1)
-    least(0, 2)
-    least(0, 3)
-    send(rank + 2, v("aU1", 0, 16), "QA1", "r_a1")
-    succ(1)
-    dA("0S", "1S")
-    least(0, 4)
-    decide(0, 3)
-    dA("2S", "3S")
-    cells(1, 0)
-    sA("0S", "1S", "2S", "3S", stop=True)
-    centres("S", 2048, 3072)
-    compare(0, 8)
-    question(0, 5)
-    question(0, 6)
-    cells(1, 1)
-    compare(8, 16)
-    centres("S", 3072, 4096)
+    compare(0, 16)
     places(0)
-    cells(1, 2)
+    mix((constants, 2), (cells, 0, 0))
+    for b in range(4):
+        table(b)
     places(1)
-    centres("S", 0, 1024)
+    cells(0, 1)
+    constants(4)
+    succ(0)
+    cells(0, 2)
+    centres("S", 0, 2048)
     pops()
-    compact(1, 0)
-    refill(0, 0)
-    compact(1, 1)
-    payload()
-    compact(1, 2)
-    question(1, 0)
-    centres("S", 1024, 2048)
+    post(0)
+    constants(3)
+    constants(8)
+    mix((constants, 5), (payload,), (decide, 0, 0))
+    question(0, "x")
+    for b in range(4):
+        dS(0, b, "c")
+    centres("S", 2048, 3072)
+    question(0, "goal")
+    move(0, 0)
+    send(rank + 2, v("Z1"), "QZ1", "r_z1")
+    mix((question, 0, "u"), (decide, 0, 2), (move, 0, 1))
+    question(0, "sq")
+    centres("S", 3072, 4096)
     keys(True)
-    sums("cS", 4, 8, 2)
+    question(0, "e")
+    for b in range(4):
+        dS(0, b, "ed")
+    mix((question, 0, "slot"), (constants, 6))
+    question(0, "pack")
+    question(0, "pick")
+    sums(1, 0, 16, raw=True)
+    cands("S", 0, 1024)
+    dV(0, 16)
+    sums(0, 0, 16)
+    sums(1, 0, 16, stop=True)
+    decide(0, 1)
+    cands("S", 1024, 1792)
+    question(0, 4)
+    dB(0, 0, "ec")
+    least(0, 0)
+    dB(1, 1, "ec")
+    dB(0, 0, "d")
+    dB(1, 1, "d")
+    decide(0, 3)
+    dB(2, 3, "ecd")
+    least(0, 1)
+    dB(3, 0, "ecd")
+    least(0, 2)
+    blocks(0, 14, 0, stop=True)
+    least(0, 3)
+    cells(1, 0)
+    compare(0, 16)
+    mix((question, 0, 5), (succ, 1))
+    question(0, 6)
+    send(rank + 2, v("aS1"), "QA1", "r_a1")
+    centres("S", 0, 1024)
+    places(0)
+    question(1, "x")
+    places(1)
+    cells(1, 1)
+    centres("S", 1024, 2048)
+    question(1, "u")
+    question(1, "sq")
+    cells(1, 2)
+    pops()
+    post(1)
+    centres("S", 2048, 3072)
+    refill(0, 0)
+    question(1, "goal")
+    for b in range(4):
+        dS(1, b, "c")
+    mix((question, 1, "slot"), (payload,), (decide, 1, 0))
     refill(0, 1)
     move(1, 0)
-    decide(1, 0)
+    centres("S", 3072, 4096)
+    question(1, "e")
     move(1, 1)
-    move(1, 2)
-    dS("4V", "0S", "5V", "1S")
-    question(1, 1)
-    decide(1, 2)
-    dS("6V")
-    question(1, 2)
-    dS("2S", "7V")
-    question(1, 3)
-    dS("3S")
-    sums("AB", 4, 8, 1)
+    for b in range(4):
+        dS(1, b, "ed")
+    keys(True)
+    question(1, "pack")
+    sums(1, 0, 16, raw=True)
+    dV(0, 8)
+    question(1, "pick")
     decide(1, 1)
     cands("S", 0, 1024)
-    sums("AB", 0, 3, 0, stop=True)
-    sums("AB", 3, 4, 0, stop=True)
-    decide(1, 3)
-    least(1, 0)
+    dV(8, 16)
+    sums(0, 0, 16)
+    sums(1, 0, 16, stop=True)
     question(1, 4)
     cands("S", 1024, 1792)
-    dA("0S")
+    dB(0, 0, "ec")
+    mix((least, 1, 0), (decide, 1, 2))
+    dB(1, 1, "ec")
+    dB(0, 0, "d")
+    dB(1, 1, "d")
+    decide(1, 3)
+    dB(2, 3, "ecd")
     least(1, 1)
+    dB(3, 0, "ecd")
     least(1, 2)
-    dA("1S")
+    blocks(0, 14, 0, stop=True)
     least(1, 3)
-    succ(2)
-    least(1, 4)
-    dA("2S", "3S")
-    sA("0S", "1S", "2S", "3S", stop=True)
     cells(2, 0)
-    compare(0, 4)
-    question(1, 5)
+    compare(0, 16)
+    mix((question, 1, 5), (succ, 2))
     question(1, 6)
-    centres("S", 2048, 3072)
-    compare(4, 16)
-    cells(2, 1)
-    centres("S", 3072, 4096)
+    centres("S", 0, 1024)
     places(0)
-    cells(2, 2)
     places(1)
-    pops()
-    refill(1, 0)
+    cells(2, 1)
     centres("S", 1024, 2048)
-    payload()
+    centres("V", 3584, 4096)
+    cells(2, 2)
+    pops()
+    centres("S", 2048, 3072)
+    for b in range(4):
+        dS(2, b, "c")
+    mix((decide, 2, 0), (payload,))
+    refill(1, 0)
+    decide(2, 1)
+    centres("S", 3072, 3584)
     keys(True)
-    sums("cS", 4, 8, 2)
-    centres("V", 0, 1024)
     refill(1, 1)
     move(2, 0)
-    decide(2, 0)
-    move(2, 1)
-    decide(2, 1)
-    decide(2, 2)
-    move(2, 2)
     store("Y", T.yz[:, :], v("Z3"), "o_z")
-    dS("4V", "0S", "5V", "1S")
+    mix((move, 2, 1), (decide, 2, 2))
+    for b in range(4):
+        dS(2, b, "ed")
+    sums(1, 0, 16, raw=True)
     decide(2, 3)
     for r in range(4):
         o = v("SA", 128 * r, 128 * r + 128)
         deps("Y", [o], [v("HF")])
         load("Y", o, T.HF[0:128:16, 2048 * r:2048 * r + 2048], "l_p%d" % r)
-    dS("6V", "2S", "7V", "3S")
-    sums("AB", 4, 8, 1)
-    sums("AB", 0, 3, 0, stop=True)
-    sums("AB", 3, 4, 0, stop=True)
-    tt(v("W2"), v("SA", 0, 256), v("SA", 256, 512), A.max)
+    dV(0, 16)
+    sums(0, 0, 16)
+    sums(1, 0, 16, stop=True)
     least(2, 0)
-    tt(v("TI"), v("W2", 0, 128), v("W2", 128, 256), A.max)
+    tt(v("W2"), v("SA", 0, 256), v("SA", 256, 512), A.max)
     least(2, 1)
     store("S", T.ya[:, :], v("YA", p1=8), "o_a")
-    ts(v("TJ"), v("TI"), 7, A.bitwise_and, 1, A.logical_shift_right)
-    ts(v("TK"), v("TI"), 1, A.bitwise_and)
-    ts(v("W1"), v("TJ"), -1.0, A.add)
+    tt(v("TI", 0, 128), v("W2", 0, 128), v("W2", 128, 256), A.max)
+    ts(v("TJ", 0, 128), v("TI", 0, 128), 7, A.bitwise_and, 1, A.logical_shift_right)
+    ts(v("TK"), v("TI", 0, 128), 1, A.bitwise_and)
+    vcopy(v("YF"), v("TJ", 0, 128))
     vcopy(v("YH"), v("TK"))
-    act(v("YF"), v("W1"), F.Abs)
-    store("Y", T.yh[:, :], v("YH"), "o_h")
-    store("S", T.yf[:, :], v("YF"), "o_f")
+    store("Y", T.yf[:, :], v("YF"), "o_f")
+    store("S", T.yh[:, :], v("YH"), "o_h")
     g.wait_ge(T.sem.sent, sent[0])
     for s, x in [("e" + q, cnt[q]) for q in cnt] + final:
         if known["G"].get(s, 0) < x:

@@ -7,29 +7,131 @@ def _b(n, c, d="bfloat16", w="sbuf", p=128):
     SCRATCH[n] = (w, [p, c], d)
 
 
-for _n, _c in (("X", 2048), ("G", 4368), ("HF", 8448), ("cS", 4096), ("AB", 4096), ("cA", 1792), ("AC", 1792), ("E", 4096),
+for _n, _c in (("X", 2048), ("G", 4736), ("HF", 8448), ("cS", 4096), ("AB", 4096), ("cA", 1792), ("AC", 1792), ("E", 4096),
                ("mI", 128), ("mNI", 128), ("m48", 128), ("mE", 256), ("SG", 128), ("G8", 128), ("LTm", 128), ("ZE", 144), ("ZK", 144),
-               ("NG", 128), ("ZS", 432), ("eB", 112), ("TRI", 128), ("WX", 128), ("KBS", 48), ("ONE", 128), ("JG", 128), ("J8", 128),
-               ("BR", 128), ("JL", 256), ("BM", 512), ("BQ", 128), ("B4", 64), ("V0", 128), ("RR", 256), ("RH", 1024),
+               ("NG", 128), ("ZS", 144), ("eB", 112), ("eT", 128), ("JR", 512), ("REP", 512), ("xq", 256), ("TRI", 128), ("WX", 128), ("KBS", 48), ("ONE", 128), ("JG", 128),
+               ("J8", 128), ("BR", 128), ("JL", 256), ("BM", 512), ("BQ", 112), ("V0", 128), ("RR", 256), ("RH", 1024),
                ("blB", 16), ("scB", 16), ("hB", 256), ("zt", 256), ("goal", 256), ("PB", 32), ("HV", 256), ("LX", 256), ("SA", 512),
-               ("Z0", 256), ("Z1", 256), ("Z2", 256), ("Z3", 256), ("AN0", 128), ("AN1", 128), ("LN0", 128), ("LN1", 128),
-               ("QZ0", 256), ("QZ1", 256)):
+               ("Z0", 256), ("Z1", 256), ("Z2", 256), ("Z3", 256), ("AN0", 112), ("AN1", 112), ("ZV", 144), ("ZJ", 144), ("Z8", 144), ("HW", 256), ("VT", 48), ("JT", 112), ("RB", 64),
+               ("QZ0", 112), ("QZ1", 256), ("ZC", 112), ("GW", 512)):
     _b(_n, _c)
 for _n, _c in (("mIh", 128), ("RP", 128), ("s16", 256), ("T16", 256), ("ZA", 144)):
     _b(_n, _c, "float16")
-for _n, _c in (("COL", 128), ("OH", 16), ("LA", 48), ("W1", 128), ("W2", 256), ("ZR16", 16), ("LL", 512), ("KS", 512), ("KT", 128),
-               ("aF", 16), ("Y1", 256), ("Y2", 256), ("YA", 256), ("YH", 128), ("YF", 128), ("CK", 32), ("cb", 64)):
+for _n, _c in (("COL", 128), ("JF", 2048), ("LA", 48), ("W1", 128), ("W2", 256), ("ZR16", 16), ("LL", 512), ("KS", 512), ("KT", 112),
+               ("aF", 16), ("Y2", 256), ("YA", 256), ("YH", 128), ("YF", 128), ("CK", 32), ("cb", 64)):
     _b(_n, _c, "float32")
 for _n, _c in (("SI", 4096), ("FI", 128), ("HI", 128), ("aI", 16), ("CI", 8), ("LI", 256), ("PK", 256), ("CW", 512),
-               ("TI", 256), ("TJ", 256), ("TK", 128), ("KI", 64), ("KQ", 32)):
+               ("TI", 256), ("TJ", 256), ("TK", 256), ("KI", 64), ("KQ", 32)):
     _b(_n, _c, "int32")
-for _n, _c in (("aS0", 16), ("aS1", 16), ("aS2", 16), ("aU", 64), ("AR", 256), ("sU", 256), ("gU", 16), ("nU", 32), ("pU", 16), ("vU", 16),
-               ("jU", 16), ("qU", 8), ("CC", 112), ("CL0", 16), ("CL1", 16), ("QL0", 16), ("QL1", 16), ("QA0", 16), ("QA1", 16)):
+for _n, _c in (("aS0", 16), ("aS1", 16), ("aS2", 16), ("AR", 256), ("sU", 256), ("gU", 16), ("nU", 96), ("pU", 16), ("vU", 16),
+               ("jU", 32), ("qU", 8), ("CC", 112), ("CS", 112), ("QC", 112), ("CL0", 16), ("CL1", 16), ("QL0", 16), ("QL1", 16), ("QA0", 16), ("QA1", 16)):
     _b(_n, _c, "uint16")
 for _n in ("D0", "D1", "D2", "D3", "KEY", "ML", "TR", "KA"):
     _b(_n, 512, "float32", "psum")
-SEMAPHORES = ["eV", "eS", "eP", "eG", "sent", "l_a", "l_z", "l_h", "l_f", "l_s", "l_x", "l_g", "l_p0", "l_p1", "l_p2", "l_p3",
-              "o_z", "o_a", "o_h", "o_f", "r_z0", "r_z1", "r_l0", "r_l1", "r_a0", "r_a1", "r_n0", "r_n1"]
+SEMAPHORES = ["eV", "eS", "eP", "eG", "sent", "l_a", "l_z", "l_h", "l_f", "l_s", "l_x", "l_g", "l_p0", "l_p1", "l_p2", "l_p3", "l_00", "l_03",
+              "o_z", "o_a", "o_h", "o_f", "r_c0", "r_z0", "r_z1", "r_l0", "r_l1", "r_a0", "r_a1", "r_n0", "r_n1"]
+STEPS = 3
+CYCLE, PE_CYCLE, GATHER, SCATTER = 0.00083, 0.00045, 1.56, 3.8
+SAME, CROSS, DMA, LOAD_RATE, ISSUE, FIRST, REMOTE, LINK_RATE = 0.06, 0.19, 2.3, 290e3, 0.8, 4.0, 3.0, 35e3
+BYTES = {"bfloat16": 2, "float16": 2, "uint16": 2, "float32": 4, "int32": 4}
+CASES = [{"": 1.0, "send": s, "load": d, "first": f, "wake": w, "plain": p, "gather": p * g, "scatter": p * c, "call": a}
+         for s, d, f, w, p, g, c, a in ((1.0, 1.0, 1.0, 1.0, 1.0, 1.0, 1.0, 0.0), (0.8, 1.15, 1.5, 1.2, 1.0, 1.2, 0.7, 0.02),
+                                        (1.4, 0.85, 0.7, 0.8, 1.0, 0.8, 1.3, 0.0), (1.0, 1.0, 1.0, 1.0, 1.3, 1.0, 1.0, 0.0),
+                                        (1.4, 1.0, 1.5, 1.3, 1.15, 1.0, 1.0, 0.03))]
+ORDER, PASSES = [], 2000
+
+
+def one_pass(calls, after, ready, rest):
+    left, ready = [0] * len(calls), list(ready)
+    for a in after:
+        for j, d in a:
+            left[j] += 1
+    free = {c["q"]: 0.0 for c in calls}
+    pool = {q: [i for i, c in enumerate(calls) if c["q"] == q and not left[i]] for q in free}
+    order, start = [], [0.0] * len(calls)
+    while len(order) < len(calls):
+        now, q = min((max(free[q], min(ready[i] for i in pool[q])), q) for q in pool if pool[q])
+        best = max((i for i in pool[q] if ready[i] <= now + 0.02), key=lambda i: (rest[i], -i))
+        cost = calls[best]["cost"]
+        for h in sorted((i for i in pool[q] if now + 0.02 < ready[i] < now + cost and rest[i] > rest[best]), key=lambda i: rest[i])[-1:]:
+            if ready[h] + max(rest[h], cost + rest[best]) < now + cost + rest[h]:
+                short = [i for i in pool[q] if max(ready[i], now) + calls[i]["cost"] <= ready[h] + 0.02]
+                best = max(short, key=lambda i: (rest[i], -i)) if short else h
+        pool[q].remove(best)
+        start[best] = max(now, ready[best])
+        free[q] = start[best] + calls[best]["cost"]
+        order.append(best)
+        for j, d in after[best]:
+            ready[j] = max(ready[j], free[q] + d)
+            left[j] -= 1
+            if not left[j]:
+                pool[calls[j]["q"]].append(j)
+    return order, start
+
+
+def length(calls, before, order, case, held=None):
+    last, end, why = {}, [0.0] * len(calls), [None] * len(calls)
+    for i in order:
+        c = calls[i]
+        by = last.get(c["q"])
+        t, queue = (0.0, False) if by is None else (end[by], True)
+        for p, late, wake in before[i]:
+            x = end[p] + late * case[calls[p]["kind"]] + wake * case["wake"]
+            if x >= t:
+                t, by, queue = x, p, False
+        end[i] = t + c["cost"] * case[c["work"]] + case["call"] * (c["q"] in "VS") + c["first"] * (case["first"] - 1)
+        last[c["q"]], why[i] = i, (by, queue)
+    t, i = max((end[i] + c["late"], i) for i, c in enumerate(calls))
+    while held is not None and i is not None:
+        if why[i][1]:
+            held.append((i, why[i][0]))
+        i = why[i][0]
+    return t
+
+
+def issue_order(calls):
+    n = len(calls)
+    after, before, waits = [[] for _ in calls], [[] for _ in calls], [[] for _ in calls]
+    for i, c in enumerate(calls):
+        for p, kind in c["preds"].items():
+            late, wake = (0.0, 0.0) if kind == "order" else (calls[p]["late"], SAME if calls[p]["q"] == c["q"] else CROSS)
+            after[p].append((i, late + wake))
+            before[i].append((p, late + wake))
+            waits[i].append((p, late, wake))
+    rest = [0.0] * n
+    for i in range(n - 1, -1, -1):
+        rest[i] = max([calls[i]["late"]] + [d + calls[j]["cost"] + rest[j] for j, d in after[i]])
+    rest = [s + c["urge"] for s, c in zip(rest, calls)]
+    runs = {}
+    for i, c in enumerate(calls):
+        runs.setdefault((c["q"], c["piece"]), []).append(i)
+    run_of = [runs[c["q"], c["piece"]] for c in calls]
+    runs = list(runs.values())
+    best, now, x, held = (1e9, None), 1e9, 1, []
+    for k in range(PASSES):
+        r = list(rest)
+        for _ in range(1 + k % 3 if k else 0):
+            x = (x * 1103515245 + 12345) % 2 ** 31
+            if k % 2 and held:
+                late, early = held[(x >> 8) % len(held)]
+                d = max(r[early] - r[late], 0.0) + 0.1 + (x >> 20) % 8 / 8.0
+                for i in run_of[late] if x >> 16 & 1 else run_of[early]:
+                    r[i] += d if x >> 16 & 1 else -d
+            else:
+                for i in runs[(x >> 8) % len(runs)]:
+                    r[i] += (x >> 20) % 25 / 8.0 - 1.5
+        order, start = one_pass(calls, after, [0.0] * n, r)
+        if k % 3 == 1:
+            r = [s + c["urge"] for s, c in zip(one_pass(calls, before, [c["late"] for c in calls], start)[1], calls)]
+            order = one_pass(calls, after, [0.0] * n, r)[0]
+        t = sum(length(calls, waits, order, case) / case["plain"] for case in CASES) / len(CASES)
+        if t < now + 0.03:
+            rest, now, held = r, t, []
+            for case in CASES:
+                length(calls, waits, order, case, held)
+            held = [(i, j) for i, j in held if run_of[i] is not run_of[j]]
+        best = min(best, (t, order))
+    return best[1]
 
 
 def rank_program(g, core, T, topo):
@@ -38,9 +140,6 @@ def rank_program(g, core, T, topo):
         return
     n = len(T.cores)
     H = {"V": g.vector, "S": g.scalar, "P": g.tensor, "G": g, "Y": g.sync}
-    cnt = {"V": 0, "S": 0, "P": 0, "G": 0}
-    known = {q: {} for q in H}
-    wr, rd, pacc = {}, {}, {}
 
     def v(name, c0=0, c1=None, st=1, p0=0, p1=None):
         sh = SCRATCH[name][1]
@@ -57,84 +156,67 @@ def rank_program(g, core, T, topo):
     def ind(win, off):
         return ("ind", win, off)
 
-    def wait(q, rec):
-        sem, val, kn = rec[1], rec[2], rec[3]
-        if known[q].get(sem, 0) >= val:
-            return
-        H[q].wait_ge(T.sem[sem], val)
-        for s, x in list(kn.items()) + [(sem, val)]:
-            if known[q].get(s, 0) < x:
-                known[q][s] = x
-
-    def flat(xs):
-        out = []
-        for x in xs:
-            if isinstance(x, tuple):
-                out += [x[1], x[2]] if x[0] == "ind" else [x]
-        return out
+    def width(x):
+        return 16 * width(x[2]) if x[0] == "ind" else len(range(x[1], x[2], x[3]))
 
     def meet(e, x):
-        return e[0] < x[2] and x[1] < e[1] and not (e[3] == x[3] > 1 and (e[0] - x[1]) % x[3])
+        return e[1] < x[2] and x[1] < e[2] and not (e[3] == x[3] > 1 and (e[1] - x[1]) % x[3])
 
-    def deps(q, ws, rs):
-        need = []
+    calls, wr, rd, bank_use, piece, urge = [], {}, {}, {}, [0], [0.0]
+
+    def note(q, run, cost, out, ins, sem=None, inc=1, late=0.0, kind="", first=0.0):
+        rs, flat = [], [x for x in ins if isinstance(x, tuple)]
+        for x in flat:
+            rs += [x[1], x[2]] if x[0] == "ind" else [x]
+        ws = [] if out is None else [out]
+        if out is not None and out[0] == "ind":
+            ws, rs = [out[1]], rs + [out[2]]
+        me, preds = len(calls), {}
         for x in ws + rs:
             if SCRATCH[x[0]][0] == "psum":
-                need += [r for k, r in pacc.get(x[0], {}).items() if k != q]
-            need += [e[2] for e in wr.get(x[0], []) if meet(e, x)]
-        for x in ws:
-            need += [e[2] for e in rd.get(x[0], []) if meet(e, x)]
-        for r in sorted(need, key=lambda r: -r[2]):
-            wait(q, r)
-
-    def note(rec, ws, rs, cover=True):
-        for x in ws + rs:
-            if SCRATCH[x[0]][0] == "psum":
-                pacc.setdefault(x[0], {})[rec[0]] = rec
-        for x in ws:
-            if SCRATCH[x[0]][0] == "psum":
-                if rec[0] == "V":
-                    pacc[x[0]]["w"] = rec
+                use = bank_use.setdefault(x[0], {})
+                for k, p in use.items():
+                    if p != me and preds.get(p) != "wait":
+                        preds[p] = "order" if k == q else "wait"
+                use[q] = me
+                if q == "V" and x in ws:
+                    use["written"] = me
                 continue
-            if x[3] == 1 and cover:
-                wr[x[0]] = [e for e in wr.get(x[0], []) if not (x[1] <= e[0] and e[1] <= x[2])]
-                rd[x[0]] = [e for e in rd.get(x[0], []) if not (x[1] <= e[0] and e[1] <= x[2])]
-            wr.setdefault(x[0], []).append((x[1], x[2], rec, x[3]))
+            for e, p in wr.get(x[0], []) + (rd.get(x[0], []) if x in ws else []):
+                if meet(e, x):
+                    preds[p] = "wait"
+        for x in ws:
+            if SCRATCH[x[0]][0] != "psum":
+                if x[3] == 1 and out[0] != "ind":
+                    for d in (wr, rd):
+                        d[x[0]] = [(e, p) for e, p in d.get(x[0], []) if not (x[1] <= e[1] and e[2] <= x[2])]
+                wr.setdefault(x[0], []).append((x, me))
         for x in rs:
             if SCRATCH[x[0]][0] != "psum":
-                rd[x[0]] = [e for e in rd.get(x[0], [])
-                            if not (e[2][0] == rec[0] and not e[2][4] and x[3] == 1 and x[1] <= e[0] and e[1] <= x[2])]
-                rd[x[0]].append((x[1], x[2], rec, x[3]))
+                rd.setdefault(x[0], []).append((x, me))
+        if not calls or calls[-1]["out"] != (ws[0][0] if ws else None):
+            piece[0] += 1
+        work = "" if run is None or sem else "scatter" if out[0] == "ind" else "gather" if len(rs) > len(flat) else "plain"
+        calls.append({"q": q, "run": run, "work": work, "urge": urge[0], "cost": cost, "late": late, "preds": preds, "sem": sem, "kind": kind, "first": first,
+                      "out": ws[0][0] if ws else None, "piece": piece[0] // 4, "inc": inc})
+        return me
 
-    held = []
-
-    def mix(*pieces):
-        rows = []
-        for p in pieces:
-            held.append([])
-            p[0](*p[1:])
-            rows.append(held.pop())
-        for k in range(max(len(r) for r in rows)):
-            for r in rows:
-                if k < len(r):
-                    r[k][0](*r[k][1:])
-
-    def op(q, call, out, *ins):
-        if held:
-            return held[-1].append((op, q, call, out) + ins)
-        ws, rs = flat([out]), flat(ins)
-        if out[0] == "ind":
-            ws, rs = [out[1]], rs + [out[2]]
-        deps(q, ws, rs)
-        cnt[q] += 1
-        call().then_inc(T.sem["e" + q], 1)
-        note((q, "e" + q, cnt[q], dict(known[q]), False), ws, rs, out[0] != "ind")
+    def op(q, call, out, *ins, rate=None):
+        full = [x for x in (out,) + ins if isinstance(x, tuple) and width(x) == width(out)]
+        if out[0] == "ind" or any(x[0] == "ind" for x in full):
+            cost = 0.06 + CYCLE * width(out) * (SCATTER if out[0] == "ind" else GATHER)
+        else:
+            if rate is None:
+                rate = 0.5 if q == "V" and all(BYTES[SCRATCH[x[0]][2]] == 2 for x in full) else 1.0
+            cost = 0.025 + CYCLE * max(64, width(out) * rate) if q == "V" else 0.08 + CYCLE * width(out)
+        note(q, call, cost, out, ins)
 
     def vcopy(out, in_):
         op("V", lambda: g.vector.tensor_copy(out=ap(out), in_=ap(in_)), out, in_)
 
     def tt(out, a, b, o):
-        op("V", lambda: g.vector.tensor_tensor(out=ap(out), in0=ap(a), in1=ap(b), op=o), out, a, b)
+        both = a[0] != "ind" and SCRATCH[a[0]][0] == SCRATCH[b[0]][0]
+        op("V", lambda: g.vector.tensor_tensor(out=ap(out), in0=ap(a), in1=ap(b), op=o), out, a, b, rate=1.0 + both)
 
     def ts(out, a, s1, o1, s2=None, o2=None):
         if o2 is None:
@@ -145,51 +227,49 @@ def rank_program(g, core, T, topo):
     def scan(out, a, b, o0, o1):
         op("V", lambda: g.vector.tensor_tensor_scan(out=ap(out), data0=ap(a), data1=ap(b), initial=0.0, op0=o0, op1=o1), out, a, b)
 
-    def act(out, in_, f=F.Copy, scale=1.0):
-        op("S", lambda: g.scalar.activation(out=ap(out), in_=ap(in_), func=f, scale=ap(scale)), out, in_, scale)
-
-    def copy(q, out, in_):
-        vcopy(out, in_) if q == "V" else act(out, in_)
-
-    def mm(out, lhsT, rhs, start, stop):
-        op("P", lambda: g.tensor.matmul(ap(out), ap(lhsT), ap(rhs), start, stop), out, lhsT, rhs)
-
-    def iota(out, pat, base=0, mult=0):
-        if SCRATCH[out[0]][2] == "int32":
-            op("G", lambda: g.iota(ap(out), pat, base, mult), out)
-        else:
-            op("G", lambda: g.iota(ap(out), pat, base, mult, allow_small_or_imprecise_dtypes=True), out)
-
-    def select(out, in_, pat, o, x, mult):
-        op("G", lambda: g.affine_select(ap(out), ap(in_), pat, o, x, 0, mult), out, in_)
+    def act(out, in_, f=F.Copy, scale=1.0, bias=0.0):
+        op("S", lambda: g.scalar.activation(out=ap(out), in_=ap(in_), func=f, scale=ap(scale), bias=ap(bias)), out, in_, scale, bias)
 
     def fill(out, x):
         op("V", lambda: g.vector.memset(ap(out), x), out)
 
-    def load(q, out, in_, sem):
-        H[q].dma_start(out=ap(out), in_=in_).then_inc(T.sem[sem], 16)
-        note((q, sem, 16, {}, True), [out], [])
+    def mm(out, lhsT, rhs, start, stop):
+        note("P", lambda: g.tensor.matmul(ap(out), ap(lhsT), ap(rhs), start, stop),
+             0.005 + PE_CYCLE * max(min(64, width(lhsT)), width(rhs)), out, (lhsT, rhs))
 
-    final, sent = [], [0]
+    def iota(out, pat, base=0, mult=0):
+        small = SCRATCH[out[0]][2] != "int32"
+        note("G", lambda: g.iota(ap(out), pat, base, mult, allow_small_or_imprecise_dtypes=small), 0.13 + 2 * CYCLE * width(out), out, ())
 
-    def store(q, out, in_, sem):
-        deps(q, [], [in_])
-        H[q].dma_start(out=out, in_=ap(in_)).then_inc(T.sem[sem], 16)
+    def select(out, in_, pat, o, x, mult):
+        masks.append(note("G", lambda: g.affine_select(ap(out), ap(in_), pat, o, x, 0, mult), 0.17 + 2 * CYCLE * width(out), out, (in_,)))
+
+    masks = []
+    loaded, last_load, sent, final = [0.0], {}, [0, 0], []
+
+    def load(q, out, in_, sem, *view):
+        loaded[0] += 128 * width(out) * BYTES[SCRATCH[out[0]][2]] / LOAD_RATE
+        me = note(q, lambda: H[q].dma_start(out=ap(out), in_=in_), 0.05, out, view, sem, 16, DMA + loaded[0], "load")
+        if q in last_load:
+            calls[me]["preds"][last_load[q]] = "order"
+        last_load[q] = me
+
+    def move_dma(q, out, src, view, sem):
+        note(q, lambda: H[q].dma_start(out=ap(out), in_=src), 0.05, out if isinstance(out, tuple) else None, (view,), sem, 16, DMA + 0.4)
         final.append((sem, 16))
 
-    def send(dst, src, buf, sem):
-        if held:
-            return held[-1].append((send, dst, src, buf, sem))
-        to = T.cores[dst % n]
+    def send(d, src, buf, sem):
+        to, buf = T.cores[(rank + d) % n], buf if isinstance(buf, tuple) else v(buf)
         rid, pid = topo.addr(to)[0], topo.addr(to)[1]
         e = topo.engines(core, to)[:8]
-        deps("G", [], [src])
-        sent[0] += len(e)
-        g.remote_dma(ap(v(buf)), ap(src), T.sem[sem], T.sem.sent, pid, rid, sum(1 << x for x in e))
-
-    def arrive(buf, sem, src):
-        e = len(topo.engines(T.cores[src % n], core)[:8])
-        wr[buf] = [(0, SCRATCH[buf][1][1], ("R", sem, e, {}, True), 1)]
+        me = note("G", lambda: g.remote_dma(ap(buf), ap(src), T.sem[sem], T.sem.sent, pid, rid, sum(1 << x for x in e)),
+                  ISSUE + (0.0 if sent[0] else FIRST), None, (src,), "sent", 0, REMOTE + 256 * abs(d) * width(src) / LINK_RATE,
+                  "send", 0.0 if sent[0] else FIRST)
+        for p in [sent[1]] if sent[0] else masks:
+            calls[me]["preds"][p] = "order"
+        sent[:2] = sent[0] + len(e), sent[1] if sent[0] else me
+        here = note("R", None, 0.0, buf, (), sem, len(topo.engines(T.cores[(rank - d) % n], core)[:8]))
+        calls[here]["preds"][me] = "wait"
 
     load("Y", v("aI"), T.a0[:, :], "l_a")
     load("S", v("FI"), T.fl0[:, :], "l_f")
@@ -198,496 +278,385 @@ def rank_program(g, core, T, topo):
     load("Y", v("SI", 0, 2048), T.su[:, :], "l_s")
     load("Y", v("X"), T.xs[:, :], "l_x")
     load("Y", v("G", 0, 4096), T.gs[:, :], "l_g")
-    for t in range(2):
-        for b in ("QZ", "QA", "QL"):
-            arrive(b + str(t), "r_" + b[1].lower() + str(t), rank - 1 - t)
-        arrive("LN%d" % t, "r_n%d" % t, rank + 1 + t)
 
-    def J(a, b):
-        return v("SI", 2048 + a, 2048 + b)
-
-    def col(k):
-        return v("COL", 4 * k, 4 * k + 1)
-    (pF, pm, pg, g15, wi, k15, ycol, rcol, c1) = [col(k) for k in range(9)]
+    (pF, pm, pg, g15, wi, k15, ycol, rcol, c1, p31, half, low, high) = [v("COL", 4 * k, 4 * k + 1) for k in range(13)]
     one_row = v("ONE", p1=1)
+    iota(v("CI", 0, 1), [[0, 1]], 0, 1)
+    iota(v("JG"), [[1, 8], [0, 16]])
+    iota(v("J8"), [[0, 16], [1, 8]])
+    iota(v("JF", 0, 512), [[1, 512]])
+    iota(v("JL"), [[1, 256]])
+    iota(v("SI", 2048, 2560), [[1, 512]])
+    masks.append(len(calls) - 1)
+    iota(v("BR", p1=1), [[0, 8], [112, 16]])
+    iota(v("CK"), [[0, 2], [32, 2], [0, 8]])
+    for k, x in enumerate((3, 2, 9, 8, 18, 19, 29, 28)):
+        iota(v("VT", k, 48, 16), [[32, 3]], 32 + x)
+    for k in range(1, 4):
+        act(v("JF", 512 * k, 512 * k + 512), v("JF", 0, 512), F.Identity, bias=512.0 * k)
+    fill(v("HF", 2048, 3328), 0.0)
+    for k in range(2):
+        act(v("HF", 1024 * k, 1024 * k + 1024), v("HF", 2048, 3072))
+    fill(v("HF", 3328, 4608), 0.0)
+    act(v("HF", 4608, 5888), v("HF", 2048, 3328))
+    load("Y", v("HF", 5888, 7168), T.HF[:, 2048:3328], "l_00", v("HF", 2048, 3328))
+    vcopy(pF, v("CI", 0, 1))
+    for j, (out, o, s) in enumerate(((pm, A.bitwise_and, 15), (pg, A.logical_shift_right, 4), (p31, A.bitwise_and, 31))):
+        ts(v("CI", 1 + j, 2 + j), v("CI", 0, 1), s, o)
+        vcopy(out, v("CI", 1 + j, 2 + j))
+    ts(g15, pg, 16.0, A.mult, 15.0, A.add)
+    ts(k15, pF, 16.0, A.mult, 15.0, A.add)
+    ts(wi, pm, 2.0, A.mult, 1.0, A.add)
+    tt(c1, wi, wi, A.mult)
+    ts(ycol, wi, 16.0, A.mult, 129.0 * 4096, A.add)
+    ts(rcol, c1, -8.0, A.mult, -0.40625, A.add)
+    ts(v("G8"), v("J8"), pg, A.is_equal)
+    ts(v("SG"), v("JG"), pg, A.is_equal)
+    ts(v("NG"), v("JG"), pg, A.is_equal, -1.0, A.mult)
+    select(v("LTm"), v("G8"), [[1, 16], [16, 8]], A.is_gt, 0.0, -1)
+    select(v("NG"), v("NG"), [[-1, 128]], A.is_ge, 0.0, 1)
+    select(v("TRI"), v("NG"), [[-1, 128]], A.not_equal, -512.0, 1)
+    for out in ("mI", "mIh"):
+        ts(v(out), v("JL", 0, 128), pF, A.is_equal)
+    for out, c, f in (("ZE", g15, 0.0625), ("ZK", k15, 1.0), ("ZA", k15, 1.0)):
+        ts(v(out), v("JL", 0, 144), c, A.is_equal, f, A.mult)
+    ts(low, pm, 0.0, A.is_equal)
+    ts(high, pm, 1.0, A.is_equal)
+    for out, src, f in ((v("mNI"), v("mI"), -1.0), (v("m48"), v("mI"), -48.0), (v("mE", 0, 128), v("mI"), 4096.0),
+                        (v("mE", 128, 256), v("mI"), -4096.0), (v("ZS"), v("ZE"), 32768.0), (v("Z8"), v("ZE"), 16.0),
+                        (v("ZV"), v("Z8"), low), (v("ZJ"), v("Z8"), high), (v("WX"), v("SG"), wi), (v("KBS", 0, 16), v("G8", 0, 16), 1024.0),
+                        (v("KBS", 16, 32), v("G8", 0, 16), 2048.0), (v("KBS", 32, 48), v("G8", 0, 16), -1024.0)):
+        act(out, src, scale=f)
+    ts(v("W2", 0, 16), v("JL", 0, 16), 16.0, A.mult, pm, A.add)
+    for k, f in enumerate((4096.0, 8192.0, -255.0)):
+        ts(v("LA", 16 * k, 16 * k + 16), v("W2", 0, 16), f, A.add)
+    ts(v("RP"), v("JG"), pF, A.is_equal)
+    for out, x in ((half, 128.5001220703125), (v("ZR16"), 0.0), (v("G", 4096, 4352), 0.0), (v("G", 4464, 4608), 0.0), (v("G", 4720, 4736), 0.0),
+                   (v("CW", 0, 112), 0), (v("GW", 0, 112), 0.0), (v("ONE"), 1.0), (v("BM"), -64.0), (v("BM", 0, 512, 16), 33554432.0)):
+        fill(out, x)
+    act(v("BQ"), v("BM", 0, 112), F.Relu)
 
-    def constants(part):
-        if part == 0:
-            iota(v("CI", 0, 1), [[0, 1]], 0, 1)
-            iota(v("JG"), [[1, 8], [0, 16]])
-            iota(v("J8"), [[0, 16], [1, 8]])
-            iota(J(0, 512), [[1, 512]])
-            iota(v("JL"), [[1, 256]])
-            fill(v("HF", 2048, 3584), 0.0)
-            vcopy(pF, v("CI", 0, 1))
-            bits = ((pm, A.bitwise_and, 15), (pg, A.logical_shift_right, 4))
-            for j, (out, o, s) in enumerate(bits):
-                ts(v("CI", 1 + j, 2 + j), v("CI", 0, 1), s, o)
-            fill(v("ZR16"), 0.0)
-            for j, (out, o, s) in enumerate(bits):
-                vcopy(out, v("CI", 1 + j, 2 + j))
-            ts(g15, pg, 16.0, A.mult, 15.0, A.add)
-            ts(v("G8"), v("J8"), pg, A.is_equal)
-            ts(v("NG"), v("JG"), pg, A.is_equal, -1.0, A.mult)
-            ts(v("SG"), v("JG"), pg, A.is_equal)
-            select(v("LTm"), v("G8"), [[1, 16], [16, 8]], A.is_gt, 0.0, -1)
-            select(v("NG"), v("NG"), [[-1, 128]], A.is_ge, 0.0, 1)
-            select(v("TRI"), v("NG"), [[-1, 128]], A.not_equal, -512.0, 1)
-            for k in range(1, 4):
-                ts(J(512 * k, 512 * k + 512), J(0, 512), 512.0 * k, A.add)
-        if part == 1:
-            ts(v("OH"), v("JL", 0, 16), pm, A.is_equal)
-            ts(v("mI"), v("JL", 0, 128), pF, A.is_equal)
-        if part == 2:
-            ts(k15, pF, 16.0, A.mult, 15.0, A.add)
-            ts(v("ZE"), v("JL", 0, 144), g15, A.is_equal, 0.0625, A.mult)
-            ts(v("LA", 32, 48), v("JL", 0, 16), 16.0, A.mult, pm, A.add)
-            ts(v("ZK"), v("JL", 0, 144), k15, A.is_equal)
-            fill(v("G", 4096, 4112), 0.0)
-            ts(v("LA", 0, 16), v("LA", 32, 48), 4112.0, A.add)
-            ts(v("LA", 16, 32), v("LA", 32, 48), 8192.0, A.add)
-            ts(wi, pm, 2.0, A.mult, 1.0, A.add)
-            ts(v("LA", 32, 48), v("LA", 32, 48), -255.0, A.add)
-        if part == 3:
-            iota(v("BR", p1=1), [[0, 8], [128, 16]])
-            iota(v("CK"), [[0, 2], [32, 2], [0, 8]])
-        if part == 4:
-            ts(v("WX"), v("SG"), wi, A.mult)
-            tt(c1, wi, wi, A.mult)
-            ts(v("mNI"), v("mI"), -1.0, A.mult)
-            ts(ycol, wi, 16.0, A.mult)
-            ts(v("m48"), v("mI"), -48.0, A.mult)
-            ts(rcol, c1, -8.0, A.mult, -0.40625, A.add)
-            vcopy(v("mIh"), v("mI"))
-            for k, f in enumerate((1.0, 2.0, -1.0)):
-                ts(v("KBS", 16 * k, 16 * k + 16), v("G8", 0, 16), 1024.0 * f, A.mult)
-        if part == 5:
-            for k, f in enumerate((4096.0, -4096.0)):
-                ts(v("mE", 128 * k, 128 * k + 128), v("mI"), f, A.mult)
-            fill(v("CW", 0, 112), 0)
-            fill(v("B4"), 0.0)
-            fill(v("BM"), -64.0)
-            fill(v("B4", 0, 64, 4), -1024.0)
-            fill(v("BM", 0, 512, 16), 33554432.0)
-            ts(v("RP"), v("JG"), pF, A.is_equal)
-            vcopy(v("ZA"), v("ZK"))
-        if part == 6:
-            fill(v("ONE"), 1.0)
-            for k, f in enumerate((1.0, 2.0, -1.0)):
-                ts(v("ZS", 144 * k, 144 * k + 144), v("ZE"), 32768.0 * f, A.mult)
-            ts(v("BR", p1=1), v("BR", p1=1), 1664.0, A.min)
-            ts(v("BQ"), v("BM", 0, 128), 0.0, A.max)
-        if part == 7:
-            iota(v("HF", 3584, 5120), [[0, 1536]])
-        if part == 8:
-            iota(v("HF", 5120, 8448), [[0, 3328]])
+    L = [v("LL", 16 * x, 16 * x + 16) for x in range(32)]
+    (ss, nn, nn4, segf, t1, ask2, popf, x2, code, k3, pos, t2, t3, tk, dj, j0, fresh) = L[:17]
+    nput, nw, slot, base = L[24:28]
+    two, own = v("LL", 384, 416), v("LL", 416, 448)
+    fi, hh, hs, hk, q8, mx = [v("LI", 16 * x, 16 * x + 16) for x in range(6)]
+    kP, ro, aP = v("ML", 64, 80), v("ML", 80, 96), v("ML", 112, 128)
+    aF, popped = v("aF"), []
+
+    def lists(o, z, src, c1, rows=128, c0=0):
+        for i in range(16):
+            mm(o, v(z, 15 - i, 143 - i, 1, 0, rows), v(src, c0 + i, c1, 16, 0, rows), i == 0 and not c0, i == 15)
+
+    def gather(engines, out, win, lst):
+        for k, q in enumerate(engines):
+            c1 = min(512 * k + 512, width(v(out)))
+            (vcopy if q == "V" else act)(v(out, 512 * k, c1), ind(win, v(lst, 32 * k, c1 // 16)))
+            if q == "V" and out == "cS":
+                for p in popped:
+                    calls[-1]["preds"].setdefault(p, "order")
 
     def start():
         vcopy(v("aS0"), v("aI"))
+        vcopy(aF, v("aI"))
+        vcopy(v("AR"), ind(v("JF"), v("aS0")))
+        send(1, v("aS0"), "QA0", "r_a0")
+        iota(v("SI", 2560, 3072), [[1, 512]], 512)
+        calls[-1]["preds"][sent[1]] = "order"
         ts(v("W1"), v("FI"), 2.0, A.mult)
-        constants(1)
-        vcopy(v("aF"), v("aI"))
         tt(v("V0"), v("W1"), v("HI"), A.add)
-        vcopy(v("AR"), ind(J(0, 2048), v("aS0")))
-        ts(q8, v("aI"), 127, A.bitwise_and)
-        vcopy(v("vU"), q8)
-        for k in range(16):
-            act(v("AB", 128 * k, 128 * k + 128), v("V0"), scale=v("OH", k, k + 1))
+        note("Y", lambda: g.sync.dma_start(out=T.HF[0:128:16, 0:2048], in_=T.V0[:, :]), 0.05, v("HF", 0, 2048), (v("V0"),), "l_03", 16,
+             DMA + loaded[0], "load")
+        calls[-1]["preds"][last_load["Y"]] = "order"
 
-    def table(b):
-        mm(v("D%d" % b), v("SG"), v("AB", 512 * b, 512 * b + 512), True, True)
-        act(v("HF", 512 * b, 512 * b + 512), v("D%d" % b))
-
-    def lists(o, z, src, c1, rows=128):
-        for i in range(16):
-            mm(o, v(z, 15 - i, 143 - i, 1, 0, rows), v(src, i, c1, 16, 0, rows), i == 0, i == 15)
-
-    L = [v("LL", 16 * x, 16 * x + 16) for x in range(32)]
-    (ss, nn, nn4, segf, t1, ask2, popf, e0, hp, u1, u2, v1, v2, k3, pos, t2, t3, hq, sq) = L[:19]
-    nput, nw, slot, base = L[24:28]
-    two, own = v("LL", 384, 416), v("LL", 416, 448)
-    mx, fi, hh, hs, hk, q8 = [v("LI", 16 * x, 16 * x + 16) for x in range(6)]
-    kP, ro, aP = v("ML", 64, 80), v("ML", 80, 96), v("ML", 112, 128)
-    aF, bank = v("aF"), v("G", 0, 4096)
-
-    def centres(q, c0, c1):
-        copy(q, v("cS", c0, c1), ind(v("X"), v("sU", c0 // 16, c1 // 16)))
-
-    def cands(q, c0, c1):
-        copy(q, v("cA", c0, c1), ind(bank, v("CC", c0 // 16, c1 // 16)))
-
-    def dA(l0, l1):
-        for m in range(16):
-            tt(v("AC", 16 * l0 + m, 16 * l1, 16), v("cA", 16 * l0 + m, 16 * l1, 16), v("D3", l0, l1), A.max)
-
-    def dB(k, b, parts):
-        wd = min(512, 1792 - 512 * k)
-        if "e" in parts:
-            for m in range(16):
-                mm(v("D%d" % b, m, wd, 16), v("mI"), v("eB", 32 * k, 32 * k + wd // 16), m == 0, False)
-        if "c" in parts:
-            mm(v("D%d" % b, 0, wd), v("mNI"), v("cA", 512 * k, 512 * k + wd), False, True)
-        if "d" in parts:
-            act(v("AC", 512 * k, 512 * k + wd), v("D%d" % b, 0, wd), F.Abs)
-
-    def dS(t, b, parts):
-        for p in parts.replace("d", ""):
-            for j in range(4):
-                w, s = (v("mNI"), v("cS", 4 * b + j, 2048, 16)) if p == "c" else (v("mI"), v("Z%d" % (t + 1), 0, 128))
-                mm(v("D%d" % b, 128 * j, 128 * j + 128), w, s, p == "c" and j == 0, p == "e" and j == 3)
-        if "d" in parts:
-            act(v("AB", 512 * b, 512 * b + 512), v("D%d" % b), F.Abs)
-
-    def dV(m0, m1):
-        for m in range(m0, m1):
-            tt(v("AB", 2048 + 128 * m, 2176 + 128 * m), v("cS", 2048 + m, 4096, 16), v("TR", 0, 128), A.max)
-
-    def sums(h, m0, m1, raw=False, stop=False):
-        for m in range(m0, m1):
-            s = v("cS", 2048 + m, 4096, 16) if raw else v("AB", 2048 * h + 128 * m, 2048 * h + 128 * m + 128)
-            kb = 2 if raw else h
-            mm(v("KEY", 256 * h + m, 256 * h + 256, 16), s, v("KBS", 16 * kb, 16 * kb + 16), False, stop and m == m1 - 1)
-
-    def blocks(b0, b1, kind, stop=False):
-        for b in range(b0, b1):
-            z = 144 * kind + 15 - b
-            mm(v("KA", 0, 128), v("ZS", z, z + 128), v("cA" if kind == 2 else "AC", 128 * b, 128 * b + 128), False, stop and b == b1 - 1)
-
-    def succ(t):
-        vcopy(v("sU"), ind(v("SI", 0, 2048), v("aS%d" % t)))
-
-    def cells(t, part):
-        if part == 0 and t:
-            act(v("RH"), ind(v("HF", 0, 8192), v("aU")))
-        if part == 0 and not t:
-            ts(v("TI"), v("AR"), 1.0 / 128, A.mult, -0.49609375, A.add)
-            ts(v("HV"), v("TI"), pm, A.is_equal, 16.0, A.mult)
-            tt(v("RH", 0, 256), ind(v("V0"), v("vU")), v("HV"), A.mult)
-        if part == 1:
-            lists(v("ML", 0, 64 if t else 16), "ZE", "RH", 1024 if t else 256)
-        if part == 2:
-            if t:
-                scan(v("cb"), v("B4"), v("ML", 0, 64), A.add, A.max)
-            ts(ss, aF, 2.0, A.mult)
-            vcopy(mx, v("cb", 3, 64, 4) if t else v("ML", 0, 16))
+    def cells(t):
+        if t:
+            for r in range(4):
+                act(v("RH", 256 * r, 256 * r + 256), ind(v("HF", 2048 * r, 2048 * r + 2048), v("aS%d" % t)))
+            lists(v("KEY", 256, 320), "ZV", "RH", 1024)
+            mm(v("KEY", 320, 352), one_row, v("RB", 32 * t - 32, 32 * t, 1, 0, 1), True, False)
+            lists(v("KEY", 320, 352), "ZJ", "RH", 1024, c0=512)
+            vcopy(v("cb", 0, 32), v("KEY", 288, 320))
+            tt(v("cb", 32, 64), v("KEY", 256, 288), v("cb", 0, 32), A.max)
+            tt(mx, v("cb", 32, 48), v("cb", 48, 64), A.max)
             ts(fi, mx, 7, A.bitwise_and, 1, A.logical_shift_right)
             ts(hh, mx, 1, A.bitwise_and)
+            ts(fresh, mx, 32.0 * t + 16, A.is_ge, 8192.0, A.mult)
+            vcopy(j0, v("KEY", 320, 336))
+            tt(dj, v("KEY", 336, 352), j0, A.subtract)
+        else:
+            ts(q8, v("aI"), 127, A.bitwise_and)
+            vcopy(v("vU"), q8)
+            ts(v("TK"), v("AR"), 1.0 / 128, A.mult, -0.49609375, A.add)
+            ts(v("HV"), v("TK"), pm, A.is_equal, 16.0, A.mult)
+            tt(v("RH", 0, 256), ind(v("V0"), v("vU")), v("HV"), A.mult)
+            lists(v("KEY", 256, 272), "ZE", "RH", 256)
+            vcopy(mx, v("KEY", 256, 272))
+            ts(fi, mx, 1, A.logical_shift_right)
+            ts(hh, mx, 1, A.bitwise_and)
+        ts(ss, aF, 2.0, A.mult)
 
-    def compare(c0, c1):
-        for c in range(c0, c1):
+    def places():
+        for c in range(16):
             e = 272 * c
             ts(v("E", e, e + 256 - 16 * c), v("AR", 16 * c, 256), v("aF", c, c + 1), A.is_equal)
             if c < 15:
                 mm(v("TR", 16 * c + 16, 256, 1, 0, 8), v("G8", 0, 8), v("E", e + 16, e + 256 - 16 * c), c == 0, False)
             if c == 0:
                 mm(v("TR", 0, 16, 1, 0, 8), v("LTm", 0, 8), v("E", 0, 16), False, False)
+        for i in range(1, 16):
+            mm(v("TR", i, 256, 16, 0, 8), v("LTm", 8 * i, 8 * i + 8), v("E", i, 4096, 272), False, i == 15)
+        vcopy(v("RR", p1=8), v("TR", 0, 256, 1, 0, 8))
+        lists(kP, "ZK", "RR", 256, 8)
 
-    def places(part):
-        if part == 0:
-            for i in range(1, 16):
-                mm(v("TR", i, 256, 16, 0, 8), v("LTm", 8 * i, 8 * i + 8), v("E", i, 4096, 272), False, i == 15)
-        if part == 1:
-            vcopy(v("RR", p1=8), v("TR", 0, 256, 1, 0, 8))
-            lists(kP, "ZK", "RR", 256, 8)
-
-    def pops():
+    def pops(t):
         tt(v("blB"), kP, fi, A.is_ge)
         tt(nn, kP, fi, A.subtract)
-        tt(hq, kP, hh, A.not_equal)
-        scan(v("scB"), v("blB"), v("ZR16"), A.add, A.add)
-        ts(nn4, nn, 1.0, A.add, 4096.0, A.mult)
-        tt(sq, ss, hq, A.add)
         tt(hs, kP, hh, A.add)
-        ts(k3, kP, 3.0, A.min, 2048.0, A.mult)
+        if t:
+            tt(tk, kP, dj, A.mult)
+        scan(v("scB"), v("blB"), v("ZR16"), A.add, A.add)
         mm(ro, v("SG"), v("scB"), True, False)
         mm(ro, v("TRI"), v("blB"), False, True)
-        tt(segf, nn4, sq, A.max)
         ts(hk, hs, 1, A.bitwise_and)
-        ts(v("gU"), segf, 4096.0, A.min)
+        ts(nn4, nn, 1.0, A.add, 8192.0, A.mult)
+        tt(slot, ss, hk, A.add)
+        if t:
+            tt(tk, tk, j0, A.add)
+            tt(tk, tk, fresh, A.min)
+            tt(nn4, nn4, tk, A.max)
+        tt(segf, nn4, slot, A.max)
+        ts(v("gU"), segf, (4096.0, 4464.0, 4720.0)[t], A.min)
+        popped[:] = [len(calls) - 1]
+        if t < 2:
+            tt(pos, ro, v("LA", 32, 48), A.min)
+            ts(v("CL%d" % t), pos, 511.0, A.add)
+            popped[:] = [len(calls) - 1]
+            send(1 + t, v("CL%d" % t), "QL%d" % t, "r_l%d" % t)
 
-    def move(t, part):
-        if part == 0:
-            tt(v("zt"), ind(v("G", 0, 4112), v("gU")), v("Z%d" % t), A.add)
-            ts(v("Z%d" % (t + 1)), v("zt"), 0.0, A.max, 255.0, A.min)
-        if part == 1:
-            ts(v("TR", 0, 128), v("zt", 128, 256), 0.0, A.max, 255.0, A.min)
+    def decide(t):
+        ts(ask2, ro, -399.0, A.is_lt, 2.0, A.mult)
+        ts(x2, nn, 2.0, A.mult, 4.0, A.add)
+        tt(code, x2, hk, A.add)
+        ts(v("vU"), code, 7.0, A.min)
+        act(v("HV"), ind(v("VT", 16 * t, 16 * t + 8), v("vU")), scale=low if t < 2 else 1.0)
+        if t == 0:
+            ts(q8, ro, 1.0 / 7, A.mult, 508.0 / 7, A.add)
+            ts(t2, q8, -6.9375, A.mult, 511.0, A.add)
+            tt(t3, ro, t2, A.add)
+            ts(v("jU", 0, 16), t3, 16.0, A.mult, 111.0, A.min)
+            act(v("HW"), ind(v("JL"), v("jU", 0, 16)), scale=high)
+        if t == 1:
+            ts(v("jU", 16, 32), pos, 511.0, A.add, 111.0, A.min)
+            act(v("HW"), ind(v("JT"), v("jU", 16, 32)), scale=high)
+        tt(nw, nn, ask2, A.is_ge)
+        ts(k3, x2, 6.0, A.min, 1024.0, A.mult)
+        tt(base, k3, aF, A.add)
+        if t == 0:
+            ts(popf, nn, 0.0, A.is_lt)
+            tt(nput, nw, popf, A.max)
+        a, b, c = (two, own, 0) if t == 0 else (nw, base, 16)
+        tt(a, a, v("LA", c, 32), A.mult)
+        tt(a, a, b, A.max)
+        vcopy(v("nU", 32 * t + c, 32 * t + 32), a)
+        cell = ind(v("HF"), v("nU", 32 * t + 16, 32 * t + 32))
+        tt(cell, v("HV"), v("HW"), A.add) if t < 2 else vcopy(cell, v("HV"))
 
-    def post(t):
-        tt(pos, ro, v("LA", 32, 48), A.min)
-        ts(v("CL%d" % t), pos, 511.0, A.add)
-        send(rank + 1 + t, v("CL%d" % t), "QL%d" % t, "r_l%d" % t)
+    def refill():
+        act(v("LX"), ind(v("G", 4352, 4464), v("jU", 0, 16)))
+        vcopy(ind(v("G", 0, 4352), v("nU", 0, 16)), v("LX"))
 
-    def payload():
+    def move(t):
+        tt(v("zt"), ind(v("G", 0, (4112, 4480, 4736)[t]), v("gU")), v("Z%d" % t), A.add)
+        ts(v("Z%d" % (t + 1)), v("zt"), 0.0, A.max, 255.0, A.min)
+        for e in range(2):
+            mm(v("TR", e, 256, 2), v("mI"), v("Z%d" % (t + 1), 128, 256), True, True)
+
+    def centres(t, engines):
+        vcopy(v("sU"), ind(v("SI", 0, 2048), v("aS%d" % t)))
+        gather(engines, "cS", v("X"), "sU")
+        for b in range(4):
+            for j in range(4):
+                mm(v("D%d" % b, 128 * j, 128 * j + 128), v("mNI"), v("cS", 4 * b + j, 2048, 16), j == 0, False)
+
+    def keys():
         ts(t1, v("blB"), 2048.0, A.mult)
         tt(t1, t1, aF, A.add)
         vcopy(v("pU"), t1)
         vcopy(v("s16"), ind(v("SI"), v("pU")))
         ts(v("hB"), v("s16"), 1.0 / 48, A.mult, 128.0, A.add)
-
-    def keys(start=False):
         for h in range(2):
             s = (128 * h, 128 * h + 128)
-            mm(v("KEY", 256 * h, 256 * h + 128), v("hB", *s), v("mI"), start and h == 0, False)
+            mm(v("KEY", 256 * h, 256 * h + 128), v("hB", *s), v("mI"), h == 0, False)
             mm(v("KEY", 256 * h + 128, 256 * h + 256), v("hB", *s), v("m48"), False, False)
             mm(v("KEY", 256 * h + 128, 256 * h + 256), v("s16", *s), v("mIh"), False, False)
+        for m in range(16):
+            mm(v("KEY", 256 + m, 512, 16), v("cS", 2048 + m, 4096, 16), v("KBS", 32, 48), False, False)
 
-    def decide(t, part):
-        if part == 0:
-            ts(ask2, ro, -399.0, A.is_lt, 2.0, A.mult)
-            ts(e0, nn, 0.0, A.is_equal)
-            ts(u1, nn, 10.0, A.mult, 32.0 * t + 50.0, A.add)
-            ts(u2, nn, 6.0, A.mult, 32.0 * t + 46.0, A.add)
-            tt(hp, e0, hk, A.is_equal)
-            tt(nw, nn, ask2, A.is_ge)
-            tt(v1, u1, u2, A.max)
-            ts(popf, nn, 0.0, A.is_lt)
-            tt(slot, ss, hk, A.add)
-            tt(v2, v1, hp, A.add)
-            tt(nput, nw, popf, A.max)
-            tt(base, k3, aF, A.add)
-            ts(v("vU"), v2, 255.0, A.min)
-            tt(two, two, v("LA", 0, 32), A.mult)
-        if part == 1:
-            act(v("HV"), ind(v("JL"), v("vU")))
-        if part == 2:
-            if t < 2:
-                ts(q8, ro, 0.125, A.mult, 63.4375, A.add)
-            tt(two, two, own, A.max)
-            if t < 2:
-                ts(t2, q8, -7.9375, A.mult, 511.0, A.add)
-            vcopy(v("nU"), two)
-            if t < 2:
-                tt(t3, ro, t2, A.add)
-                ts(v("jU"), t3, 16.0, A.mult, 127.0, A.min)
-        if part == 3:
-            vcopy(ind(v("HF"), v("nU", 16, 32)), v("HV"))
-
-    def refill(t, part):
-        if part == 0:
-            act(v("LX"), ind(v("LN%d" % t), v("jU")))
-        if part == 1:
-            vcopy(ind(v("G"), v("nU", 0, 16)), v("LX"))
-
-    def question(t, part):
-        a, b, qz = v("TI"), v("TJ"), v("QZ%d" % t)
-        if part == "x":
-            mm(v("KA", 0, 256), v("WX"), qz, True, True)
-        if part == "u":
-            vcopy(a, v("KA", 0, 256))
-            ts(b, a, 4095, A.bitwise_and)
-            ts(v("Y1"), b, ycol, A.add)
-        if part == "sq":
-            act(v("Y2"), v("Y1"), F.Square)
-        if part == "slot":
-            ts(a, v("Y2"), 0.03125, A.mult, rcol, A.add)
-            ts(b, a, 4095, A.bitwise_and)
-        if part == "goal":
-            act(v("goal"), ind(v("X"), v("QA%d" % t)))
-        if part == "e":
-            mm(v("KA", 256, 512), v("mE", 0, 128), v("goal"), True, False)
-            mm(v("KA", 256, 512), v("mE", 128, 256), qz, False, True)
-        if part == "pack":
-            tt(v("PK"), b, v("KA", 256, 512), A.add)
-        if part == "pick":
-            vcopy(ind(v("CW"), v("QL%d" % t)), v("PK"))
-            ts(v("TI", 0, 112), v("CW", 0, 112), 4095, A.bitwise_and)
-            ts(v("TJ", 0, 112), v("CW", 0, 112), 12, A.arith_shift_right)
-            vcopy(v("CC"), v("TI", 0, 112))
-            ts(v("eB"), v("TJ", 0, 112), -16.0, A.max, 16.0, A.min)
-        if part == "clip":
-            ts(v("D3", 64, 112), v("TJ", 64, 112), -16.0, A.max, 16.0, A.min)
-        if part == 4:
-            mm(v("KA", 0, 128), one_row, v("JL", 0, 128, 1, 0, 1), True, False)
-            mm(v("KA", 0, 128), v("BR", p1=1), one_row, False, False)
-        if part == 5:
-            scan(v("KT"), v("BQ"), v("KA", 0, 128), A.add, A.min)
-            vcopy(v("KQ", 0, 8), v("KT", 15, 128, 16))
-            ts(v("KQ", 16, 24), v("KQ", 0, 8), 2047, A.bitwise_and)
-            vcopy(v("qU"), v("KQ", 16, 24))
-        if part == 6:
-            vcopy(v("AN%d" % t), ind(v("cA"), v("qU")))
-            send(rank - 1 - t, v("AN%d" % t), "LN%d" % t, "r_n%d" % t)
-
-    def least(t, part):
-        if part == 0:
-            scan(v("KS"), v("BM"), v("KEY"), A.add, A.min)
-            tt(v("KI", 0, 32), v("KS", 15, 512, 16), v("CK"), A.add)
-            ts(v("KI", 32, 64), v("KI", 0, 32), 63, A.bitwise_and)
-            vcopy(v("PB"), v("KI", 32, 64))
-            for h in range(2):
-                o = v("TR", 128 * h, 128 * h + 128, 1, 0, 8)
-                mm(o, v("PB", 16 * h, 16 * h + 8), v("m48"), True, False)
-                mm(o, v("PB", 16 * h + 8, 16 * h + 16), v("mNI"), False, True)
-        if part == 1:
-            ts(v("YA" if t == 2 else "T16", p1=8), v("TR", 0, 256, 1, 0, 8), -1.0, A.mult, -32.0, A.add)
-            if t < 2:
-                mm(v("D2", 0, 256), v("RP", p1=8), v("T16", p1=8), True, True)
-                lists(aP, "ZA", "T16", 256, 8)
-        if part == 2:
-            vcopy(v("AR"), v("D2", 0, 256))
-        if part == 3:
-            for r in range(4):
-                ts(v("aU", r, 64, 4), aP, 2048.0 * r, A.add)
+    def search(t):
+        for m in range(16):
+            b, j = m // 4, m % 4
+            mm(v("D%d" % b, 128 * j, 128 * j + 128), v("mI"), v("Z%d" % (t + 1), 0, 128), False, j == 3)
+            if j == 3:
+                act(v("AB", 512 * b, 512 * b + 512), v("D%d" % b), F.Abs)
+        for m in range(8):
+            tt(v("AB", 2048 + 256 * m, 2304 + 256 * m), v("cS", 2048 + m, 4096, 8), v("TR", 0, 256), A.max)
+        for b in range(4):
+            for m in (2 * b, 2 * b + 8, 2 * b + 1, 2 * b + 9):
+                c = 2048 + 256 * (m % 8)
+                mm(v("KEY", 256 + m, 512, 16), v("AB", c + m // 8, c + 256, 2), v("KBS", 16, 32), False, False)
+            for m in range(4 * b, 4 * b + 4):
+                mm(v("KEY", m, 256, 16), v("AB", 128 * m, 128 * m + 128), v("KBS", 0, 16), False, m == 15)
+        scan(v("KS"), v("BM"), v("KEY"), A.add, A.min)
+        tt(v("KI", 0, 32), v("KS", 15, 512, 16), v("CK"), A.add)
+        ts(v("KI", 32, 64), v("KI", 0, 32), 63, A.bitwise_and)
+        vcopy(v("PB"), v("KI", 32, 64))
+        for h in range(2):
+            o = v("TR", 128 * h, 128 * h + 128, 1, 0, 8)
+            mm(o, v("PB", 16 * h, 16 * h + 8), v("m48"), True, False)
+            mm(o, v("PB", 16 * h + 8, 16 * h + 16), v("mNI"), False, True)
+        ts(v("YA" if t == 2 else "T16", p1=8), v("TR", 0, 256, 1, 0, 8), -1.0, A.mult, -32.0, A.add)
+        if t < 2:
+            mm(v("KEY", 0, 256), v("RP", p1=8), v("T16", p1=8), True, True)
+            lists(aP, "ZA", "T16", 256, 8)
+            vcopy(v("AR"), v("KEY", 0, 256))
             vcopy(aF, aP)
             vcopy(v("aS%d" % (t + 1)), aP)
 
-    constants(0)
+    def question(t):
+        a, b, qz = v("TI"), v("TJ"), v("QZ1" if t else "Z0")
+        mm(v("KA", 0, 256), v("WX"), qz, True, True)
+        act(v("xq"), v("KA", 0, 256), F.Identity, 1.0 / 4096, half)
+        mm(v("KA", 0, 256), v("WX"), qz, True, False)
+        mm(v("KA", 0, 256), v("mE", 128, 256), v("xq"), False, True)
+        act(v("Y2"), v("KA", 0, 256), F.Square, bias=ycol)
+        ts(a, v("Y2"), 0.03125, A.mult, rcol, A.add)
+        ts(b, a, 4095, A.bitwise_and)
+        if t:
+            act(v("goal"), ind(v("X"), v("QA1")))
+            mm(v("KA", 256, 512), v("mE", 0, 128), v("goal"), True, False)
+        mm(v("KA", 256, 512), v("mE", 128, 256), qz, not t, True)
+        tt(v("PK"), b, v("KA", 256, 512), A.add)
+
+    def pick(t):
+        vcopy(ind(v("CW"), v("QL1" if t else "CL0")), v("PK"))
+        ts(v("TI", 0, 112), v("CW", 0, 112), 4095, A.bitwise_and)
+        vcopy(v("CC" if t else "CS"), v("TI", 0, 112))
+        ts(v("TJ", 0, 112), v("CW", 0, 112), 12, A.arith_shift_right)
+        if t:
+            ts(v("eB"), v("TJ", 0, 112), -16.0, A.max, 16.0, A.min)
+        else:
+            send(1, v("CS"), "QC", "r_c0")
+            slots = len(calls) - 2
+            vcopy(v("ZC"), v("TJ", 0, 112))
+            send(1, v("ZC"), "QZ0", "r_z0")
+            calls[-2]["preds"][slots] = "order"
+
+    def answer(t):
+        e = v("KA", 256, 384, 1, 0, 112)
+        if t:
+            pick(t)
+            mm(e, v("eB"), v("mI"), True, True)
+            act(v("eT", p1=112), e)
+        else:
+            act(v("goal"), ind(v("X"), v("QA0")))
+            vcopy(ind(v("GW"), v("QL0")), v("goal"))
+            mm(e, v("GW", 0, 112), v("mI"), True, False)
+            mm(e, v("QZ0"), v("mI"), False, True)
+            ts(v("eT", p1=112), e, -16.0, A.max, 16.0, A.min)
+        gather("VSSS", "cA", v("G", 0, 4096), "CC" if t else "QC")
+        mm(v("KA", 0, 112), one_row, v("JL", 0, 112, 1, 0, 1), True, False)
+        mm(v("KA", 0, 112), v("BR", p1=1), v("ONE", 0, 112, 1, 0, 1), False, False)
+        for k in range(4):
+            wd = min(512, 1792 - 512 * k)
+            r = (32 * k, 32 * k + wd // 16)
+            mm(v("D%d" % k, 0, wd), v("eT", 0, 128, 1, *r), v("REP", 0, wd, 1, *r), True, False)
+            mm(v("D%d" % k, 0, wd), v("mNI"), v("cA", 512 * k, 512 * k + wd), False, True)
+            act(v("AC", 512 * k, 512 * k + wd), v("D%d" % k, 0, wd), F.Abs)
+        for b in range(16):
+            mm(v("KA", 0, 112), v("ZS", 15 - b, 143 - b), v("AC", 112 * b, 112 * b + 112), False, b == 15)
+        scan(v("KT"), v("BQ"), v("KA", 0, 112), A.add, A.min)
+        vcopy(v("KQ", 0, 7), v("KT", 15, 112, 16))
+        ts(v("KQ", 16, 23), v("KQ", 0, 7), 2047, A.bitwise_and)
+        vcopy(v("qU", 0, 7), v("KQ", 16, 23))
+        vcopy(v("AN%d" % t), ind(v("cA"), v("qU", 0, 7)))
+        send(-1 - t, v("AN%d" % t), v("G", 4352 + 256 * t, 4464 + 256 * t), "r_n%d" % t)
+
     start()
-    send(rank + 1, v("Z0"), "QZ0", "r_z0")
-    send(rank + 1, v("aS0"), "QA0", "r_a0")
-    constants(7)
-    compare(0, 16)
-    places(0)
-    mix((constants, 2), (cells, 0, 0))
-    for b in range(4):
-        table(b)
-    places(1)
-    cells(0, 1)
-    constants(4)
-    succ(0)
-    cells(0, 2)
-    centres("S", 0, 2048)
-    pops()
-    post(0)
-    constants(3)
-    constants(8)
-    mix((constants, 5), (payload,), (decide, 0, 0))
-    question(0, "x")
-    for b in range(4):
-        dS(0, b, "c")
-    centres("S", 2048, 3072)
-    question(0, "goal")
-    move(0, 0)
-    send(rank + 2, v("Z1"), "QZ1", "r_z1")
-    mix((question, 0, "u"), (decide, 0, 2), (move, 0, 1))
-    question(0, "sq")
-    centres("S", 3072, 4096)
-    keys(True)
-    question(0, "e")
-    for b in range(4):
-        dS(0, b, "ed")
-    mix((question, 0, "slot"), (constants, 6))
-    question(0, "pack")
-    question(0, "pick")
-    sums(1, 0, 16, raw=True)
-    cands("S", 0, 1024)
-    dV(0, 16)
-    sums(0, 0, 16)
-    sums(1, 0, 16, stop=True)
-    decide(0, 1)
-    cands("S", 1024, 1792)
-    question(0, 4)
-    dB(0, 0, "ec")
-    least(0, 0)
-    dB(1, 1, "ec")
-    dB(0, 0, "d")
-    dB(1, 1, "d")
-    decide(0, 3)
-    dB(2, 3, "ecd")
-    least(0, 1)
-    dB(3, 0, "ecd")
-    least(0, 2)
-    blocks(0, 14, 0, stop=True)
-    least(0, 3)
-    cells(1, 0)
-    compare(0, 16)
-    mix((question, 0, 5), (succ, 1))
-    question(0, 6)
-    send(rank + 2, v("aS1"), "QA1", "r_a1")
-    centres("S", 0, 1024)
-    places(0)
-    question(1, "x")
-    places(1)
-    cells(1, 1)
-    centres("S", 1024, 2048)
-    question(1, "u")
-    question(1, "sq")
-    cells(1, 2)
-    pops()
-    post(1)
-    centres("S", 2048, 3072)
-    refill(0, 0)
-    question(1, "goal")
-    for b in range(4):
-        dS(1, b, "c")
-    mix((question, 1, "slot"), (payload,), (decide, 1, 0))
-    refill(0, 1)
-    move(1, 0)
-    centres("S", 3072, 4096)
-    question(1, "e")
-    move(1, 1)
-    for b in range(4):
-        dS(1, b, "ed")
-    keys(True)
-    question(1, "pack")
-    sums(1, 0, 16, raw=True)
-    dV(0, 8)
-    question(1, "pick")
-    decide(1, 1)
-    cands("S", 0, 1024)
-    dV(8, 16)
-    sums(0, 0, 16)
-    sums(1, 0, 16, stop=True)
-    question(1, 4)
-    cands("S", 1024, 1792)
-    dB(0, 0, "ec")
-    mix((least, 1, 0), (decide, 1, 2))
-    dB(1, 1, "ec")
-    dB(0, 0, "d")
-    dB(1, 1, "d")
-    decide(1, 3)
-    dB(2, 3, "ecd")
-    least(1, 1)
-    dB(3, 0, "ecd")
-    least(1, 2)
-    blocks(0, 14, 0, stop=True)
-    least(1, 3)
-    cells(2, 0)
-    compare(0, 16)
-    mix((question, 1, 5), (succ, 2))
-    question(1, 6)
-    centres("S", 0, 1024)
-    places(0)
-    places(1)
-    cells(2, 1)
-    centres("S", 1024, 2048)
-    centres("V", 3584, 4096)
-    cells(2, 2)
-    pops()
-    centres("S", 2048, 3072)
-    for b in range(4):
-        dS(2, b, "c")
-    mix((decide, 2, 0), (payload,))
-    refill(1, 0)
-    decide(2, 1)
-    centres("S", 3072, 3584)
-    keys(True)
-    refill(1, 1)
-    move(2, 0)
-    store("Y", T.yz[:, :], v("Z3"), "o_z")
-    mix((move, 2, 1), (decide, 2, 2))
-    for b in range(4):
-        dS(2, b, "ed")
-    sums(1, 0, 16, raw=True)
-    decide(2, 3)
+    for t in range(STEPS):
+        cells(t)
+        places()
+        pops(t)
+        if t == 0:
+            question(0)
+            pick(0)
+            ranks = len(calls) - 2
+            for k in range(1024, 2048, 512):
+                iota(v("SI", 2048 + k, 2560 + k), [[1, 512]], k)
+                calls[-1]["preds"][ranks] = "order"
+            for k in range(7168, 8448, 640):
+                iota(v("HF", k, k + 640), [[0, 640]])
+                calls[-1]["preds"][ranks] = "order"
+            for k in range(2):
+                iota(v("JR", 256 * k, 256 * k + 256), [[1, 16], [0, 16]], 16 * k)
+                calls[-1]["preds"][ranks] = "order"
+            iota(v("JT"), [[1, 16], [16, 7]])
+            calls[-1]["preds"][ranks] = "order"
+            iota(v("RB", p1=1), [[256, 2], [0, 32]], 4352)
+            calls[-1]["preds"][ranks] = "order"
+            ts(v("REP"), v("JR"), p31, A.is_equal)
+        decide(t)
+        centres(t, "SSSSSSSV" if t else "SSSSSSVV")
+        keys()
+        if t == 1:
+            question(t)
+        move(t)
+        if t == 1:
+            refill()
+        if t == 0:
+            send(2, v("Z1"), "QZ1", "r_z1")
+        search(t)
+        if t == 0:
+            send(2, v("aS1"), "QA1", "r_a1")
+        if t < 2:
+            answer(t)
+    move_dma("Y", T.yz[:, :], T.Z3[:, :], v("Z3"), "o_z")
+    move_dma("S", T.ya[:, :], T.YA[0:8, :], v("YA"), "o_a")
     for r in range(4):
-        o = v("SA", 128 * r, 128 * r + 128)
-        deps("Y", [o], [v("HF")])
-        load("Y", o, T.HF[0:128:16, 2048 * r:2048 * r + 2048], "l_p%d" % r)
-    dV(0, 16)
-    sums(0, 0, 16)
-    sums(1, 0, 16, stop=True)
-    least(2, 0)
+        move_dma("Y", v("SA", 128 * r, 128 * r + 128), T.HF[0:128:16, 2048 * r:2048 * r + 2048], v("HF"), "l_p%d" % r)
     tt(v("W2"), v("SA", 0, 256), v("SA", 256, 512), A.max)
-    least(2, 1)
-    store("S", T.ya[:, :], v("YA", p1=8), "o_a")
     tt(v("TI", 0, 128), v("W2", 0, 128), v("W2", 128, 256), A.max)
     ts(v("TJ", 0, 128), v("TI", 0, 128), 7, A.bitwise_and, 1, A.logical_shift_right)
-    ts(v("TK"), v("TI", 0, 128), 1, A.bitwise_and)
+    ts(v("TK", 0, 128), v("TI", 0, 128), 1, A.bitwise_and)
     vcopy(v("YF"), v("TJ", 0, 128))
-    vcopy(v("YH"), v("TK"))
-    store("Y", T.yf[:, :], v("YF"), "o_f")
-    store("S", T.yh[:, :], v("YH"), "o_h")
+    vcopy(v("YH"), v("TK", 0, 128))
+    move_dma("Y", T.yf[:, :], T.YF[:, :], v("YF"), "o_f")
+    move_dma("S", T.yh[:, :], T.YH[:, :], v("YH"), "o_h")
+
+    if not ORDER:
+        ORDER.extend(issue_order(calls))
+    cnt = {"V": 0, "S": 0, "P": 0, "G": 0}
+    known = {q: {} for q in H}
+    done = {}
+    for i in ORDER:
+        c = calls[i]
+        q = c["q"]
+        if q == "R":
+            done[i] = (c["sem"], c["inc"], {})
+            continue
+        for sem, val, kn in sorted((done[p] for p, kind in c["preds"].items() if kind == "wait"), key=lambda r: -r[1]):
+            if known[q].get(sem, 0) < val:
+                H[q].wait_ge(T.sem[sem], val)
+                for s, x in list(kn.items()) + [(sem, val)]:
+                    known[q][s] = max(known[q].get(s, 0), x)
+        call = c["run"]()
+        if c["sem"] is None:
+            cnt[q] += 1
+            call.then_inc(T.sem["e" + q], 1)
+            done[i] = ("e" + q, cnt[q], dict(known[q]))
+        elif c["inc"]:
+            call.then_inc(T.sem[c["sem"]], c["inc"])
+            done[i] = (c["sem"], c["inc"], {})
     g.wait_ge(T.sem.sent, sent[0])
     for s, x in [("e" + q, cnt[q]) for q in cnt] + final:
         if known["G"].get(s, 0) < x:

@@ -7,32 +7,38 @@ def _b(n, c, d="bfloat16", w="sbuf", p=128):
     SCRATCH[n] = (w, [p, c], d)
 
 
-for _n, _c in (("X", 2048), ("G", 4736), ("HF", 8448), ("cS", 4096), ("AB", 4096), ("cA", 1792), ("AC", 1792), ("E", 4096),
-               ("mI", 128), ("mNI", 128), ("m48", 128), ("mE", 256), ("SG", 128), ("G8", 128), ("LTm", 128), ("ZE", 144), ("ZK", 144),
-               ("NG", 128), ("ZS", 144), ("eB", 112), ("eT", 128), ("JR", 512), ("REP", 512), ("xq", 256), ("TRI", 128), ("WX", 128), ("KBS", 48), ("ONE", 128), ("JG", 128),
-               ("J8", 128), ("BR", 128), ("JL", 256), ("BM", 512), ("BQ", 112), ("V0", 128), ("RR", 256), ("RH", 1024),
-               ("blB", 16), ("scB", 16), ("hB", 256), ("zt", 256), ("goal", 256), ("PB", 32), ("HV", 256), ("LX", 256), ("SA", 512),
-               ("Z0", 256), ("Z1", 256), ("Z2", 256), ("Z3", 256), ("AN0", 112), ("AN1", 112), ("ZV", 144), ("ZJ", 144), ("Z8", 144), ("HW", 256), ("VT", 48), ("JT", 112), ("RB", 64),
-               ("QZ0", 112), ("QZ1", 256), ("ZC", 112), ("GW", 512)):
+for _n, _c in (("X", 2048), ("G", 4608), ("HF", 9216), ("cS", 4096), ("AB", 4096), ("cA", 1792), ("AC", 1792), ("E", 4096),
+               ("mI", 128), ("mNI", 128), ("m48", 128), ("p48", 128), ("R960", 256), ("SG", 128), ("SGs", 128), ("G8", 16), ("LT", 128),
+               ("ZS", 144), ("ZS2", 144), ("ZSn", 144), ("eB", 112), ("eT", 128), ("JR", 512), ("REP", 512), ("xq", 256), ("TRI", 128), ("WX", 128), ("KBS", 48),
+               ("ONE", 128), ("JG", 128), ("J8", 16), ("BR", 128), ("JL", 256), ("BM", 512), ("BQ", 128), ("V0", 128), ("RH", 1024),
+               ("blZ", 16), ("scB", 16), ("hB", 256), ("zt", 256), ("goal", 256), ("PB", 32), ("HV", 256), ("LX", 256), ("SA", 512),
+               ("Z0", 256), ("Z1", 256), ("Z2", 256), ("Z3", 256), ("AN0", 112), ("AN1", 112), ("ZV", 144), ("ZJ0", 144), ("ZJ1", 144),
+               ("Z8", 144), ("HW", 256), ("VT", 32), ("JT", 112), ("QZ0", 112), ("QZ1", 256), ("ZC", 112), ("CW", 512), ("PD", 256)):
     _b(_n, _c)
-for _n, _c in (("mIh", 128), ("RP", 128), ("s16", 256), ("T16", 256), ("ZA", 144)):
+for _n, _c in (("mIh", 128), ("RP", 128), ("s16", 256), ("T16", 256), ("ZA", 144), ("I2", 128), ("Iq", 128), ("mQ", 128), ("a16", 48)):
     _b(_n, _c, "float16")
-for _n, _c in (("COL", 128), ("JF", 2048), ("LA", 48), ("W1", 128), ("W2", 256), ("ZR16", 16), ("LL", 512), ("KS", 512), ("KT", 112),
-               ("aF", 16), ("Y2", 256), ("YA", 256), ("YH", 128), ("YF", 128), ("CK", 32), ("cb", 64)):
+for _n, _c in (("COL", 128), ("LA", 64), ("W1", 128), ("W2", 256), ("ZR16", 16), ("LL", 320), ("KS", 512), ("KT", 112),
+               ("aF", 16), ("Y2", 256), ("YA", 256), ("YH", 128), ("YF", 128), ("cb", 192), ("KI", 32), ("KL", 368),
+               ("OH", 16), ("YK", 256)):
     _b(_n, _c, "float32")
-for _n, _c in (("SI", 4096), ("FI", 128), ("HI", 128), ("aI", 16), ("CI", 8), ("LI", 256), ("PK", 256), ("CW", 512),
-               ("TI", 256), ("TJ", 256), ("TK", 256), ("KI", 64), ("KQ", 32)):
+for _n, _c in (("SI", 2048), ("FI", 128), ("HI", 128), ("aI", 16), ("CI", 8), ("LI", 128), ("MX", 48), ("TI", 256), ("TJ", 256), ("KQ", 32)):
     _b(_n, _c, "int32")
-for _n, _c in (("aS0", 16), ("aS1", 16), ("aS2", 16), ("AR", 256), ("sU", 256), ("gU", 16), ("nU", 96), ("pU", 16), ("vU", 16),
-               ("jU", 32), ("qU", 8), ("CC", 112), ("CS", 112), ("QC", 112), ("CL0", 16), ("CL1", 16), ("QL0", 16), ("QL1", 16), ("QA0", 16), ("QA1", 16)):
+for _n, _c in (("aS0", 16), ("aS1", 16), ("aS2", 16), ("AR", 256), ("sU", 256), ("gU", 16), ("nU", 64), ("vU", 16), ("cU", 32),
+               ("jU", 32), ("qU", 8), ("CL", 16), ("CS", 120), ("QC", 120), ("CC", 112), ("LC1", 8), ("QL1", 8), ("QA0", 16), ("QA1", 16)):
     _b(_n, _c, "uint16")
-for _n in ("D0", "D1", "D2", "D3", "KEY", "ML", "TR", "KA"):
-    _b(_n, 512, "float32", "psum")
-SEMAPHORES = ["eV", "eS", "eP", "eG", "sent", "l_a", "l_z", "l_h", "l_f", "l_s", "l_x", "l_g", "l_p0", "l_p1", "l_p2", "l_p3", "l_00", "l_03",
-              "o_z", "o_a", "o_h", "o_f", "r_c0", "r_z0", "r_z1", "r_l0", "r_l1", "r_a0", "r_a1", "r_n0", "r_n1"]
-STEPS = 3
+for _n, _c in (("D0", 1024), ("D1", 1024), ("KEY", 512), ("ML", 512), ("TR", 512), ("KA", 512)):
+    _b(_n, _c, "float32", "psum")
+SEMAPHORES = ["eV", "eS", "eP", "eG", "sent", "l_a", "l_z", "l_h", "l_f", "l_s", "l_x", "l_g", "l_p0", "l_p1", "l_p2", "l_p3", "l_00", "l_01", "l_03",
+              "o_z", "o_a", "o_h", "o_f", "r_c0", "r_c1", "r_z0", "r_z1", "r_a0", "r_a1", "r_n0", "r_n1"]
+STEPS, BASE = 3, 880.21875
+ZERO = 2304
+FILLS = [("V", 2304, 3328), ("S", 0, 1024), ("S", 1024, 2048), ("S", 3328, 4352), ("V", 4608, 5632), ("V", 5632, 6656), ("G", 6912, 7552),
+         ("G", 7552, 8192), ("G", 8192, 8960)]
+CENTRES = [[("S", 1024), ("S", 1024), ("S", 512), ("V", 512), ("V", 512), ("V", 512)]] + [[("S", 1024)] * 4, [("S", 1024)] * 3 + [("S", 512), ("V", 512)]]
+CANDS = [[("S", 1024), ("S", 768)], [("V", 512), ("V", 384), ("S", 384), ("S", 512)]]
+MAXED = [0, 8]
 CYCLE, PE_CYCLE, GATHER, SCATTER = 0.00083, 0.00045, 1.56, 3.8
-SAME, CROSS, DMA, LOAD_RATE, ISSUE, FIRST, REMOTE, LINK_RATE = 0.06, 0.19, 2.3, 290e3, 0.8, 4.0, 3.0, 35e3
+SAME, CROSS, DMA, LOAD_RATE, ISSUE, FIRST, REMOTE, LINK_RATE = 0.06, 0.26, 1.5, 380e3, 0.7, 4.0, 1.8, 60e3
 BYTES = {"bfloat16": 2, "float16": 2, "uint16": 2, "float32": 4, "int32": 4}
 CASES = [{"": 1.0, "send": s, "load": d, "first": f, "wake": w, "plain": p, "gather": p * g, "scatter": p * c, "call": a}
          for s, d, f, w, p, g, c, a in ((1.0, 1.0, 1.0, 1.0, 1.0, 1.0, 1.0, 0.0), (0.8, 1.15, 1.5, 1.2, 1.0, 1.2, 0.7, 0.02),
@@ -101,7 +107,6 @@ def issue_order(calls):
     rest = [0.0] * n
     for i in range(n - 1, -1, -1):
         rest[i] = max([calls[i]["late"]] + [d + calls[j]["cost"] + rest[j] for j, d in after[i]])
-    rest = [s + c["urge"] for s, c in zip(rest, calls)]
     runs = {}
     for i, c in enumerate(calls):
         runs.setdefault((c["q"], c["piece"]), []).append(i)
@@ -122,7 +127,7 @@ def issue_order(calls):
                     r[i] += (x >> 20) % 25 / 8.0 - 1.5
         order, start = one_pass(calls, after, [0.0] * n, r)
         if k % 3 == 1:
-            r = [s + c["urge"] for s, c in zip(one_pass(calls, before, [c["late"] for c in calls], start)[1], calls)]
+            r = one_pass(calls, before, [c["late"] for c in calls], start)[1]
             order = one_pass(calls, after, [0.0] * n, r)[0]
         t = sum(length(calls, waits, order, case) / case["plain"] for case in CASES) / len(CASES)
         if t < now + 0.03:
@@ -162,7 +167,7 @@ def rank_program(g, core, T, topo):
     def meet(e, x):
         return e[1] < x[2] and x[1] < e[2] and not (e[3] == x[3] > 1 and (e[1] - x[1]) % x[3])
 
-    calls, wr, rd, bank_use, piece, urge = [], {}, {}, {}, [0], [0.0]
+    calls, wr, rd, bank_use, piece = [], {}, {}, {}, [0]
 
     def note(q, run, cost, out, ins, sem=None, inc=1, late=0.0, kind="", first=0.0):
         rs, flat = [], [x for x in ins if isinstance(x, tuple)]
@@ -174,13 +179,12 @@ def rank_program(g, core, T, topo):
         me, preds = len(calls), {}
         for x in ws + rs:
             if SCRATCH[x[0]][0] == "psum":
-                use = bank_use.setdefault(x[0], {})
-                for k, p in use.items():
-                    if p != me and preds.get(p) != "wait":
-                        preds[p] = "order" if k == q else "wait"
-                use[q] = me
-                if q == "V" and x in ws:
-                    use["written"] = me
+                for bank in range(x[1] // 512, (x[2] - 1) // 512 + 1):
+                    use = bank_use.setdefault((x[0], bank), {})
+                    for k, p in use.items():
+                        if p != me and preds.get(p) != "wait":
+                            preds[p] = "order" if k == q else "wait"
+                    use[q] = me
                 continue
             for e, p in wr.get(x[0], []) + (rd.get(x[0], []) if x in ws else []):
                 if meet(e, x):
@@ -197,7 +201,7 @@ def rank_program(g, core, T, topo):
         if not calls or calls[-1]["out"] != (ws[0][0] if ws else None):
             piece[0] += 1
         work = "" if run is None or sem else "scatter" if out[0] == "ind" else "gather" if len(rs) > len(flat) else "plain"
-        calls.append({"q": q, "run": run, "work": work, "urge": urge[0], "cost": cost, "late": late, "preds": preds, "sem": sem, "kind": kind, "first": first,
+        calls.append({"q": q, "run": run, "work": work, "cost": cost, "late": late, "preds": preds, "sem": sem, "kind": kind, "first": first,
                       "out": ws[0][0] if ws else None, "piece": piece[0] // 4, "inc": inc})
         return me
 
@@ -235,14 +239,14 @@ def rank_program(g, core, T, topo):
 
     def mm(out, lhsT, rhs, start, stop):
         note("P", lambda: g.tensor.matmul(ap(out), ap(lhsT), ap(rhs), start, stop),
-             0.005 + PE_CYCLE * max(min(64, width(lhsT)), width(rhs)), out, (lhsT, rhs))
+             0.005 + PE_CYCLE * max(min(64, width(lhsT)), width(rhs)) * BYTES[SCRATCH[rhs[0]][2]] ** 2 / 4, out, (lhsT, rhs))
 
     def iota(out, pat, base=0, mult=0):
         small = SCRATCH[out[0]][2] != "int32"
         note("G", lambda: g.iota(ap(out), pat, base, mult, allow_small_or_imprecise_dtypes=small), 0.13 + 2 * CYCLE * width(out), out, ())
 
-    def select(out, in_, pat, o, x, mult):
-        masks.append(note("G", lambda: g.affine_select(ap(out), ap(in_), pat, o, x, 0, mult), 0.17 + 2 * CYCLE * width(out), out, (in_,)))
+    def select(out, in_, pat, o, x, mult, base=0):
+        masks.append(note("G", lambda: g.affine_select(ap(out), ap(in_), pat, o, x, base, mult), 0.17 + 2 * CYCLE * width(out), out, (in_,)))
 
     masks = []
     loaded, last_load, sent, final = [0.0], {}, [0, 0], []
@@ -255,7 +259,8 @@ def rank_program(g, core, T, topo):
         last_load[q] = me
 
     def move_dma(q, out, src, view, sem):
-        note(q, lambda: H[q].dma_start(out=ap(out), in_=src), 0.05, out if isinstance(out, tuple) else None, (view,), sem, 16, DMA + 0.4)
+        note(q, lambda: H[q].dma_start(out=ap(out), in_=src), 0.05, out if isinstance(out, tuple) else None, (view,), sem, 16,
+             DMA + (1.6 if isinstance(out, tuple) else 0.4))
         final.append((sem, 16))
 
     def send(d, src, buf, sem):
@@ -279,90 +284,124 @@ def rank_program(g, core, T, topo):
     load("Y", v("X"), T.xs[:, :], "l_x")
     load("Y", v("G", 0, 4096), T.gs[:, :], "l_g")
 
-    (pF, pm, pg, g15, wi, k15, ycol, rcol, c1, p31, half, low, high) = [v("COL", 4 * k, 4 * k + 1) for k in range(13)]
-    one_row = v("ONE", p1=1)
+    pm, pg, p31, side = [v("COL", k, k + 1) for k in range(4)]
+    (pF, k15, g15, wi, ycol, rcol, c1, half, cj0, cj1, back, odd) = [v("COL", 4 * k, 4 * k + 1) for k in range(1, 13)]
+    stamp, lift = [[v("COL", c + k, c + k + 1) for k in range(3)] for c in (72, 76)]
+    low, one_row = v("OH", 0, 1), v("ONE", p1=1)
     iota(v("CI", 0, 1), [[0, 1]], 0, 1)
-    iota(v("JG"), [[1, 8], [0, 16]])
-    iota(v("J8"), [[0, 16], [1, 8]])
-    iota(v("JF", 0, 512), [[1, 512]])
+    iota(pF, [[0, 1]], 0, 1)
     iota(v("JL"), [[1, 256]])
-    iota(v("SI", 2048, 2560), [[1, 512]])
-    masks.append(len(calls) - 1)
-    iota(v("BR", p1=1), [[0, 8], [112, 16]])
-    iota(v("CK"), [[0, 2], [32, 2], [0, 8]])
-    for k, x in enumerate((3, 2, 9, 8, 18, 19, 29, 28)):
-        iota(v("VT", k, 48, 16), [[32, 3]], 32 + x)
-    for k in range(1, 4):
-        act(v("JF", 512 * k, 512 * k + 512), v("JF", 0, 512), F.Identity, bias=512.0 * k)
-    fill(v("HF", 2048, 3328), 0.0)
-    for k in range(2):
-        act(v("HF", 1024 * k, 1024 * k + 1024), v("HF", 2048, 3072))
-    fill(v("HF", 3328, 4608), 0.0)
-    act(v("HF", 4608, 5888), v("HF", 2048, 3328))
-    load("Y", v("HF", 5888, 7168), T.HF[:, 2048:3328], "l_00", v("HF", 2048, 3328))
-    vcopy(pF, v("CI", 0, 1))
-    for j, (out, o, s) in enumerate(((pm, A.bitwise_and, 15), (pg, A.logical_shift_right, 4), (p31, A.bitwise_and, 31))):
+    iota(v("JG"), [[1, 8], [0, 16]])
+    for j, (o, s) in enumerate(((A.bitwise_and, 15), (A.logical_shift_right, 4), (A.bitwise_and, 31))):
         ts(v("CI", 1 + j, 2 + j), v("CI", 0, 1), s, o)
-        vcopy(out, v("CI", 1 + j, 2 + j))
-    ts(g15, pg, 16.0, A.mult, 15.0, A.add)
-    ts(k15, pF, 16.0, A.mult, 15.0, A.add)
-    ts(wi, pm, 2.0, A.mult, 1.0, A.add)
-    tt(c1, wi, wi, A.mult)
-    ts(ycol, wi, 16.0, A.mult, 129.0 * 4096, A.add)
-    ts(rcol, c1, -8.0, A.mult, -0.40625, A.add)
-    ts(v("G8"), v("J8"), pg, A.is_equal)
+    ts(v("CI", 4, 5), v("CI", 0, 1), 15, A.bitwise_and, 1, A.logical_shift_right)
+    vcopy(v("COL", 0, 4), v("CI", 1, 5))
+    for out, src, f, x in ((g15, pg, 16.0, 15.0), (k15, pF, 16.0, 15.0), (wi, pm, 2.0, 1.0), (ycol, pm, 32.0, 129.0 * 4096 + 16)):
+        act(out, src, F.Identity, f, x)
+    act(c1, wi, F.Square)
+    act(rcol, c1, F.Identity, -8.0, -0.40625)
     ts(v("SG"), v("JG"), pg, A.is_equal)
-    ts(v("NG"), v("JG"), pg, A.is_equal, -1.0, A.mult)
-    select(v("LTm"), v("G8"), [[1, 16], [16, 8]], A.is_gt, 0.0, -1)
-    select(v("NG"), v("NG"), [[-1, 128]], A.is_ge, 0.0, 1)
-    select(v("TRI"), v("NG"), [[-1, 128]], A.not_equal, -512.0, 1)
-    for out in ("mI", "mIh"):
-        ts(v(out), v("JL", 0, 128), pF, A.is_equal)
-    for out, c, f in (("ZE", g15, 0.0625), ("ZK", k15, 1.0), ("ZA", k15, 1.0)):
-        ts(v(out), v("JL", 0, 144), c, A.is_equal, f, A.mult)
-    ts(low, pm, 0.0, A.is_equal)
-    ts(high, pm, 1.0, A.is_equal)
-    for out, src, f in ((v("mNI"), v("mI"), -1.0), (v("m48"), v("mI"), -48.0), (v("mE", 0, 128), v("mI"), 4096.0),
-                        (v("mE", 128, 256), v("mI"), -4096.0), (v("ZS"), v("ZE"), 32768.0), (v("Z8"), v("ZE"), 16.0),
-                        (v("ZV"), v("Z8"), low), (v("ZJ"), v("Z8"), high), (v("WX"), v("SG"), wi), (v("KBS", 0, 16), v("G8", 0, 16), 1024.0),
-                        (v("KBS", 16, 32), v("G8", 0, 16), 2048.0), (v("KBS", 32, 48), v("G8", 0, 16), -1024.0)):
-        act(out, src, scale=f)
-    ts(v("W2", 0, 16), v("JL", 0, 16), 16.0, A.mult, pm, A.add)
-    for k, f in enumerate((4096.0, 8192.0, -255.0)):
-        ts(v("LA", 16 * k, 16 * k + 16), v("W2", 0, 16), f, A.add)
+    ts(v("TRI"), v("JG"), pg, A.is_equal, -1.0 / 8192, A.mult)
+    select(v("LT"), v("SG"), [[1, 128]], A.is_gt, 0.0, -1)
+    select(v("LT"), v("LT"), [[16, 8], [201, 16]], A.not_equal, 1024.0, -1, -3000)
+    select(v("TRI"), v("TRI"), [[-1, 128]], A.is_ge, 0.0, 1)
+    select(v("TRI"), v("TRI"), [[-1, 128]], A.not_equal, 768.0 / 8192, 1)
+    for out, f in (("mI", 1.0), ("mIh", 1.0), ("I2", 2.0), ("Iq", 2.0 ** -14), ("mQ", 9.0 / 64)):
+        ts(v(out), v("JL", 0, 128), pF, A.is_equal, f, A.mult)
+    for out, c in (("Z8", g15), ("ZA", k15)):
+        ts(v(out), v("JL", 0, 144), c, A.is_equal)
     ts(v("RP"), v("JG"), pF, A.is_equal)
-    for out, x in ((half, 128.5001220703125), (v("ZR16"), 0.0), (v("G", 4096, 4352), 0.0), (v("G", 4464, 4608), 0.0), (v("G", 4720, 4736), 0.0),
-                   (v("CW", 0, 112), 0), (v("GW", 0, 112), 0.0), (v("ONE"), 1.0), (v("BM"), -64.0), (v("BM", 0, 512, 16), 33554432.0)):
+    ts(v("OH"), v("JL", 0, 16), pm, A.is_equal)
+    for out, src, f, x in ((cj0, v("OH", 2, 3), 4352.0, v("OH", 3, 4)), (cj1, v("OH", 4, 5), 4352.0, v("OH", 5, 6)),
+                           (odd, v("OH", 3, 4), 1.0, v("OH", 5, 6)), (v("COL", 72, 75), v("JL", 32, 128, 32), low, 0.0),
+                           (lift[0], odd, -1.0, 1.0), (lift[1], odd, 127.0, 1.0), (back, v("OH", 15, 16), 1024.0, -1024.0)):
+        act(out, src, F.Identity, f, x)
+    for out, src, f in ((v("mNI"), v("mI"), -1.0), (v("m48"), v("mI"), -48.0), (v("p48"), v("mI"), 48.0),
+                        (v("SGs"), v("SG"), 1.0 / 8192), (v("ZS"), v("Z8"), 2048.0),
+                        (v("ZS2"), v("Z8"), 4096.0), (v("ZSn"), v("Z8"), -2048.0),
+                        (v("ZV"), v("Z8"), low), (v("ZJ0"), v("Z8"), cj0), (v("ZJ1"), v("Z8"), cj1), (v("WX"), v("SG"), wi),
+                        (v("KBS", 0, 16), v("G8"), 1024.0), (v("KBS", 16, 32), v("G8"), 2048.0), (v("KBS", 32, 48), v("G8"), -1024.0)):
+        if out[0] == "KBS" and not out[1]:
+            iota(v("J8"), [[0, 2], [1, 8]])
+            ts(v("G8"), v("J8"), pg, A.is_equal)
+        act(out, src, scale=f)
+    act(v("PD", 0, 16), v("OH"), scale=-4096.0)
+    act(v("W2", 0, 16), v("OH"), scale=1024.0)
+    tt(v("PD", 1, 16), v("PD", 1, 16), v("W2", 0, 15), A.add)
+    for k in (16, 32, 64, 128):
+        act(v("PD", k, 2 * k), v("PD", 0, k))
+    act(v("W2", 16, 32), v("JL", 0, 16), F.Identity, 16.0, pm)
+    for k, (f, x) in enumerate(((1.0, 513.0), (2.0 ** -14, BASE + 8960.0 / 16384), (1.0, 4096.0))):
+        act(v("LA", 16 * k, 16 * k + 16), v("W2", 16, 32), F.Identity, f, x)
+    for out, x in ((half, 526336.5), (v("ZR16"), 0.0), (v("G", 4096, 4352), 0.0), (v("G", 4464, 4480), 0.0), (v("G", 4592, 4608), 0.0),
+                   (v("CW", 256, 368), 0.0), (v("CS", 112, 120), 0), (v("LC1"), 0), (v("ONE"), 1.0), (v("BM"), -64.0),
+                   (v("BM", 0, 512, 16), 33554432.0), (v("BQ", 112, 128), 736.0), (v("R960", p1=1), 960.0)):
         fill(out, x)
-    act(v("BQ"), v("BM", 0, 112), F.Relu)
+    act(v("BQ", 0, 112), v("BM", 0, 112), F.Relu)
+    ts(v("a16", 32, 48), v("BQ", 112, 128), BASE - 1022 * 9.0 / 64 - 736.0, A.add)
 
-    L = [v("LL", 16 * x, 16 * x + 16) for x in range(32)]
-    (ss, nn, nn4, segf, t1, ask2, popf, x2, code, k3, pos, t2, t3, tk, dj, j0, fresh) = L[:17]
-    nput, nw, slot, base = L[24:28]
-    two, own = v("LL", 384, 416), v("LL", 416, 448)
-    fi, hh, hs, hk, q8, mx = [v("LI", 16 * x, 16 * x + 16) for x in range(6)]
-    kP, ro, aP = v("ML", 64, 80), v("ML", 80, 96), v("ML", 112, 128)
-    aF, popped = v("aF"), []
+    def late_constants(after):
+        first = len(calls)
+        iota(v("VT", 16, 20), [[6, 2], [-1, 2]], 3)
+        iota(v("VT", 20, 22), [[1, 2]], 18)
+        iota(v("VT", 22, 24), [[-1, 2]], 29)
+        iota(v("VT", 24, 28), [[0, 4]], -5)
+        iota(v("VT", 28, 32), [[0, 2], [1, 2]], 1)
+        iota(v("BR", p1=1), [[0, 8], [112, 16]])
+        for k in range(2):
+            iota(v("JR", 256 * k, 256 * k + 256), [[1, 16], [0, 16]], 16 * k)
+        iota(v("JT"), [[1, 16], [16, 7]])
+        for c in calls[first:]:
+            c["preds"][after] = "order"
+        ts(v("VT", 24, 32), v("VT", 24, 32), side, A.is_equal)
+        act(v("VT", 16, 24), v("VT", 16, 24), scale=low)
+        tt(v("VT", 0, 8), v("VT", 16, 24), v("VT", 24, 32), A.add)
+        ts(v("REP"), v("JR"), p31, A.is_equal)
 
-    def lists(o, z, src, c1, rows=128, c0=0):
+    for q, c0, c2 in FILLS:
+        if q == "V":
+            fill(v("HF", c0, c2), 0.0)
+    for k, (q, c0, c2) in enumerate(x for x in FILLS if x[0] == "Y"):
+        load("Y", v("HF", c0, c2), T.HF[:, ZERO:ZERO + c2 - c0], "l_0%d" % k, v("HF", ZERO, ZERO + c2 - c0))
+    for q, c0, c2 in FILLS:
+        if q == "S":
+            act(v("HF", c0, c2), v("HF", ZERO, ZERO + c2 - c0))
+
+    (ss, dd, y1, y2, w, pos, t1, t2, t3, code, p1, p2) = [v("LL", 16 * x, 16 * x + 16) for x in range(12)]
+    a16, nn = v("a16", 0, 16), v("a16", 16, 32)
+    fi, hs, hk, q8 = [v("LI", 16 * x, 16 * x + 16) for x in range(4)]
+    ro, Qs, x2, aP = [v("ML", c, c + 16) for c in (0, 16, 32, 112)]
+    rows = v("ML", 128, 384, 1, 0, 8)
+    aF, blZ, kL, popped = v("aF"), v("blZ"), v("KL", 15, 256, 16), []
+    cellS, col0, col1 = [v("MX", q, 48, 3) for q in range(3)]
+
+    def bank(b, c0=0, c1=512):
+        return v("D%d" % (b // 2), 512 * (b % 2) + c0, 512 * (b % 2) + c1)
+
+    def lists(o, z, src, c0, c1, rows=128, start=False, stop=True):
         for i in range(16):
-            mm(o, v(z, 15 - i, 143 - i, 1, 0, rows), v(src, c0 + i, c1, 16, 0, rows), i == 0 and not c0, i == 15)
+            mm(o, v(z, 15 - i, 143 - i, 1, 0, rows), v(src, c0 + i, c1, 16, 0, rows), start and i == 0, stop and i == 15)
 
     def gather(engines, out, win, lst):
-        for k, q in enumerate(engines):
-            c1 = min(512 * k + 512, width(v(out)))
-            (vcopy if q == "V" else act)(v(out, 512 * k, c1), ind(win, v(lst, 32 * k, c1 // 16)))
+        c0 = 0
+        for q, wd in engines:
+            (vcopy if q == "V" else act)(v(out, c0, c0 + wd), ind(win, v(lst, c0 // 16, (c0 + wd) // 16)))
+            c0 += wd
             if q == "V" and out == "cS":
                 for p in popped:
                     calls[-1]["preds"].setdefault(p, "order")
 
     def start():
         vcopy(v("aS0"), v("aI"))
+        vcopy(a16, v("aI"))
         vcopy(aF, v("aI"))
-        vcopy(v("AR"), ind(v("JF"), v("aS0")))
+        for i in range(16):
+            mm(v("TR", i, 256, 16, 0, 8), v("mIh", i, 128, 16), a16, i == 0, i == 15)
+        vcopy(v("T16", p1=8), v("TR", 0, 256, 1, 0, 8))
+        mm(v("KEY", 0, 256), v("RP", p1=8), v("T16", p1=8), True, True)
+        vcopy(v("AR"), v("KEY", 0, 256))
         send(1, v("aS0"), "QA0", "r_a0")
-        iota(v("SI", 2560, 3072), [[1, 512]], 512)
-        calls[-1]["preds"][sent[1]] = "order"
+        late_constants(sent[1])
         ts(v("W1"), v("FI"), 2.0, A.mult)
         tt(v("V0"), v("W1"), v("HI"), A.add)
         note("Y", lambda: g.sync.dma_start(out=T.HF[0:128:16, 0:2048], in_=T.V0[:, :]), 0.05, v("HF", 0, 2048), (v("V0"),), "l_03", 16,
@@ -371,120 +410,112 @@ def rank_program(g, core, T, topo):
 
     def cells(t):
         if t:
-            for r in range(4):
-                act(v("RH", 256 * r, 256 * r + 256), ind(v("HF", 2048 * r, 2048 * r + 2048), v("aS%d" % t)))
-            lists(v("KEY", 256, 320), "ZV", "RH", 1024)
-            mm(v("KEY", 320, 352), one_row, v("RB", 32 * t - 32, 32 * t, 1, 0, 1), True, False)
-            lists(v("KEY", 320, 352), "ZJ", "RH", 1024, c0=512)
-            vcopy(v("cb", 0, 32), v("KEY", 288, 320))
-            tt(v("cb", 32, 64), v("KEY", 256, 288), v("cb", 0, 32), A.max)
-            tt(mx, v("cb", 32, 48), v("cb", 48, 64), A.max)
-            ts(fi, mx, 7, A.bitwise_and, 1, A.logical_shift_right)
-            ts(hh, mx, 1, A.bitwise_and)
-            ts(fresh, mx, 32.0 * t + 16, A.is_ge, 8192.0, A.mult)
-            vcopy(j0, v("KEY", 320, 336))
-            tt(dj, v("KEY", 336, 352), j0, A.subtract)
+            for r in (2, 3, 0, 1):
+                act(v("RH", 256 * r, 256 * r + 256), ind(v("HF", 2304 * r, 2304 * r + 2048), v("aS%d" % t)))
+            for c in (257, 258, 305, 306):
+                mm(v("KEY", c, c + 46, 3), v("I2"), a16, c == 257, False)
+            mm(v("KEY", 306, 352, 3), v("mI"), v("ONE", 0, 16), False, False)
+            lists(v("KEY", 353, 448, 3), "ZJ0", "RH", 512, 1024, stop=False)
+            lists(v("KEY", 354, 448, 3), "ZJ1", "RH", 512, 1024, stop=False)
+            lists(v("KEY", 256, 448, 3), "ZV", "RH", 0, 1024)
+            vcopy(v("cb", 0, 96), v("KEY", 352, 448))
+            tt(v("cb", 96, 192), v("KEY", 256, 352), v("cb", 0, 96), A.max)
+            tt(v("MX"), v("cb", 96, 144), v("cb", 144, 192), A.max)
+            tt(dd, col1, col0, A.subtract)
         else:
-            ts(q8, v("aI"), 127, A.bitwise_and)
-            vcopy(v("vU"), q8)
-            ts(v("TK"), v("AR"), 1.0 / 128, A.mult, -0.49609375, A.add)
-            ts(v("HV"), v("TK"), pm, A.is_equal, 16.0, A.mult)
-            tt(v("RH", 0, 256), ind(v("V0"), v("vU")), v("HV"), A.mult)
-            lists(v("KEY", 256, 272), "ZE", "RH", 256)
-            vcopy(mx, v("KEY", 256, 272))
-            ts(fi, mx, 1, A.logical_shift_right)
-            ts(hh, mx, 1, A.bitwise_and)
-        ts(ss, aF, 2.0, A.mult)
+            ts(v("LI", 96, 112), v("aI"), 127, A.bitwise_and)
+            ts(v("LI", 112, 128), v("aI"), 7, A.logical_shift_right)
+            vcopy(v("cU"), v("LI", 96, 128))
+            act(v("HV"), ind(v("OH"), v("cU", 16, 32)))
+            tt(v("RH", 0, 256), ind(v("V0"), v("cU", 0, 16)), v("HV"), A.mult)
+            lists(v("KEY", 256, 272), "Z8", "RH", 0, 256, start=True)
+            vcopy(cellS, v("KEY", 256, 272))
+            ts(ss, aF, 2.0, A.mult)
+        ts(fi, cellS, 7, A.bitwise_and, 1, A.logical_shift_right)
 
     def places():
         for c in range(16):
             e = 272 * c
             ts(v("E", e, e + 256 - 16 * c), v("AR", 16 * c, 256), v("aF", c, c + 1), A.is_equal)
             if c < 15:
-                mm(v("TR", 16 * c + 16, 256, 1, 0, 8), v("G8", 0, 8), v("E", e + 16, e + 256 - 16 * c), c == 0, False)
-            if c == 0:
-                mm(v("TR", 0, 16, 1, 0, 8), v("LTm", 0, 8), v("E", 0, 16), False, False)
-        for i in range(1, 16):
-            mm(v("TR", i, 256, 16, 0, 8), v("LTm", 8 * i, 8 * i + 8), v("E", i, 4096, 272), False, i == 15)
-        vcopy(v("RR", p1=8), v("TR", 0, 256, 1, 0, 8))
-        lists(kP, "ZK", "RR", 256, 8)
+                mm(v("TR", 16 * c + 16, 256), v("SG"), v("E", e + 16, e + 256 - 16 * c), c == 0, False)
+            mm(v("TR", 16 * c, 16 * c + 16), v("LT"), v("E", e, e + 16), False, c == 15)
+        scan(v("KL", 0, 256), v("PD"), v("TR", 0, 256), A.add, A.max)
 
     def pops(t):
-        tt(v("blB"), kP, fi, A.is_ge)
-        tt(nn, kP, fi, A.subtract)
-        tt(hs, kP, hh, A.add)
-        if t:
-            tt(tk, kP, dj, A.mult)
-        scan(v("scB"), v("blB"), v("ZR16"), A.add, A.add)
-        mm(ro, v("SG"), v("scB"), True, False)
-        mm(ro, v("TRI"), v("blB"), False, True)
+        mm(Qs, v("mIh"), v("a16", 32, 48), True, False)
+        mm(Qs, v("Iq"), a16, False, False)
+        tt(nn, kL, fi, A.subtract)
+        tt(hs, kL, cellS, A.add)
+        ts(blZ, nn, 1024.0, A.is_ge, 8192.0, A.mult)
+        scan(v("scB"), blZ, v("ZR16"), A.add, A.add)
+        mm(Qs, v("mQ"), nn, False, False)
+        mm(x2, v("I2"), nn, False, False)
+        mm(ro, v("TRI"), blZ, False, False)
+        mm(ro, v("SGs"), v("scB"), False, True)
+        tt(pos, ro, v("LA", 0, 16), A.max)
         ts(hk, hs, 1, A.bitwise_and)
-        ts(nn4, nn, 1.0, A.add, 8192.0, A.mult)
-        tt(slot, ss, hk, A.add)
+
+    def segments(t):
         if t:
-            tt(tk, tk, j0, A.add)
-            tt(tk, tk, fresh, A.min)
-            tt(nn4, nn4, tk, A.max)
-        tt(segf, nn4, slot, A.max)
-        ts(v("gU"), segf, (4096.0, 4464.0, 4720.0)[t], A.min)
+            tt(y1, hk, dd, A.mult)
+        tt(y2, col0 if t else ss, blZ, A.add)
+        tt(w, y1 if t else hk, y2, A.add)
+        ts(v("gU"), w, (4096.0, 4464.0, 4592.0)[t], A.min)
         popped[:] = [len(calls) - 1]
-        if t < 2:
-            tt(pos, ro, v("LA", 32, 48), A.min)
-            ts(v("CL%d" % t), pos, 511.0, A.add)
-            popped[:] = [len(calls) - 1]
-            send(1 + t, v("CL%d" % t), "QL%d" % t, "r_l%d" % t)
 
     def decide(t):
-        ts(ask2, ro, -399.0, A.is_lt, 2.0, A.mult)
-        ts(x2, nn, 2.0, A.mult, 4.0, A.add)
         tt(code, x2, hk, A.add)
-        ts(v("vU"), code, 7.0, A.min)
-        act(v("HV"), ind(v("VT", 16 * t, 16 * t + 8), v("vU")), scale=low if t < 2 else 1.0)
+        ts(v("vU"), code, -2044.0, A.add, 7.0, A.min)
+        act(v("HV"), ind(v("VT", 0, 8), v("vU")), F.Identity, bias=stamp[t])
         if t == 0:
-            ts(q8, ro, 1.0 / 7, A.mult, 508.0 / 7, A.add)
-            ts(t2, q8, -6.9375, A.mult, 511.0, A.add)
-            tt(t3, ro, t2, A.add)
+            ts(q8, pos, 1.0 / 7, A.mult, -772.0 / 7, A.add)
+            ts(t2, q8, -6.9375, A.mult, -769.0, A.add)
+            tt(t3, pos, t2, A.add)
             ts(v("jU", 0, 16), t3, 16.0, A.mult, 111.0, A.min)
-            act(v("HW"), ind(v("JL"), v("jU", 0, 16)), scale=high)
+            act(v("HW"), ind(v("JL"), v("jU", 0, 16)), F.Identity, odd, lift[0])
         if t == 1:
-            ts(v("jU", 16, 32), pos, 511.0, A.add, 111.0, A.min)
-            act(v("HW"), ind(v("JT"), v("jU", 16, 32)), scale=high)
-        tt(nw, nn, ask2, A.is_ge)
-        ts(k3, x2, 6.0, A.min, 1024.0, A.mult)
-        tt(base, k3, aF, A.add)
+            ts(v("jU", 16, 32), pos, -769.0, A.add, 111.0, A.min)
+            act(v("HW"), ind(v("JT"), v("jU", 16, 32)), F.Identity, odd, lift[1])
+        tt(t1, Qs, pos, A.max)
+        tt(t1, t1, v("LA", 16, 32), A.min)
+        ts(v("nU", 16 * t + 16, 16 * t + 32), t1, -BASE, A.add, 16384.0, A.mult)
         if t == 0:
-            ts(popf, nn, 0.0, A.is_lt)
-            tt(nput, nw, popf, A.max)
-        a, b, c = (two, own, 0) if t == 0 else (nw, base, 16)
-        tt(a, a, v("LA", c, 32), A.mult)
-        tt(a, a, b, A.max)
-        vcopy(v("nU", 32 * t + c, 32 * t + 32), a)
-        cell = ind(v("HF"), v("nU", 32 * t + 16, 32 * t + 32))
-        tt(cell, v("HV"), v("HW"), A.add) if t < 2 else vcopy(cell, v("HV"))
+            ts(p1, t1, BASE + 8960.0 / 16384, A.is_ge, 8192.0, A.mult)
+            ts(p2, blZ, -2.0, A.mult, 8192.0, A.add)
+            tt(p2, p2, w, A.add)
+            tt(p1, p1, p2, A.add)
+            tt(p1, p1, v("LA", 32, 48), A.min)
+            vcopy(v("nU", 0, 16), p1)
+        cell = ind(v("HF"), v("nU", 16 * t + 16, 16 * t + 32))
+        tt(cell, v("HV"), v("HW"), A.mult) if t < 2 else vcopy(cell, v("HV"))
 
     def refill():
         act(v("LX"), ind(v("G", 4352, 4464), v("jU", 0, 16)))
         vcopy(ind(v("G", 0, 4352), v("nU", 0, 16)), v("LX"))
 
     def move(t):
-        tt(v("zt"), ind(v("G", 0, (4112, 4480, 4736)[t]), v("gU")), v("Z%d" % t), A.add)
+        tt(v("zt"), ind(v("G", 0, (4112, 4480, 4608)[t]), v("gU")), v("Z%d" % t), A.add)
         ts(v("Z%d" % (t + 1)), v("zt"), 0.0, A.max, 255.0, A.min)
-        for e in range(2):
-            mm(v("TR", e, 256, 2), v("mI"), v("Z%d" % (t + 1), 128, 256), True, True)
+        for e in range(4):
+            mm(v("TR", e, 512, 4), v("mI"), v("Z%d" % (t + 1), 128, 256), True, True)
 
-    def centres(t, engines):
+    def centres(t):
         vcopy(v("sU"), ind(v("SI", 0, 2048), v("aS%d" % t)))
-        gather(engines, "cS", v("X"), "sU")
+        gather(CENTRES[t], "cS", v("X"), "sU")
         for b in range(4):
             for j in range(4):
-                mm(v("D%d" % b, 128 * j, 128 * j + 128), v("mNI"), v("cS", 4 * b + j, 2048, 16), j == 0, False)
+                mm(bank(b, 128 * j, 128 * j + 128), v("mNI"), v("cS", 4 * b + j, 2048, 16), j == 0, False)
 
     def keys():
-        ts(t1, v("blB"), 2048.0, A.mult)
-        tt(t1, t1, aF, A.add)
-        vcopy(v("pU"), t1)
-        vcopy(v("s16"), ind(v("SI"), v("pU")))
-        ts(v("hB"), v("s16"), 1.0 / 48, A.mult, 128.0, A.add)
+        ts(v("s16"), v("sU"), 0.0, A.add)
+        ts(v("hB"), v("sU"), 1.0 / 48, A.mult, 172.0, A.add)
+        mm(v("TR", 256, 512, 1, 0, 8), v("mIh", 0, 8, 1, 0, 8), v("T16", p1=8), True, False)
+        mm(rows, v("ONE", 0, 8, 1, 0, 1), v("R960", p1=1), True, False)
+        for i in range(16):
+            mm(v("TR", 256 + i, 512, 16, 0, 8), v("mNI", i, 128, 16), blZ, False, i == 15)
+            mm(v("ML", 128 + i, 384, 16, 0, 8), v("mI", i, 128, 16), blZ, False, False)
+        act(v("YK", p1=8), v("TR", 256, 512, 1, 0, 8), F.Identity, 1.0, 8192.0)
         for h in range(2):
             s = (128 * h, 128 * h + 128)
             mm(v("KEY", 256 * h, 256 * h + 128), v("hB", *s), v("mI"), h == 0, False)
@@ -496,125 +527,119 @@ def rank_program(g, core, T, topo):
     def search(t):
         for m in range(16):
             b, j = m // 4, m % 4
-            mm(v("D%d" % b, 128 * j, 128 * j + 128), v("mI"), v("Z%d" % (t + 1), 0, 128), False, j == 3)
-            if j == 3:
-                act(v("AB", 512 * b, 512 * b + 512), v("D%d" % b), F.Abs)
-        for m in range(8):
-            tt(v("AB", 2048 + 256 * m, 2304 + 256 * m), v("cS", 2048 + m, 4096, 8), v("TR", 0, 256), A.max)
+            mm(bank(b, 128 * j, 128 * j + 128), v("mI"), v("Z%d" % (t + 1), 0, 128), False, j == 3)
+            if m == 7:
+                act(v("AB", 0, 1024), v("D0"), F.Abs)
+            if m in (11, 15):
+                act(v("AB", 512 * b, 512 * b + 512), bank(b), F.Abs)
         for b in range(4):
-            for m in (2 * b, 2 * b + 8, 2 * b + 1, 2 * b + 9):
-                c = 2048 + 256 * (m % 8)
-                mm(v("KEY", 256 + m, 512, 16), v("AB", c + m // 8, c + 256, 2), v("KBS", 16, 32), False, False)
-            for m in range(4 * b, 4 * b + 4):
+            tt(v("AB", 2048 + 512 * b, 2560 + 512 * b), v("cS", 2048 + b, 4096, 4), v("TR"), A.max)
+        for b in range(4):
+            for e in range(4):
+                mm(v("KEY", 256 + b + 4 * e, 512, 16), v("AB", 2048 + 512 * b + e, 2560 + 512 * b, 4), v("KBS", 16, 32), False, False)
+            for m in range(4 * b - 4 * (b == 1), 4 * b + 4) if b else ():
                 mm(v("KEY", m, 256, 16), v("AB", 128 * m, 128 * m + 128), v("KBS", 0, 16), False, m == 15)
         scan(v("KS"), v("BM"), v("KEY"), A.add, A.min)
-        tt(v("KI", 0, 32), v("KS", 15, 512, 16), v("CK"), A.add)
-        ts(v("KI", 32, 64), v("KI", 0, 32), 63, A.bitwise_and)
-        vcopy(v("PB"), v("KI", 32, 64))
+        ts(v("KI"), v("KS", 15, 512, 16), 1.5 * 2 ** 29, A.add, 1.5 * 2 ** 29, A.subtract)
+        tt(v("PB"), v("KS", 15, 512, 16), v("KI"), A.subtract)
         for h in range(2):
-            o = v("TR", 128 * h, 128 * h + 128, 1, 0, 8)
-            mm(o, v("PB", 16 * h, 16 * h + 8), v("m48"), True, False)
-            mm(o, v("PB", 16 * h + 8, 16 * h + 16), v("mNI"), False, True)
-        ts(v("YA" if t == 2 else "T16", p1=8), v("TR", 0, 256, 1, 0, 8), -1.0, A.mult, -32.0, A.add)
+            o = v("ML", 128 + 128 * h, 256 + 128 * h, 1, 0, 8)
+            mm(o, v("PB", 16 * h, 16 * h + 8), v("p48"), False, False)
+            mm(o, v("PB", 16 * h + 8, 16 * h + 16), v("mI"), False, h == 1)
+        tt(v("YA" if t == 2 else "T16", p1=8), rows, v("YK", p1=8), A.min)
         if t < 2:
+            lists(aP, "ZA", "T16", 0, 256, 8, start=True)
             mm(v("KEY", 0, 256), v("RP", p1=8), v("T16", p1=8), True, True)
-            lists(aP, "ZA", "T16", 256, 8)
             vcopy(v("AR"), v("KEY", 0, 256))
             vcopy(aF, aP)
             vcopy(v("aS%d" % (t + 1)), aP)
+            vcopy(a16, aP)
 
-    def question(t):
-        a, b, qz = v("TI"), v("TJ"), v("QZ1" if t else "Z0")
-        mm(v("KA", 0, 256), v("WX"), qz, True, True)
-        act(v("xq"), v("KA", 0, 256), F.Identity, 1.0 / 4096, half)
-        mm(v("KA", 0, 256), v("WX"), qz, True, False)
-        mm(v("KA", 0, 256), v("mE", 128, 256), v("xq"), False, True)
-        act(v("Y2"), v("KA", 0, 256), F.Square, bias=ycol)
-        ts(a, v("Y2"), 0.03125, A.mult, rcol, A.add)
-        ts(b, a, 4095, A.bitwise_and)
-        if t:
-            act(v("goal"), ind(v("X"), v("QA1")))
-            mm(v("KA", 256, 512), v("mE", 0, 128), v("goal"), True, False)
-        mm(v("KA", 256, 512), v("mE", 128, 256), qz, not t, True)
-        tt(v("PK"), b, v("KA", 256, 512), A.add)
+    def slots(qz):
+        x = v("KA", 0, 256)
+        mm(x, v("WX"), qz, True, True)
+        act(v("xq"), x, F.Identity, 1.0, half)
+        mm(x, v("WX"), qz, True, False)
+        mm(x, v("mNI"), v("xq"), False, True)
+        act(v("Y2"), x, F.Square, bias=ycol)
+        ts(v("TI"), v("Y2"), 0.03125, A.mult, rcol, A.add)
+        ts(v("TJ"), v("TI"), 4095, A.bitwise_and)
 
-    def pick(t):
-        vcopy(ind(v("CW"), v("QL1" if t else "CL0")), v("PK"))
-        ts(v("TI", 0, 112), v("CW", 0, 112), 4095, A.bitwise_and)
-        vcopy(v("CC" if t else "CS"), v("TI", 0, 112))
-        ts(v("TJ", 0, 112), v("CW", 0, 112), 12, A.arith_shift_right)
+    def ask(t):
+        lanes = v("LC1", 0, 7) if t else v("CS", 112, 119)
+        if t == 0:
+            slots(v("Z0"))
+        ts(v("CL"), pos, -513.0, A.add)
+        vcopy(ind(v("CW"), v("CL")), v("JL"))
+        scan(v("KL", 256, 368), v("PD", 0, 112), v("CW", 256, 368), A.add, A.max)
+        ts(lanes, v("KL", 271, 368, 16), back, A.add)
         if t:
-            ts(v("eB"), v("TJ", 0, 112), -16.0, A.max, 16.0, A.min)
+            send(2, v("LC1"), "QL1", "r_c1")
         else:
+            vcopy(v("CS", 0, 112), ind(v("TJ"), lanes))
             send(1, v("CS"), "QC", "r_c0")
-            slots = len(calls) - 2
-            vcopy(v("ZC"), v("TJ", 0, 112))
+            act(v("ZC"), ind(v("Z0"), lanes))
             send(1, v("ZC"), "QZ0", "r_z0")
-            calls[-2]["preds"][slots] = "order"
+            asked = len(calls) - 2
+            for q, c0, c2 in FILLS:
+                if q == "G":
+                    iota(v("HF", c0, c2), [[0, c2 - c0]])
+                    calls[-1]["preds"][asked] = "order"
 
     def answer(t):
-        e = v("KA", 256, 384, 1, 0, 112)
+        e, qc = v("KA", 256, 384, 1, 0, 112), "CC" if t else "QC"
         if t:
-            pick(t)
-            mm(e, v("eB"), v("mI"), True, True)
-            act(v("eT", p1=112), e)
-        else:
-            act(v("goal"), ind(v("X"), v("QA0")))
-            vcopy(ind(v("GW"), v("QL0")), v("goal"))
-            mm(e, v("GW", 0, 112), v("mI"), True, False)
-            mm(e, v("QZ0"), v("mI"), False, True)
-            ts(v("eT", p1=112), e, -16.0, A.max, 16.0, A.min)
-        gather("VSSS", "cA", v("G", 0, 4096), "CC" if t else "QC")
+            slots(v("QZ1"))
+            vcopy(v("CC"), ind(v("TJ"), v("QL1", 0, 7)))
+            act(v("QZ0"), ind(v("QZ1"), v("QL1", 0, 7)))
+        act(v("goal"), ind(v("X"), v("QA%d" % t)))
+        act(v("eB"), ind(v("goal"), v("QL1", 0, 7) if t else v("QC", 112, 119)))
+        mm(e, v("eB"), v("mI"), True, False)
+        mm(e, v("QZ0"), v("mNI"), False, True)
+        ts(v("eT", p1=112), e, -16.0, A.max, 16.0, A.min)
+        gather(CANDS[t], "cA", v("G", 0, 4096), qc)
         mm(v("KA", 0, 112), one_row, v("JL", 0, 112, 1, 0, 1), True, False)
         mm(v("KA", 0, 112), v("BR", p1=1), v("ONE", 0, 112, 1, 0, 1), False, False)
+        cut = 112 * MAXED[t]
         for k in range(4):
-            wd = min(512, 1792 - 512 * k)
-            r = (32 * k, 32 * k + wd // 16)
-            mm(v("D%d" % k, 0, wd), v("eT", 0, 128, 1, *r), v("REP", 0, wd, 1, *r), True, False)
-            mm(v("D%d" % k, 0, wd), v("mNI"), v("cA", 512 * k, 512 * k + wd), False, True)
-            act(v("AC", 512 * k, 512 * k + wd), v("D%d" % k, 0, wd), F.Abs)
-        for b in range(16):
-            mm(v("KA", 0, 112), v("ZS", 15 - b, 143 - b), v("AC", 112 * b, 112 * b + 112), False, b == 15)
-        scan(v("KT"), v("BQ"), v("KA", 0, 112), A.add, A.min)
+            c0, c2 = 512 * k, min(512 * k + 512, 1792)
+            r = (32 * k, c2 // 16)
+            mm(bank(k, 0, c2 - c0), v("eT", 0, 128, 1, *r), v("REP", 0, c2 - c0, 1, *r), True, c2 <= cut)
+            if c2 > cut:
+                c1 = max(c0, cut)
+                mm(bank(k, c1 - c0, c2 - c0), v("mNI"), v("cA", c1, c2), False, True)
+                act(v("AC", c1, c2), bank(k, c1 - c0, c2 - c0), F.Abs)
+            if c0 < cut:
+                c1 = min(c2, cut)
+                tt(v("AC", c0, c1), v("cA", c0, c1), bank(k, 0, c1 - c0), A.max)
+        for b in range(MAXED[t]):
+            mm(v("KA", 0, 112), v("ZSn", 15 - b, 143 - b), v("cA", 112 * b, 112 * b + 112), False, False)
+        turn = [b for p in zip(range(8), range(8, 16)) for b in p]
+        for b in turn:
+            mm(v("KA", 0, 112), v("ZS2" if b < MAXED[t] else "ZS", 15 - b, 143 - b), v("AC", 112 * b, 112 * b + 112), False, b == turn[-1])
+        scan(v("KT"), v("BQ", 0, 112), v("KA", 0, 112), A.add, A.min)
         vcopy(v("KQ", 0, 7), v("KT", 15, 112, 16))
         ts(v("KQ", 16, 23), v("KQ", 0, 7), 2047, A.bitwise_and)
         vcopy(v("qU", 0, 7), v("KQ", 16, 23))
         vcopy(v("AN%d" % t), ind(v("cA"), v("qU", 0, 7)))
-        send(-1 - t, v("AN%d" % t), v("G", 4352 + 256 * t, 4464 + 256 * t), "r_n%d" % t)
+        send(-1 - t, v("AN%d" % t), v("G", 4352 + 128 * t, 4464 + 128 * t), "r_n%d" % t)
 
     start()
     for t in range(STEPS):
         cells(t)
         places()
         pops(t)
-        if t == 0:
-            question(0)
-            pick(0)
-            ranks = len(calls) - 2
-            for k in range(1024, 2048, 512):
-                iota(v("SI", 2048 + k, 2560 + k), [[1, 512]], k)
-                calls[-1]["preds"][ranks] = "order"
-            for k in range(7168, 8448, 640):
-                iota(v("HF", k, k + 640), [[0, 640]])
-                calls[-1]["preds"][ranks] = "order"
-            for k in range(2):
-                iota(v("JR", 256 * k, 256 * k + 256), [[1, 16], [0, 16]], 16 * k)
-                calls[-1]["preds"][ranks] = "order"
-            iota(v("JT"), [[1, 16], [16, 7]])
-            calls[-1]["preds"][ranks] = "order"
-            iota(v("RB", p1=1), [[256, 2], [0, 32]], 4352)
-            calls[-1]["preds"][ranks] = "order"
-            ts(v("REP"), v("JR"), p31, A.is_equal)
+        if t < 2:
+            ask(t)
+        segments(t)
         decide(t)
-        centres(t, "SSSSSSSV" if t else "SSSSSSVV")
+        centres(t)
         keys()
-        if t == 1:
-            question(t)
         move(t)
-        if t == 1:
-            refill()
         if t == 0:
             send(2, v("Z1"), "QZ1", "r_z1")
+        if t == 1:
+            refill()
         search(t)
         if t == 0:
             send(2, v("aS1"), "QA1", "r_a1")
@@ -623,13 +648,13 @@ def rank_program(g, core, T, topo):
     move_dma("Y", T.yz[:, :], T.Z3[:, :], v("Z3"), "o_z")
     move_dma("S", T.ya[:, :], T.YA[0:8, :], v("YA"), "o_a")
     for r in range(4):
-        move_dma("Y", v("SA", 128 * r, 128 * r + 128), T.HF[0:128:16, 2048 * r:2048 * r + 2048], v("HF"), "l_p%d" % r)
+        move_dma("Y", v("SA", 128 * r, 128 * r + 128), T.HF[0:128:16, 2304 * r:2304 * r + 2048], v("HF"), "l_p%d" % r)
     tt(v("W2"), v("SA", 0, 256), v("SA", 256, 512), A.max)
     tt(v("TI", 0, 128), v("W2", 0, 128), v("W2", 128, 256), A.max)
     ts(v("TJ", 0, 128), v("TI", 0, 128), 7, A.bitwise_and, 1, A.logical_shift_right)
-    ts(v("TK", 0, 128), v("TI", 0, 128), 1, A.bitwise_and)
+    ts(v("TJ", 128, 256), v("TI", 0, 128), 1, A.bitwise_and)
     vcopy(v("YF"), v("TJ", 0, 128))
-    vcopy(v("YH"), v("TK", 0, 128))
+    vcopy(v("YH"), v("TJ", 128, 256))
     move_dma("Y", T.yf[:, :], T.YF[:, :], v("YF"), "o_f")
     move_dma("S", T.yh[:, :], T.YH[:, :], v("YH"), "o_h")
 

@@ -8,7 +8,7 @@ def _b(n, c, d="bfloat16", w="sbuf", p=128):
 
 
 for _n, _c in (("X", 2048), ("G", 4608), ("HF", 9216), ("cS", 4096), ("AB", 4096), ("cA", 1792), ("AC", 1792), ("E", 4096),
-               ("mI", 128), ("mNI", 128), ("m48", 128), ("p48", 128), ("R960", 256), ("SG", 128), ("SGs", 128), ("G8", 16), ("LT", 128),
+               ("mI", 128), ("mNI", 128), ("p48", 128), ("R960", 256), ("SG", 128), ("SGs", 128), ("G8", 16), ("LT", 128),
                ("ZS", 144), ("ZS2", 144), ("ZSn", 144), ("eB", 112), ("eT", 128), ("JR", 512), ("REP", 512), ("xq", 256), ("TRI", 128), ("WX", 128), ("KBS", 48),
                ("ONE", 128), ("JG", 128), ("J8", 16), ("BR", 128), ("JL", 256), ("BM", 512), ("BQ", 128), ("V0", 128), ("RH", 1024),
                ("blZ", 16), ("scB", 16), ("hB", 256), ("zt", 256), ("goal", 256), ("PB", 32), ("HV", 256), ("LX", 256), ("SA", 512),
@@ -28,23 +28,23 @@ for _n, _c in (("aS0", 16), ("aS1", 16), ("aS2", 16), ("AR", 256), ("sU", 256), 
     _b(_n, _c, "uint16")
 for _n, _c in (("D0", 1024), ("D1", 1024), ("KEY", 512), ("ML", 512), ("TR", 512), ("KA", 512)):
     _b(_n, _c, "float32", "psum")
-SEMAPHORES = ["eV", "eS", "eP", "eG", "sent", "l_a", "l_z", "l_h", "l_f", "l_s", "l_x", "l_g", "l_p0", "l_p1", "l_p2", "l_p3", "l_00", "l_01", "l_03",
+SEMAPHORES = ["eV", "eS", "eP", "eG", "sent", "l_a", "l_z", "l_h", "l_f", "l_s", "l_x", "l_g", "l_p0", "l_p1", "l_p2", "l_p3", "l_00", "l_01", "l_02", "l_03", "l_v",
               "o_z", "o_a", "o_h", "o_f", "r_c0", "r_c1", "r_z0", "r_z1", "r_a0", "r_a1", "r_n0", "r_n1"]
 STEPS, BASE = 3, 880.21875
 ZERO = 2304
-FILLS = [("V", 2304, 3328), ("S", 0, 1024), ("S", 1024, 2048), ("S", 3328, 4352), ("V", 4608, 5632), ("V", 5632, 6656), ("G", 6912, 7552),
+FILLS = [("V", 2304, 3328), ("S", 0, 1024), ("Y", 1024, 2048), ("Y", 3328, 4352), ("Y", 4608, 5632), ("Y", 5632, 6656), ("G", 6912, 7552),
          ("G", 7552, 8192), ("G", 8192, 8960)]
-CENTRES = [[("S", 1024), ("S", 1024), ("S", 512), ("V", 512), ("V", 512), ("V", 512)]] + [[("S", 1024)] * 4, [("S", 1024)] * 3 + [("S", 512), ("V", 512)]]
-CANDS = [[("S", 1024), ("S", 768)], [("V", 512), ("V", 384), ("S", 384), ("S", 512)]]
-MAXED = [0, 8]
+CENTRES = [[("S", 1024)] * 3 + [("V", 512), ("V", 512)]] + [[("S", 2048), ("S", 1024), ("S", 1024)], [("S", 2048), ("S", 1024), ("S", 512), ("V", 512)]]
+CANDS = [[("V", 672), ("S", 352), ("S", 768)], [("V", 512), ("V", 384), ("S", 384), ("S", 512)]]
+MAXED = [6, 8]
 CYCLE, PE_CYCLE, GATHER, SCATTER = 0.00083, 0.00045, 1.56, 3.8
-SAME, CROSS, DMA, LOAD_RATE, ISSUE, FIRST, REMOTE, LINK_RATE = 0.06, 0.26, 1.5, 380e3, 0.7, 4.0, 1.8, 60e3
+SAME, CROSS, DMA, LOAD_RATE, ISSUE, FIRST, REMOTE, LINK_RATE = 0.07, 0.33, 1.0, 360e3, 0.6, 3.5, 1.1, 90e3
 BYTES = {"bfloat16": 2, "float16": 2, "uint16": 2, "float32": 4, "int32": 4}
 CASES = [{"": 1.0, "send": s, "load": d, "first": f, "wake": w, "plain": p, "gather": p * g, "scatter": p * c, "call": a}
          for s, d, f, w, p, g, c, a in ((1.0, 1.0, 1.0, 1.0, 1.0, 1.0, 1.0, 0.0), (0.8, 1.15, 1.5, 1.2, 1.0, 1.2, 0.7, 0.02),
                                         (1.4, 0.85, 0.7, 0.8, 1.0, 0.8, 1.3, 0.0), (1.0, 1.0, 1.0, 1.0, 1.3, 1.0, 1.0, 0.0),
                                         (1.4, 1.0, 1.5, 1.3, 1.15, 1.0, 1.0, 0.03))]
-ORDER, PASSES = [], 2000
+ORDER, PASSES = [], 3000
 
 
 def one_pass(calls, after, ready, rest):
@@ -101,6 +101,8 @@ def issue_order(calls):
     for i, c in enumerate(calls):
         for p, kind in c["preds"].items():
             late, wake = (0.0, 0.0) if kind == "order" else (calls[p]["late"], SAME if calls[p]["q"] == c["q"] else CROSS)
+            if kind == "after":
+                late, wake = late - DMA, 0.0
             after[p].append((i, late + wake))
             before[i].append((p, late + wake))
             waits[i].append((p, late, wake))
@@ -137,6 +139,23 @@ def issue_order(calls):
             held = [(i, j) for i, j in held if run_of[i] is not run_of[j]]
         best = min(best, (t, order))
     return best[1]
+
+
+def joined(calls):
+    head, parts, short = [], [], []
+    for i, c in enumerate(calls):
+        preds = {}
+        for p, kind in c["preds"].items():
+            if preds.get(head[p]) != "wait":
+                preds[head[p]] = kind
+        if c["q"] == "P" and c["preds"].get(i - 1) == "order" and all(p == head[-1] or short[-1]["preds"].get(p) in (k, "wait") for p, k in preds.items()):
+            short[-1]["cost"] += c["cost"]
+            parts[-1].append(i)
+        else:
+            short.append(dict(c, preds=preds))
+            parts.append([i])
+        head.append(len(short) - 1)
+    return [i for j in issue_order(short) for i in parts[j]]
 
 
 def rank_program(g, core, T, topo):
@@ -252,15 +271,15 @@ def rank_program(g, core, T, topo):
     loaded, last_load, sent, final = [0.0], {}, [0, 0], []
 
     def load(q, out, in_, sem, *view):
-        loaded[0] += 128 * width(out) * BYTES[SCRATCH[out[0]][2]] / LOAD_RATE
+        loaded[0] = 128 * width(out) * BYTES[SCRATCH[out[0]][2]] / LOAD_RATE + (0.0 if view else loaded[0])
         me = note(q, lambda: H[q].dma_start(out=ap(out), in_=in_), 0.05, out, view, sem, 16, DMA + loaded[0], "load")
         if q in last_load:
-            calls[me]["preds"][last_load[q]] = "order"
+            calls[me]["preds"].setdefault(last_load[q], "after" if view else "order")
         last_load[q] = me
 
     def move_dma(q, out, src, view, sem):
         note(q, lambda: H[q].dma_start(out=ap(out), in_=src), 0.05, out if isinstance(out, tuple) else None, (view,), sem, 16,
-             DMA + (1.6 if isinstance(out, tuple) else 0.4))
+             DMA + (1.0 if isinstance(out, tuple) else 0.4))
         final.append((sem, 16))
 
     def send(d, src, buf, sem):
@@ -316,7 +335,7 @@ def rank_program(g, core, T, topo):
                            (odd, v("OH", 3, 4), 1.0, v("OH", 5, 6)), (v("COL", 72, 75), v("JL", 32, 128, 32), low, 0.0),
                            (lift[0], odd, -1.0, 1.0), (lift[1], odd, 127.0, 1.0), (back, v("OH", 15, 16), 1024.0, -1024.0)):
         act(out, src, F.Identity, f, x)
-    for out, src, f in ((v("mNI"), v("mI"), -1.0), (v("m48"), v("mI"), -48.0), (v("p48"), v("mI"), 48.0),
+    for out, src, f in ((v("mNI"), v("mI"), -1.0), (v("p48"), v("mI"), 48.0),
                         (v("SGs"), v("SG"), 1.0 / 8192), (v("ZS"), v("Z8"), 2048.0),
                         (v("ZS2"), v("Z8"), 4096.0), (v("ZSn"), v("Z8"), -2048.0),
                         (v("ZV"), v("Z8"), low), (v("ZJ0"), v("Z8"), cj0), (v("ZJ1"), v("Z8"), cj1), (v("WX"), v("SG"), wi),
@@ -333,11 +352,9 @@ def rank_program(g, core, T, topo):
     act(v("W2", 16, 32), v("JL", 0, 16), F.Identity, 16.0, pm)
     for k, (f, x) in enumerate(((1.0, 513.0), (2.0 ** -14, BASE + 8960.0 / 16384), (1.0, 4096.0))):
         act(v("LA", 16 * k, 16 * k + 16), v("W2", 16, 32), F.Identity, f, x)
-    for out, x in ((half, 526336.5), (v("ZR16"), 0.0), (v("G", 4096, 4352), 0.0), (v("G", 4464, 4480), 0.0), (v("G", 4592, 4608), 0.0),
-                   (v("CW", 256, 368), 0.0), (v("CS", 112, 120), 0), (v("LC1"), 0), (v("ONE"), 1.0), (v("BM"), -64.0),
-                   (v("BM", 0, 512, 16), 33554432.0), (v("BQ", 112, 128), 736.0), (v("R960", p1=1), 960.0)):
+    for out, x in ((half, 526336.5), (v("ZR16"), 0.0), (v("G", 4096, 4112), 0.0),
+                   (v("CW", 256, 368), 0.0), (v("CS", 112, 120), 0), (v("LC1"), 0), (v("ONE"), 1.0), (v("BQ", 112, 128), 736.0)):
         fill(out, x)
-    act(v("BQ", 0, 112), v("BM", 0, 112), F.Relu)
     ts(v("a16", 32, 48), v("BQ", 112, 128), BASE - 1022 * 9.0 / 64 - 736.0, A.add)
 
     def late_constants(after):
@@ -351,6 +368,9 @@ def rank_program(g, core, T, topo):
         for k in range(2):
             iota(v("JR", 256 * k, 256 * k + 256), [[1, 16], [0, 16]], 16 * k)
         iota(v("JT"), [[1, 16], [16, 7]])
+        for out, x in ((v("R960", p1=1), 960), (v("BM"), -64), (v("BM", 0, 512, 16), 16000000), (v("BQ", 0, 112), 0), (v("BQ", 0, 112, 16), 16000000),
+                       (v("G", 4112, 4352), 0), (v("G", 4464, 4480), 0), (v("G", 4592, 4608), 0)):
+            iota(out, [[0, width(out)]], x)
         for c in calls[first:]:
             c["preds"][after] = "order"
         ts(v("VT", 24, 32), v("VT", 24, 32), side, A.is_equal)
@@ -404,9 +424,9 @@ def rank_program(g, core, T, topo):
         late_constants(sent[1])
         ts(v("W1"), v("FI"), 2.0, A.mult)
         tt(v("V0"), v("W1"), v("HI"), A.add)
-        note("Y", lambda: g.sync.dma_start(out=T.HF[0:128:16, 0:2048], in_=T.V0[:, :]), 0.05, v("HF", 0, 2048), (v("V0"),), "l_03", 16,
-             DMA + loaded[0], "load")
-        calls[-1]["preds"][last_load["Y"]] = "order"
+        note("Y", lambda: g.sync.dma_start(out=T.HF[0:128:16, 0:2048], in_=T.V0[:, :]), 0.05, v("HF", 0, 2048), (v("V0"),), "l_v", 16,
+             DMA + 0.4, "load")
+        calls[-1]["preds"].setdefault(last_load["Y"], "after")
 
     def cells(t):
         if t:
@@ -508,7 +528,7 @@ def rank_program(g, core, T, topo):
                 mm(bank(b, 128 * j, 128 * j + 128), v("mNI"), v("cS", 4 * b + j, 2048, 16), j == 0, False)
 
     def keys():
-        ts(v("s16"), v("sU"), 0.0, A.add)
+        ts(v("s16"), v("sU"), -1.0, A.mult)
         ts(v("hB"), v("sU"), 1.0 / 48, A.mult, 172.0, A.add)
         mm(v("TR", 256, 512, 1, 0, 8), v("mIh", 0, 8, 1, 0, 8), v("T16", p1=8), True, False)
         mm(rows, v("ONE", 0, 8, 1, 0, 1), v("R960", p1=1), True, False)
@@ -519,7 +539,7 @@ def rank_program(g, core, T, topo):
         for h in range(2):
             s = (128 * h, 128 * h + 128)
             mm(v("KEY", 256 * h, 256 * h + 128), v("hB", *s), v("mI"), h == 0, False)
-            mm(v("KEY", 256 * h + 128, 256 * h + 256), v("hB", *s), v("m48"), False, False)
+            mm(v("KEY", 256 * h + 128, 256 * h + 256), v("hB", *s), v("p48"), False, False)
             mm(v("KEY", 256 * h + 128, 256 * h + 256), v("s16", *s), v("mIh"), False, False)
         for m in range(16):
             mm(v("KEY", 256 + m, 512, 16), v("cS", 2048 + m, 4096, 16), v("KBS", 32, 48), False, False)
@@ -545,7 +565,7 @@ def rank_program(g, core, T, topo):
         for h in range(2):
             o = v("ML", 128 + 128 * h, 256 + 128 * h, 1, 0, 8)
             mm(o, v("PB", 16 * h, 16 * h + 8), v("p48"), False, False)
-            mm(o, v("PB", 16 * h + 8, 16 * h + 16), v("mI"), False, h == 1)
+            mm(o, v("PB", 16 * h + 8, 16 * h + 16), v("mNI"), False, h == 1)
         tt(v("YA" if t == 2 else "T16", p1=8), rows, v("YK", p1=8), A.min)
         if t < 2:
             lists(aP, "ZA", "T16", 0, 256, 8, start=True)
@@ -656,10 +676,10 @@ def rank_program(g, core, T, topo):
     vcopy(v("YF"), v("TJ", 0, 128))
     vcopy(v("YH"), v("TJ", 128, 256))
     move_dma("Y", T.yf[:, :], T.YF[:, :], v("YF"), "o_f")
-    move_dma("S", T.yh[:, :], T.YH[:, :], v("YH"), "o_h")
+    move_dma("Y", T.yh[:, :], T.YH[:, :], v("YH"), "o_h")
 
     if not ORDER:
-        ORDER.extend(issue_order(calls))
+        ORDER.extend(joined(calls))
     cnt = {"V": 0, "S": 0, "P": 0, "G": 0}
     known = {q: {} for q in H}
     done = {}

from concourse.mybir import AluOpType as A, ActivationFunctionType as F

SCRATCH = {}


def _b(n, c, d="bfloat16", w="sbuf", p=128):
    SCRATCH[n] = (w, [p, c], d)


for _n, _c in (("X", 2048), ("G", 4608), ("HF", 9216), ("cS", 4096), ("AB", 4096), ("cA", 1792), ("AC", 1792), ("E", 4096),
               ("mI", 128), ("mNI", 128), ("p48", 128), ("R960", 256), ("SG", 128), ("SGs", 128), ("G8", 16), ("LT", 128),
               ("ZS", 144), ("ZS2", 144), ("ZSn", 144), ("eB", 112), ("eT", 128), ("JR", 512), ("REP", 512), ("xq", 256), ("TRI", 128), ("WX", 128), ("KBS", 48),
               ("ONE", 128), ("JG", 128), ("J8", 16), ("BR", 128), ("JL", 256), ("BM", 512), ("BQ", 128), ("V0", 128), ("RH", 1024),
               ("blZ", 16), ("scB", 16), ("hB", 256), ("zt", 256), ("goal", 256), ("PB", 32), ("HV", 256), ("LX", 256), ("SA", 512),
               ("Z0", 256), ("Z1", 256), ("Z2", 256), ("Z3", 256), ("AN0", 112), ("AN1", 112), ("ZV", 144), ("ZJ0", 144), ("ZJ1", 144),
               ("Z8", 144), ("HW", 256), ("VT", 32), ("JT", 112), ("QZ0", 112), ("QZ1", 256), ("ZC", 112), ("CW", 512), ("PD", 256)):
    _b(_n, _c)
for _n, _c in (("mIh", 128), ("RP", 128), ("s16", 256), ("T16", 256), ("ZA", 144), ("I2", 128), ("Iq", 128), ("mQ", 128), ("a16", 48)):
    _b(_n, _c, "float16")
for _n, _c in (("COL", 128), ("LA", 64), ("W1", 128), ("W2", 256), ("ZR16", 16), ("LL", 320), ("KS", 512), ("KT", 112),
               ("aF", 16), ("Y2", 256), ("YA", 256), ("YH", 128), ("YF", 128), ("cb", 192), ("KI", 32), ("KL", 368),
               ("OH", 16), ("YK", 256)):
    _b(_n, _c, "float32")
for _n, _c in (("SI", 2048), ("FI", 128), ("HI", 128), ("aI", 16), ("CI", 8), ("LI", 128), ("MX", 48), ("TI", 256), ("TJ", 256), ("KQ", 32)):
    _b(_n, _c, "int32")
for _n, _c in (("aS0", 16), ("aS1", 16), ("aS2", 16), ("AR", 256), ("sU", 256), ("gU", 16), ("nU", 64), ("vU", 16), ("cU", 32),
               ("jU", 32), ("qU", 8), ("CL", 16), ("CS", 120), ("QC", 120), ("CC", 112), ("LC1", 8), ("QL1", 8), ("QA0", 16), ("QA1", 16)):
    _b(_n, _c, "uint16")
for _n, _c in (("D0", 1024), ("D1", 1024), ("KEY", 512), ("ML", 512), ("TR", 512), ("KA", 512)):
    _b(_n, _c, "float32", "psum")
SEMAPHORES = ["eV", "eS", "eP", "eG", "sent", "l_a", "l_z", "l_h", "l_f", "l_s", "l_x", "l_g", "l_p0", "l_p1", "l_p2", "l_p3", "l_00", "l_01", "l_02", "l_03", "l_v",
              "o_z", "o_a", "o_h", "o_f", "r_c0", "r_c1", "r_z0", "r_z1", "r_a0", "r_a1", "r_n0", "r_n1"]
STEPS, BASE = 3, 880.21875
ZERO = 2304
FILLS = [("V", 2304, 3328), ("S", 0, 1024), ("Y", 1024, 2048), ("Y", 3328, 4352), ("Y", 4608, 5632), ("Y", 5632, 6656), ("G", 6912, 7552),
         ("G", 7552, 8192), ("G", 8192, 8960)]
CENTRES = [[("S", 1024)] * 3 + [("V", 512), ("V", 512)]] + [[("S", 2048), ("S", 1024), ("S", 1024)], [("S", 2048), ("S", 1024), ("S", 512), ("V", 512)]]
CANDS = [[("V", 672), ("S", 352), ("S", 768)], [("V", 512), ("V", 384), ("S", 384), ("S", 512)]]
MAXED = [6, 8]
CYCLE, PE_CYCLE, GATHER, SCATTER = 0.00083, 0.00045, 1.56, 3.8
SAME, CROSS, DMA, LOAD_RATE, ISSUE, FIRST, REMOTE, LINK_RATE = 0.07, 0.33, 1.0, 360e3, 0.6, 3.5, 1.1, 90e3
BYTES = {"bfloat16": 2, "float16": 2, "uint16": 2, "float32": 4, "int32": 4}
CASES = [{"": 1.0, "send": s, "load": d, "first": f, "wake": w, "plain": p, "gather": p * g, "scatter": p * c, "call": a}
         for s, d, f, w, p, g, c, a in ((1.0, 1.0, 1.0, 1.0, 1.0, 1.0, 1.0, 0.0), (0.8, 1.15, 1.5, 1.2, 1.0, 1.2, 0.7, 0.02),
                                        (1.4, 0.85, 0.7, 0.8, 1.0, 0.8, 1.3, 0.0), (1.0, 1.0, 1.0, 1.0, 1.3, 1.0, 1.0, 0.0),
                                        (1.4, 1.0, 1.5, 1.3, 1.15, 1.0, 1.0, 0.03))]
ORDER, PASSES = [], 3000


def one_pass(calls, after, ready, rest):
    left, ready = [0] * len(calls), list(ready)
    for a in after:
        for j, d in a:
            left[j] += 1
    free = {c["q"]: 0.0 for c in calls}
    pool = {q: [i for i, c in enumerate(calls) if c["q"] == q and not left[i]] for q in free}
    order, start = [], [0.0] * len(calls)
    while len(order) < len(calls):
        now, q = min((max(free[q], min(ready[i] for i in pool[q])), q) for q in pool if pool[q])
        best = max((i for i in pool[q] if ready[i] <= now + 0.02), key=lambda i: (rest[i], -i))
        cost = calls[best]["cost"]
        for h in sorted((i for i in pool[q] if now + 0.02 < ready[i] < now + cost and rest[i] > rest[best]), key=lambda i: rest[i])[-1:]:
            if ready[h] + max(rest[h], cost + rest[best]) < now + cost + rest[h]:
                short = [i for i in pool[q] if max(ready[i], now) + calls[i]["cost"] <= ready[h] + 0.02]
                best = max(short, key=lambda i: (rest[i], -i)) if short else h
        pool[q].remove(best)
        start[best] = max(now, ready[best])
        free[q] = start[best] + calls[best]["cost"]
        order.append(best)
        for j, d in after[best]:
            ready[j] = max(ready[j], free[q] + d)
            left[j] -= 1
            if not left[j]:
                pool[calls[j]["q"]].append(j)
    return order, start


def length(calls, before, order, case, held=None):
    last, end, why = {}, [0.0] * len(calls), [None] * len(calls)
    for i in order:
        c = calls[i]
        by = last.get(c["q"])
        t, queue = (0.0, False) if by is None else (end[by], True)
        for p, late, wake in before[i]:
            x = end[p] + late * case[calls[p]["kind"]] + wake * case["wake"]
            if x >= t:
                t, by, queue = x, p, False
        end[i] = t + c["cost"] * case[c["work"]] + case["call"] * (c["q"] in "VS") + c["first"] * (case["first"] - 1)
        last[c["q"]], why[i] = i, (by, queue)
    t, i = max((end[i] + c["late"], i) for i, c in enumerate(calls))
    while held is not None and i is not None:
        if why[i][1]:
            held.append((i, why[i][0]))
        i = why[i][0]
    return t


def issue_order(calls):
    n = len(calls)
    after, before, waits = [[] for _ in calls], [[] for _ in calls], [[] for _ in calls]
    for i, c in enumerate(calls):
        for p, kind in c["preds"].items():
            late, wake = (0.0, 0.0) if kind == "order" else (calls[p]["late"], SAME if calls[p]["q"] == c["q"] else CROSS)
            if kind == "after":
                late, wake = late - DMA, 0.0
            after[p].append((i, late + wake))
            before[i].append((p, late + wake))
            waits[i].append((p, late, wake))
    rest = [0.0] * n
    for i in range(n - 1, -1, -1):
        rest[i] = max([calls[i]["late"]] + [d + calls[j]["cost"] + rest[j] for j, d in after[i]])
    runs = {}
    for i, c in enumerate(calls):
        runs.setdefault((c["q"], c["piece"]), []).append(i)
    run_of = [runs[c["q"], c["piece"]] for c in calls]
    runs = list(runs.values())
    best, now, x, held = (1e9, None), 1e9, 1, []
    for k in range(PASSES):
        r = list(rest)
        for _ in range(1 + k % 3 if k else 0):
            x = (x * 1103515245 + 12345) % 2 ** 31
            if k % 2 and held:
                late, early = held[(x >> 8) % len(held)]
                d = max(r[early] - r[late], 0.0) + 0.1 + (x >> 20) % 8 / 8.0
                for i in run_of[late] if x >> 16 & 1 else run_of[early]:
                    r[i] += d if x >> 16 & 1 else -d
            else:
                for i in runs[(x >> 8) % len(runs)]:
                    r[i] += (x >> 20) % 25 / 8.0 - 1.5
        order, start = one_pass(calls, after, [0.0] * n, r)
        if k % 3 == 1:
            r = one_pass(calls, before, [c["late"] for c in calls], start)[1]
            order = one_pass(calls, after, [0.0] * n, r)[0]
        t = sum(length(calls, waits, order, case) / case["plain"] for case in CASES) / len(CASES)
        if t < now + 0.03:
            rest, now, held = r, t, []
            for case in CASES:
                length(calls, waits, order, case, held)
            held = [(i, j) for i, j in held if run_of[i] is not run_of[j]]
        best = min(best, (t, order))
    return best[1]


def joined(calls):
    head, parts, short = [], [], []
    for i, c in enumerate(calls):
        preds = {}
        for p, kind in c["preds"].items():
            if preds.get(head[p]) != "wait":
                preds[head[p]] = kind
        if c["q"] == "P" and c["preds"].get(i - 1) == "order" and all(p == head[-1] or short[-1]["preds"].get(p) in (k, "wait") for p, k in preds.items()):
            short[-1]["cost"] += c["cost"]
            parts[-1].append(i)
        else:
            short.append(dict(c, preds=preds))
            parts.append([i])
        head.append(len(short) - 1)
    return [i for j in issue_order(short) for i in parts[j]]


def rank_program(g, core, T, topo):
    rank = T.rank_of(core)
    if rank is None:
        return
    n = len(T.cores)
    H = {"V": g.vector, "S": g.scalar, "P": g.tensor, "G": g, "Y": g.sync}

    def v(name, c0=0, c1=None, st=1, p0=0, p1=None):
        sh = SCRATCH[name][1]
        return (name, c0, sh[1] if c1 is None else c1, st, p0, sh[0] if p1 is None else p1)

    def ap(x):
        if not isinstance(x, tuple):
            return x
        if x[0] == "ind":
            return ap(x[1]).indirect(ap(x[2]))
        name, c0, c1, st, p0, p1 = x
        return T[name][p0:p1, c0:c1] if st == 1 else T[name][p0:p1, c0:c1:st]

    def ind(win, off):
        return ("ind", win, off)

    def width(x):
        return 16 * width(x[2]) if x[0] == "ind" else len(range(x[1], x[2], x[3]))

    def meet(e, x):
        return e[1] < x[2] and x[1] < e[2] and not (e[3] == x[3] > 1 and (e[1] - x[1]) % x[3])

    calls, wr, rd, bank_use, piece = [], {}, {}, {}, [0]

    def note(q, run, cost, out, ins, sem=None, inc=1, late=0.0, kind="", first=0.0):
        rs, flat = [], [x for x in ins if isinstance(x, tuple)]
        for x in flat:
            rs += [x[1], x[2]] if x[0] == "ind" else [x]
        ws = [] if out is None else [out]
        if out is not None and out[0] == "ind":
            ws, rs = [out[1]], rs + [out[2]]
        me, preds = len(calls), {}
        for x in ws + rs:
            if SCRATCH[x[0]][0] == "psum":
                for bank in range(x[1] // 512, (x[2] - 1) // 512 + 1):
                    use = bank_use.setdefault((x[0], bank), {})
                    for k, p in use.items():
                        if p != me and preds.get(p) != "wait":
                            preds[p] = "order" if k == q else "wait"
                    use[q] = me
                continue
            for e, p in wr.get(x[0], []) + (rd.get(x[0], []) if x in ws else []):
                if meet(e, x):
                    preds[p] = "wait"
        for x in ws:
            if SCRATCH[x[0]][0] != "psum":
                if x[3] == 1 and out[0] != "ind":
                    for d in (wr, rd):
                        d[x[0]] = [(e, p) for e, p in d.get(x[0], []) if not (x[1] <= e[1] and e[2] <= x[2])]
                wr.setdefault(x[0], []).append((x, me))
        for x in rs:
            if SCRATCH[x[0]][0] != "psum":
                rd.setdefault(x[0], []).append((x, me))
        if not calls or calls[-1]["out"] != (ws[0][0] if ws else None):
            piece[0] += 1
        work = "" if run is None or sem else "scatter" if out[0] == "ind" else "gather" if len(rs) > len(flat) else "plain"
        calls.append({"q": q, "run": run, "work": work, "cost": cost, "late": late, "preds": preds, "sem": sem, "kind": kind, "first": first,
                      "out": ws[0][0] if ws else None, "piece": piece[0] // 4, "inc": inc})
        return me

    def op(q, call, out, *ins, rate=None):
        full = [x for x in (out,) + ins if isinstance(x, tuple) and width(x) == width(out)]
        if out[0] == "ind" or any(x[0] == "ind" for x in full):
            cost = 0.06 + CYCLE * width(out) * (SCATTER if out[0] == "ind" else GATHER)
        else:
            if rate is None:
                rate = 0.5 if q == "V" and all(BYTES[SCRATCH[x[0]][2]] == 2 for x in full) else 1.0
            cost = 0.025 + CYCLE * max(64, width(out) * rate) if q == "V" else 0.08 + CYCLE * width(out)
        note(q, call, cost, out, ins)

    def vcopy(out, in_):
        op("V", lambda: g.vector.tensor_copy(out=ap(out), in_=ap(in_)), out, in_)

    def tt(out, a, b, o):
        both = a[0] != "ind" and SCRATCH[a[0]][0] == SCRATCH[b[0]][0]
        op("V", lambda: g.vector.tensor_tensor(out=ap(out), in0=ap(a), in1=ap(b), op=o), out, a, b, rate=1.0 + both)

    def ts(out, a, s1, o1, s2=None, o2=None):
        if o2 is None:
            op("V", lambda: g.vector.tensor_scalar(out=ap(out), in0=ap(a), scalar1=ap(s1), scalar2=None, op0=o1), out, a, s1)
        else:
            op("V", lambda: g.vector.tensor_scalar(out=ap(out), in0=ap(a), scalar1=ap(s1), scalar2=ap(s2), op0=o1, op1=o2), out, a, s1, s2)

    def scan(out, a, b, o0, o1):
        op("V", lambda: g.vector.tensor_tensor_scan(out=ap(out), data0=ap(a), data1=ap(b), initial=0.0, op0=o0, op1=o1), out, a, b)

    def act(out, in_, f=F.Copy, scale=1.0, bias=0.0):
        op("S", lambda: g.scalar.activation(out=ap(out), in_=ap(in_), func=f, scale=ap(scale), bias=ap(bias)), out, in_, scale, bias)

    def fill(out, x):
        op("V", lambda: g.vector.memset(ap(out), x), out)

    def mm(out, lhsT, rhs, start, stop):
        note("P", lambda: g.tensor.matmul(ap(out), ap(lhsT), ap(rhs), start, stop),
             0.005 + PE_CYCLE * max(min(64, width(lhsT)), width(rhs)) * BYTES[SCRATCH[rhs[0]][2]] ** 2 / 4, out, (lhsT, rhs))

    def iota(out, pat, base=0, mult=0):
        small = SCRATCH[out[0]][2] != "int32"
        note("G", lambda: g.iota(ap(out), pat, base, mult, allow_small_or_imprecise_dtypes=small), 0.13 + 2 * CYCLE * width(out), out, ())

    def select(out, in_, pat, o, x, mult, base=0):
        masks.append(note("G", lambda: g.affine_select(ap(out), ap(in_), pat, o, x, base, mult), 0.17 + 2 * CYCLE * width(out), out, (in_,)))

    masks = []
    loaded, last_load, sent, final = [0.0], {}, [0, 0], []

    def load(q, out, in_, sem, *view):
        loaded[0] = 128 * width(out) * BYTES[SCRATCH[out[0]][2]] / LOAD_RATE + (0.0 if view else loaded[0])
        me = note(q, lambda: H[q].dma_start(out=ap(out), in_=in_), 0.05, out, view, sem, 16, DMA + loaded[0], "load")
        if q in last_load:
            calls[me]["preds"].setdefault(last_load[q], "after" if view else "order")
        last_load[q] = me

    def move_dma(q, out, src, view, sem):
        note(q, lambda: H[q].dma_start(out=ap(out), in_=src), 0.05, out if isinstance(out, tuple) else None, (view,), sem, 16,
             DMA + (1.0 if isinstance(out, tuple) else 0.4))
        final.append((sem, 16))

    def send(d, src, buf, sem):
        to, buf = T.cores[(rank + d) % n], buf if isinstance(buf, tuple) else v(buf)
        rid, pid = topo.addr(to)[0], topo.addr(to)[1]
        e = topo.engines(core, to)[:8]
        me = note("G", lambda: g.remote_dma(ap(buf), ap(src), T.sem[sem], T.sem.sent, pid, rid, sum(1 << x for x in e)),
                  ISSUE + (0.0 if sent[0] else FIRST), None, (src,), "sent", 0, REMOTE + 256 * abs(d) * width(src) / LINK_RATE,
                  "send", 0.0 if sent[0] else FIRST)
        for p in [sent[1]] if sent[0] else masks:
            calls[me]["preds"][p] = "order"
        sent[:2] = sent[0] + len(e), sent[1] if sent[0] else me
        here = note("R", None, 0.0, buf, (), sem, len(topo.engines(T.cores[(rank - d) % n], core)[:8]))
        calls[here]["preds"][me] = "wait"

    load("Y", v("aI"), T.a0[:, :], "l_a")
    load("S", v("FI"), T.fl0[:, :], "l_f")
    load("Y", v("HI"), T.hd0[:, :], "l_h")
    load("S", v("Z0"), T.z0[:, :], "l_z")
    load("Y", v("SI", 0, 2048), T.su[:, :], "l_s")
    load("Y", v("X"), T.xs[:, :], "l_x")
    load("Y", v("G", 0, 4096), T.gs[:, :], "l_g")

    pm, pg, p31, side = [v("COL", k, k + 1) for k in range(4)]
    (pF, k15, g15, wi, ycol, rcol, c1, half, cj0, cj1, back, odd) = [v("COL", 4 * k, 4 * k + 1) for k in range(1, 13)]
    stamp, lift = [[v("COL", c + k, c + k + 1) for k in range(3)] for c in (72, 76)]
    low, one_row = v("OH", 0, 1), v("ONE", p1=1)
    iota(v("CI", 0, 1), [[0, 1]], 0, 1)
    iota(pF, [[0, 1]], 0, 1)
    iota(v("JL"), [[1, 256]])
    iota(v("JG"), [[1, 8], [0, 16]])
    for j, (o, s) in enumerate(((A.bitwise_and, 15), (A.logical_shift_right, 4), (A.bitwise_and, 31))):
        ts(v("CI", 1 + j, 2 + j), v("CI", 0, 1), s, o)
    ts(v("CI", 4, 5), v("CI", 0, 1), 15, A.bitwise_and, 1, A.logical_shift_right)
    vcopy(v("COL", 0, 4), v("CI", 1, 5))
    for out, src, f, x in ((g15, pg, 16.0, 15.0), (k15, pF, 16.0, 15.0), (wi, pm, 2.0, 1.0), (ycol, pm, 32.0, 129.0 * 4096 + 16)):
        act(out, src, F.Identity, f, x)
    act(c1, wi, F.Square)
    act(rcol, c1, F.Identity, -8.0, -0.40625)
    ts(v("SG"), v("JG"), pg, A.is_equal)
    ts(v("TRI"), v("JG"), pg, A.is_equal, -1.0 / 8192, A.mult)
    select(v("LT"), v("SG"), [[1, 128]], A.is_gt, 0.0, -1)
    select(v("LT"), v("LT"), [[16, 8], [201, 16]], A.not_equal, 1024.0, -1, -3000)
    select(v("TRI"), v("TRI"), [[-1, 128]], A.is_ge, 0.0, 1)
    select(v("TRI"), v("TRI"), [[-1, 128]], A.not_equal, 768.0 / 8192, 1)
    for out, f in (("mI", 1.0), ("mIh", 1.0), ("I2", 2.0), ("Iq", 2.0 ** -14), ("mQ", 9.0 / 64)):
        ts(v(out), v("JL", 0, 128), pF, A.is_equal, f, A.mult)
    for out, c in (("Z8", g15), ("ZA", k15)):
        ts(v(out), v("JL", 0, 144), c, A.is_equal)
    ts(v("RP"), v("JG"), pF, A.is_equal)
    ts(v("OH"), v("JL", 0, 16), pm, A.is_equal)
    for out, src, f, x in ((cj0, v("OH", 2, 3), 4352.0, v("OH", 3, 4)), (cj1, v("OH", 4, 5), 4352.0, v("OH", 5, 6)),
                           (odd, v("OH", 3, 4), 1.0, v("OH", 5, 6)), (v("COL", 72, 75), v("JL", 32, 128, 32), low, 0.0),
                           (lift[0], odd, -1.0, 1.0), (lift[1], odd, 127.0, 1.0), (back, v("OH", 15, 16), 1024.0, -1024.0)):
        act(out, src, F.Identity, f, x)
    for out, src, f in ((v("mNI"), v("mI"), -1.0), (v("p48"), v("mI"), 48.0),
                        (v("SGs"), v("SG"), 1.0 / 8192), (v("ZS"), v("Z8"), 2048.0),
                        (v("ZS2"), v("Z8"), 4096.0), (v("ZSn"), v("Z8"), -2048.0),
                        (v("ZV"), v("Z8"), low), (v("ZJ0"), v("Z8"), cj0), (v("ZJ1"), v("Z8"), cj1), (v("WX"), v("SG"), wi),
                        (v("KBS", 0, 16), v("G8"), 1024.0), (v("KBS", 16, 32), v("G8"), 2048.0), (v("KBS", 32, 48), v("G8"), -1024.0)):
        if out[0] == "KBS" and not out[1]:
            iota(v("J8"), [[0, 2], [1, 8]])
            ts(v("G8"), v("J8"), pg, A.is_equal)
        act(out, src, scale=f)
    act(v("PD", 0, 16), v("OH"), scale=-4096.0)
    act(v("W2", 0, 16), v("OH"), scale=1024.0)
    tt(v("PD", 1, 16), v("PD", 1, 16), v("W2", 0, 15), A.add)
    for k in (16, 32, 64, 128):
        act(v("PD", k, 2 * k), v("PD", 0, k))
    act(v("W2", 16, 32), v("JL", 0, 16), F.Identity, 16.0, pm)
    for k, (f, x) in enumerate(((1.0, 513.0), (2.0 ** -14, BASE + 8960.0 / 16384), (1.0, 4096.0))):
        act(v("LA", 16 * k, 16 * k + 16), v("W2", 16, 32), F.Identity, f, x)
    for out, x in ((half, 526336.5), (v("ZR16"), 0.0), (v("G", 4096, 4112), 0.0),
                   (v("CW", 256, 368), 0.0), (v("CS", 112, 120), 0), (v("LC1"), 0), (v("ONE"), 1.0), (v("BQ", 112, 128), 736.0)):
        fill(out, x)
    ts(v("a16", 32, 48), v("BQ", 112, 128), BASE - 1022 * 9.0 / 64 - 736.0, A.add)

    def late_constants(after):
        first = len(calls)
        iota(v("VT", 16, 20), [[6, 2], [-1, 2]], 3)
        iota(v("VT", 20, 22), [[1, 2]], 18)
        iota(v("VT", 22, 24), [[-1, 2]], 29)
        iota(v("VT", 24, 28), [[0, 4]], -5)
        iota(v("VT", 28, 32), [[0, 2], [1, 2]], 1)
        iota(v("BR", p1=1), [[0, 8], [112, 16]])
        for k in range(2):
            iota(v("JR", 256 * k, 256 * k + 256), [[1, 16], [0, 16]], 16 * k)
        iota(v("JT"), [[1, 16], [16, 7]])
        for out, x in ((v("R960", p1=1), 960), (v("BM"), -64), (v("BM", 0, 512, 16), 16000000), (v("BQ", 0, 112), 0), (v("BQ", 0, 112, 16), 16000000),
                       (v("G", 4112, 4352), 0), (v("G", 4464, 4480), 0), (v("G", 4592, 4608), 0)):
            iota(out, [[0, width(out)]], x)
        for c in calls[first:]:
            c["preds"][after] = "order"
        ts(v("VT", 24, 32), v("VT", 24, 32), side, A.is_equal)
        act(v("VT", 16, 24), v("VT", 16, 24), scale=low)
        tt(v("VT", 0, 8), v("VT", 16, 24), v("VT", 24, 32), A.add)
        ts(v("REP"), v("JR"), p31, A.is_equal)

    for q, c0, c2 in FILLS:
        if q == "V":
            fill(v("HF", c0, c2), 0.0)
    for k, (q, c0, c2) in enumerate(x for x in FILLS if x[0] == "Y"):
        load("Y", v("HF", c0, c2), T.HF[:, ZERO:ZERO + c2 - c0], "l_0%d" % k, v("HF", ZERO, ZERO + c2 - c0))
    for q, c0, c2 in FILLS:
        if q == "S":
            act(v("HF", c0, c2), v("HF", ZERO, ZERO + c2 - c0))

    (ss, dd, y1, y2, w, pos, t1, t2, t3, code, p1, p2) = [v("LL", 16 * x, 16 * x + 16) for x in range(12)]
    a16, nn = v("a16", 0, 16), v("a16", 16, 32)
    fi, hs, hk, q8 = [v("LI", 16 * x, 16 * x + 16) for x in range(4)]
    ro, Qs, x2, aP = [v("ML", c, c + 16) for c in (0, 16, 32, 112)]
    rows = v("ML", 128, 384, 1, 0, 8)
    aF, blZ, kL, popped = v("aF"), v("blZ"), v("KL", 15, 256, 16), []
    cellS, col0, col1 = [v("MX", q, 48, 3) for q in range(3)]

    def bank(b, c0=0, c1=512):
        return v("D%d" % (b // 2), 512 * (b % 2) + c0, 512 * (b % 2) + c1)

    def lists(o, z, src, c0, c1, rows=128, start=False, stop=True):
        for i in range(16):
            mm(o, v(z, 15 - i, 143 - i, 1, 0, rows), v(src, c0 + i, c1, 16, 0, rows), start and i == 0, stop and i == 15)

    def gather(engines, out, win, lst):
        c0 = 0
        for q, wd in engines:
            (vcopy if q == "V" else act)(v(out, c0, c0 + wd), ind(win, v(lst, c0 // 16, (c0 + wd) // 16)))
            c0 += wd
            if q == "V" and out == "cS":
                for p in popped:
                    calls[-1]["preds"].setdefault(p, "order")

    def start():
        vcopy(v("aS0"), v("aI"))
        vcopy(a16, v("aI"))
        vcopy(aF, v("aI"))
        for i in range(16):
            mm(v("TR", i, 256, 16, 0, 8), v("mIh", i, 128, 16), a16, i == 0, i == 15)
        vcopy(v("T16", p1=8), v("TR", 0, 256, 1, 0, 8))
        mm(v("KEY", 0, 256), v("RP", p1=8), v("T16", p1=8), True, True)
        vcopy(v("AR"), v("KEY", 0, 256))
        send(1, v("aS0"), "QA0", "r_a0")
        late_constants(sent[1])
        ts(v("W1"), v("FI"), 2.0, A.mult)
        tt(v("V0"), v("W1"), v("HI"), A.add)
        note("Y", lambda: g.sync.dma_start(out=T.HF[0:128:16, 0:2048], in_=T.V0[:, :]), 0.05, v("HF", 0, 2048), (v("V0"),), "l_v", 16,
             DMA + 0.4, "load")
        calls[-1]["preds"].setdefault(last_load["Y"], "after")

    def cells(t):
        if t:
            for r in (2, 3, 0, 1):
                act(v("RH", 256 * r, 256 * r + 256), ind(v("HF", 2304 * r, 2304 * r + 2048), v("aS%d" % t)))
            for c in (257, 258, 305, 306):
                mm(v("KEY", c, c + 46, 3), v("I2"), a16, c == 257, False)
            mm(v("KEY", 306, 352, 3), v("mI"), v("ONE", 0, 16), False, False)
            lists(v("KEY", 353, 448, 3), "ZJ0", "RH", 512, 1024, stop=False)
            lists(v("KEY", 354, 448, 3), "ZJ1", "RH", 512, 1024, stop=False)
            lists(v("KEY", 256, 448, 3), "ZV", "RH", 0, 1024)
            vcopy(v("cb", 0, 96), v("KEY", 352, 448))
            tt(v("cb", 96, 192), v("KEY", 256, 352), v("cb", 0, 96), A.max)
            tt(v("MX"), v("cb", 96, 144), v("cb", 144, 192), A.max)
            tt(dd, col1, col0, A.subtract)
        else:
            ts(v("LI", 96, 112), v("aI"), 127, A.bitwise_and)
            ts(v("LI", 112, 128), v("aI"), 7, A.logical_shift_right)
            vcopy(v("cU"), v("LI", 96, 128))
            act(v("HV"), ind(v("OH"), v("cU", 16, 32)))
            tt(v("RH", 0, 256), ind(v("V0"), v("cU", 0, 16)), v("HV"), A.mult)
            lists(v("KEY", 256, 272), "Z8", "RH", 0, 256, start=True)
            vcopy(cellS, v("KEY", 256, 272))
            ts(ss, aF, 2.0, A.mult)
        ts(fi, cellS, 7, A.bitwise_and, 1, A.logical_shift_right)

    def places():
        for c in range(16):
            e = 272 * c
            ts(v("E", e, e + 256 - 16 * c), v("AR", 16 * c, 256), v("aF", c, c + 1), A.is_equal)
            if c < 15:
                mm(v("TR", 16 * c + 16, 256), v("SG"), v("E", e + 16, e + 256 - 16 * c), c == 0, False)
            mm(v("TR", 16 * c, 16 * c + 16), v("LT"), v("E", e, e + 16), False, c == 15)
        scan(v("KL", 0, 256), v("PD"), v("TR", 0, 256), A.add, A.max)

    def pops(t):
        mm(Qs, v("mIh"), v("a16", 32, 48), True, False)
        mm(Qs, v("Iq"), a16, False, False)
        tt(nn, kL, fi, A.subtract)
        tt(hs, kL, cellS, A.add)
        ts(blZ, nn, 1024.0, A.is_ge, 8192.0, A.mult)
        scan(v("scB"), blZ, v("ZR16"), A.add, A.add)
        mm(Qs, v("mQ"), nn, False, False)
        mm(x2, v("I2"), nn, False, False)
        mm(ro, v("TRI"), blZ, False, False)
        mm(ro, v("SGs"), v("scB"), False, True)
        tt(pos, ro, v("LA", 0, 16), A.max)
        ts(hk, hs, 1, A.bitwise_and)

    def segments(t):
        if t:
            tt(y1, hk, dd, A.mult)
        tt(y2, col0 if t else ss, blZ, A.add)
        tt(w, y1 if t else hk, y2, A.add)
        ts(v("gU"), w, (4096.0, 4464.0, 4592.0)[t], A.min)
        popped[:] = [len(calls) - 1]

    def decide(t):
        tt(code, x2, hk, A.add)
        ts(v("vU"), code, -2044.0, A.add, 7.0, A.min)
        act(v("HV"), ind(v("VT", 0, 8), v("vU")), F.Identity, bias=stamp[t])
        if t == 0:
            ts(q8, pos, 1.0 / 7, A.mult, -772.0 / 7, A.add)
            ts(t2, q8, -6.9375, A.mult, -769.0, A.add)
            tt(t3, pos, t2, A.add)
            ts(v("jU", 0, 16), t3, 16.0, A.mult, 111.0, A.min)
            act(v("HW"), ind(v("JL"), v("jU", 0, 16)), F.Identity, odd, lift[0])
        if t == 1:
            ts(v("jU", 16, 32), pos, -769.0, A.add, 111.0, A.min)
            act(v("HW"), ind(v("JT"), v("jU", 16, 32)), F.Identity, odd, lift[1])
        tt(t1, Qs, pos, A.max)
        tt(t1, t1, v("LA", 16, 32), A.min)
        ts(v("nU", 16 * t + 16, 16 * t + 32), t1, -BASE, A.add, 16384.0, A.mult)
        if t == 0:
            ts(p1, t1, BASE + 8960.0 / 16384, A.is_ge, 8192.0, A.mult)
            ts(p2, blZ, -2.0, A.mult, 8192.0, A.add)
            tt(p2, p2, w, A.add)
            tt(p1, p1, p2, A.add)
            tt(p1, p1, v("LA", 32, 48), A.min)
            vcopy(v("nU", 0, 16), p1)
        cell = ind(v("HF"), v("nU", 16 * t + 16, 16 * t + 32))
        tt(cell, v("HV"), v("HW"), A.mult) if t < 2 else vcopy(cell, v("HV"))

    def refill():
        act(v("LX"), ind(v("G", 4352, 4464), v("jU", 0, 16)))
        vcopy(ind(v("G", 0, 4352), v("nU", 0, 16)), v("LX"))

    def move(t):
        tt(v("zt"), ind(v("G", 0, (4112, 4480, 4608)[t]), v("gU")), v("Z%d" % t), A.add)
        ts(v("Z%d" % (t + 1)), v("zt"), 0.0, A.max, 255.0, A.min)
        for e in range(4):
            mm(v("TR", e, 512, 4), v("mI"), v("Z%d" % (t + 1), 128, 256), True, True)

    def centres(t):
        vcopy(v("sU"), ind(v("SI", 0, 2048), v("aS%d" % t)))
        gather(CENTRES[t], "cS", v("X"), "sU")
        for b in range(4):
            for j in range(4):
                mm(bank(b, 128 * j, 128 * j + 128), v("mNI"), v("cS", 4 * b + j, 2048, 16), j == 0, False)

    def keys():
        ts(v("s16"), v("sU"), -1.0, A.mult)
        ts(v("hB"), v("sU"), 1.0 / 48, A.mult, 172.0, A.add)
        mm(v("TR", 256, 512, 1, 0, 8), v("mIh", 0, 8, 1, 0, 8), v("T16", p1=8), True, False)
        mm(rows, v("ONE", 0, 8, 1, 0, 1), v("R960", p1=1), True, False)
        for i in range(16):
            mm(v("TR", 256 + i, 512, 16, 0, 8), v("mNI", i, 128, 16), blZ, False, i == 15)
            mm(v("ML", 128 + i, 384, 16, 0, 8), v("mI", i, 128, 16), blZ, False, False)
        act(v("YK", p1=8), v("TR", 256, 512, 1, 0, 8), F.Identity, 1.0, 8192.0)
        for h in range(2):
            s = (128 * h, 128 * h + 128)
            mm(v("KEY", 256 * h, 256 * h + 128), v("hB", *s), v("mI"), h == 0, False)
            mm(v("KEY", 256 * h + 128, 256 * h + 256), v("hB", *s), v("p48"), False, False)
            mm(v("KEY", 256 * h + 128, 256 * h + 256), v("s16", *s), v("mIh"), False, False)
        for m in range(16):
            mm(v("KEY", 256 + m, 512, 16), v("cS", 2048 + m, 4096, 16), v("KBS", 32, 48), False, False)

    def search(t):
        for m in range(16):
            b, j = m // 4, m % 4
            mm(bank(b, 128 * j, 128 * j + 128), v("mI"), v("Z%d" % (t + 1), 0, 128), False, j == 3)
            if m == 7:
                act(v("AB", 0, 1024), v("D0"), F.Abs)
            if m in (11, 15):
                act(v("AB", 512 * b, 512 * b + 512), bank(b), F.Abs)
        for b in range(4):
            tt(v("AB", 2048 + 512 * b, 2560 + 512 * b), v("cS", 2048 + b, 4096, 4), v("TR"), A.max)
        for b in range(4):
            for e in range(4):
                mm(v("KEY", 256 + b + 4 * e, 512, 16), v("AB", 2048 + 512 * b + e, 2560 + 512 * b, 4), v("KBS", 16, 32), False, False)
            for m in range(4 * b - 4 * (b == 1), 4 * b + 4) if b else ():
                mm(v("KEY", m, 256, 16), v("AB", 128 * m, 128 * m + 128), v("KBS", 0, 16), False, m == 15)
        scan(v("KS"), v("BM"), v("KEY"), A.add, A.min)
        ts(v("KI"), v("KS", 15, 512, 16), 1.5 * 2 ** 29, A.add, 1.5 * 2 ** 29, A.subtract)
        tt(v("PB"), v("KS", 15, 512, 16), v("KI"), A.subtract)
        for h in range(2):
            o = v("ML", 128 + 128 * h, 256 + 128 * h, 1, 0, 8)
            mm(o, v("PB", 16 * h, 16 * h + 8), v("p48"), False, False)
            mm(o, v("PB", 16 * h + 8, 16 * h + 16), v("mNI"), False, h == 1)
        tt(v("YA" if t == 2 else "T16", p1=8), rows, v("YK", p1=8), A.min)
        if t < 2:
            lists(aP, "ZA", "T16", 0, 256, 8, start=True)
            mm(v("KEY", 0, 256), v("RP", p1=8), v("T16", p1=8), True, True)
            vcopy(v("AR"), v("KEY", 0, 256))
            vcopy(aF, aP)
            vcopy(v("aS%d" % (t + 1)), aP)
            vcopy(a16, aP)

    def slots(qz):
        x = v("KA", 0, 256)
        mm(x, v("WX"), qz, True, True)
        act(v("xq"), x, F.Identity, 1.0, half)
        mm(x, v("WX"), qz, True, False)
        mm(x, v("mNI"), v("xq"), False, True)
        act(v("Y2"), x, F.Square, bias=ycol)
        ts(v("TI"), v("Y2"), 0.03125, A.mult, rcol, A.add)
        ts(v("TJ"), v("TI"), 4095, A.bitwise_and)

    def ask(t):
        lanes = v("LC1", 0, 7) if t else v("CS", 112, 119)
        if t == 0:
            slots(v("Z0"))
        ts(v("CL"), pos, -513.0, A.add)
        vcopy(ind(v("CW"), v("CL")), v("JL"))
        scan(v("KL", 256, 368), v("PD", 0, 112), v("CW", 256, 368), A.add, A.max)
        ts(lanes, v("KL", 271, 368, 16), back, A.add)
        if t:
            send(2, v("LC1"), "QL1", "r_c1")
        else:
            vcopy(v("CS", 0, 112), ind(v("TJ"), lanes))
            send(1, v("CS"), "QC", "r_c0")
            act(v("ZC"), ind(v("Z0"), lanes))
            send(1, v("ZC"), "QZ0", "r_z0")
            asked = len(calls) - 2
            for q, c0, c2 in FILLS:
                if q == "G":
                    iota(v("HF", c0, c2), [[0, c2 - c0]])
                    calls[-1]["preds"][asked] = "order"

    def answer(t):
        e, qc = v("KA", 256, 384, 1, 0, 112), "CC" if t else "QC"
        if t:
            slots(v("QZ1"))
            vcopy(v("CC"), ind(v("TJ"), v("QL1", 0, 7)))
            act(v("QZ0"), ind(v("QZ1"), v("QL1", 0, 7)))
        act(v("goal"), ind(v("X"), v("QA%d" % t)))
        act(v("eB"), ind(v("goal"), v("QL1", 0, 7) if t else v("QC", 112, 119)))
        mm(e, v("eB"), v("mI"), True, False)
        mm(e, v("QZ0"), v("mNI"), False, True)
        ts(v("eT", p1=112), e, -16.0, A.max, 16.0, A.min)
        gather(CANDS[t], "cA", v("G", 0, 4096), qc)
        mm(v("KA", 0, 112), one_row, v("JL", 0, 112, 1, 0, 1), True, False)
        mm(v("KA", 0, 112), v("BR", p1=1), v("ONE", 0, 112, 1, 0, 1), False, False)
        cut = 112 * MAXED[t]
        for k in range(4):
            c0, c2 = 512 * k, min(512 * k + 512, 1792)
            r = (32 * k, c2 // 16)
            mm(bank(k, 0, c2 - c0), v("eT", 0, 128, 1, *r), v("REP", 0, c2 - c0, 1, *r), True, c2 <= cut)
            if c2 > cut:
                c1 = max(c0, cut)
                mm(bank(k, c1 - c0, c2 - c0), v("mNI"), v("cA", c1, c2), False, True)
                act(v("AC", c1, c2), bank(k, c1 - c0, c2 - c0), F.Abs)
            if c0 < cut:
                c1 = min(c2, cut)
                tt(v("AC", c0, c1), v("cA", c0, c1), bank(k, 0, c1 - c0), A.max)
        for b in range(MAXED[t]):
            mm(v("KA", 0, 112), v("ZSn", 15 - b, 143 - b), v("cA", 112 * b, 112 * b + 112), False, False)
        turn = [b for p in zip(range(8), range(8, 16)) for b in p]
        for b in turn:
            mm(v("KA", 0, 112), v("ZS2" if b < MAXED[t] else "ZS", 15 - b, 143 - b), v("AC", 112 * b, 112 * b + 112), False, b == turn[-1])
        scan(v("KT"), v("BQ", 0, 112), v("KA", 0, 112), A.add, A.min)
        vcopy(v("KQ", 0, 7), v("KT", 15, 112, 16))
        ts(v("KQ", 16, 23), v("KQ", 0, 7), 2047, A.bitwise_and)
        vcopy(v("qU", 0, 7), v("KQ", 16, 23))
        vcopy(v("AN%d" % t), ind(v("cA"), v("qU", 0, 7)))
        send(-1 - t, v("AN%d" % t), v("G", 4352 + 128 * t, 4464 + 128 * t), "r_n%d" % t)

    start()
    for t in range(STEPS):
        cells(t)
        places()
        pops(t)
        if t < 2:
            ask(t)
        segments(t)
        decide(t)
        centres(t)
        keys()
        move(t)
        if t == 0:
            send(2, v("Z1"), "QZ1", "r_z1")
        if t == 1:
            refill()
        search(t)
        if t == 0:
            send(2, v("aS1"), "QA1", "r_a1")
        if t < 2:
            answer(t)
    move_dma("Y", T.yz[:, :], T.Z3[:, :], v("Z3"), "o_z")
    move_dma("S", T.ya[:, :], T.YA[0:8, :], v("YA"), "o_a")
    for r in range(4):
        move_dma("Y", v("SA", 128 * r, 128 * r + 128), T.HF[0:128:16, 2304 * r:2304 * r + 2048], v("HF"), "l_p%d" % r)
    tt(v("W2"), v("SA", 0, 256), v("SA", 256, 512), A.max)
    tt(v("TI", 0, 128), v("W2", 0, 128), v("W2", 128, 256), A.max)
    ts(v("TJ", 0, 128), v("TI", 0, 128), 7, A.bitwise_and, 1, A.logical_shift_right)
    ts(v("TJ", 128, 256), v("TI", 0, 128), 1, A.bitwise_and)
    vcopy(v("YF"), v("TJ", 0, 128))
    vcopy(v("YH"), v("TJ", 128, 256))
    move_dma("Y", T.yf[:, :], T.YF[:, :], v("YF"), "o_f")
    move_dma("Y", T.yh[:, :], T.YH[:, :], v("YH"), "o_h")

    if not ORDER:
        ORDER.extend(joined(calls))
    cnt = {"V": 0, "S": 0, "P": 0, "G": 0}
    known = {q: {} for q in H}
    done = {}
    for i in ORDER:
        c = calls[i]
        q = c["q"]
        if q == "R":
            done[i] = (c["sem"], c["inc"], {})
            continue
        for sem, val, kn in sorted((done[p] for p, kind in c["preds"].items() if kind == "wait"), key=lambda r: -r[1]):
            if known[q].get(sem, 0) < val:
                H[q].wait_ge(T.sem[sem], val)
                for s, x in list(kn.items()) + [(sem, val)]:
                    known[q][s] = max(known[q].get(s, 0), x)
        call = c["run"]()
        if c["sem"] is None:
            cnt[q] += 1
            call.then_inc(T.sem["e" + q], 1)
            done[i] = ("e" + q, cnt[q], dict(known[q]))
        elif c["inc"]:
            call.then_inc(T.sem[c["sem"]], c["inc"])
            done[i] = (c["sem"], c["inc"], {})
    g.wait_ge(T.sem.sent, sent[0])
    for s, x in [("e" + q, cnt[q]) for q in cnt] + final:
        if known["G"].get(s, 0) < x:
            g.wait_ge(T.sem[s], x)
